import numpy as np
import ml_dtypes


def mxq(x, axis, fmt="e4m3"):
    dtype, down = {"e4m3": (ml_dtypes.float8_e4m3fn, 7), "e5m2": (ml_dtypes.float8_e5m2, 14)}[fmt]
    v = np.moveaxis(np.asarray(x, np.float32).astype(ml_dtypes.bfloat16).astype(np.float64), axis, -1)
    blocks = v.reshape(v.shape[:-1] + (-1, 32))
    amax = np.abs(blocks).max(-1, keepdims=True)
    byte = np.maximum(np.where(amax > 0, np.frexp(amax)[1] - 1 + 127, 0) - down, 1)
    scale = np.exp2(byte - 127.0)
    codes = (blocks / scale).astype(np.float32).astype(dtype).astype(np.float64)
    return np.moveaxis((codes * scale).reshape(v.shape), -1, axis)


WIDE = False


def mx_kscale(k):
    if not WIDE:
        return np.ones(k)
    levels = np.array([10, -10, 5, -5, 0])
    if k % 512:
        return np.exp2(np.random.permutation(np.resize(levels, k // 32))).repeat(32)
    a = np.empty((k // 512, 16))
    for p in range(k // 512):
        a[p, :8] = np.random.permutation(np.resize(levels, 8))
        for g in range(8):
            far = levels[np.abs(levels - a[p, g]) >= 10]
            a[p, g + 8] = far[np.random.randint(len(far))]
    return np.exp2(a.ravel()).repeat(32)


BF16 = ml_dtypes.bfloat16


def bf(x):
    return np.asarray(x, np.float32).astype(BF16)


def f64(x):
    return np.asarray(x).astype(np.float64)


E2M1 = np.array([0.0, 0.5, 1.0, 1.5, 2.0, 3.0, 4.0, 6.0, -0.0, -0.5, -1.0, -1.5, -2.0, -3.0, -4.0, -6.0])


def pack_weight(w, fmt):
    k, n = w.shape
    w = f64(bf(w)).reshape(k // 32, 32, n)
    amax = np.abs(w).max(1)
    if fmt == "e4m3":
        byte = np.frexp(amax)[1] - 1 + 127 - 7
    else:
        mant, ex = np.frexp(amax / 6.0)
        byte = np.where(mant > 0.5, ex, ex - 1) + 127
    byte = np.clip(np.where(amax > 0, byte, 1), 1, 254)
    scaled = (w * np.exp2(127.0 - byte)[:, None, :]).reshape(k, n).astype(np.float32)
    by_word = np.ascontiguousarray(scaled.reshape(k // 512, 128, 4, n).transpose(0, 1, 3, 2))
    if fmt == "e4m3":
        words = by_word.astype(ml_dtypes.float8_e4m3fn).view(np.uint8)
    else:
        c = by_word.astype(ml_dtypes.float4_e2m1fn).view(np.uint8) & 0xF
        words = c[..., 0::2] | (c[..., 1::2] << 4)
    return np.ascontiguousarray(words), np.ascontiguousarray(byte.astype(np.uint8).reshape(k // 512, 16, n))


def unpack_weight(words, scales, fmt):
    g, p, n, _ = words.shape
    if fmt == "e4m3":
        vals = np.ascontiguousarray(words).view(ml_dtypes.float8_e4m3fn).astype(np.float64)
    else:
        nib = np.empty((g, p, n, 4), np.uint8)
        nib[..., 0::2] = words & 0xF
        nib[..., 1::2] = words >> 4
        vals = E2M1[nib]
    vals = vals * np.repeat(np.exp2(scales.astype(np.float64) - 127.0), 8, axis=1)[..., None]
    return vals.transpose(0, 1, 3, 2).reshape(g * 512, n)
def pack4(w):
    words, scales = pack_weight(w, "e2m1")
    return words.reshape(words.shape[0], 128, -1), scales


def unpack4(words, scales):
    return unpack_weight(words.reshape(words.shape[0], 128, -1, 2), scales, "e2m1")


E4M3FN = np.array([(-1.0 if i & 128 else 1.0) * ((1.0 + (i & 7) / 8.0) * 2.0 ** (((i >> 3) & 15) - 7) if i & 120 else (i & 7) * 2.0 ** -9) for i in range(256)])


def e4m3fn_bytes(y):
    return np.clip(np.asarray(y, np.float64), -448.0, 448.0).astype(np.float32).astype(ml_dtypes.float8_e4m3fn).view(np.uint8)


def e4m3fn_values(b):
    return E4M3FN[b]


N, D, F, R = 1024, 1024, 1024, 512


def draw0():
    s = mx_kscale(D)
    u = mx_kscale(R)
    v = mx_kscale(R)
    x = bf(np.random.standard_normal((N, D)) * s)
    w0_words, w0_scales = pack4(np.random.standard_normal((D, F)) / np.sqrt(D) / s[:, None])
    a_words, a_scales = pack4(np.random.standard_normal((D, R)) / np.sqrt(D) / s[:, None])
    d = bf((1.0 + 0.1 * np.random.standard_normal(R)) * v)
    m = np.random.standard_normal((R, R)) / np.sqrt(R) * u[None, :] / v[:, None]
    m_words, m_scales = pack4(np.ascontiguousarray(m.T))
    bu_words, bu_scales = pack4(np.random.standard_normal((R, F)) / u[:, None])
    return {
        "x": x,
        "w0_words": w0_words,
        "w0_scales": w0_scales,
        "a_words": a_words,
        "a_scales": a_scales,
        "d": d,
        "m_words": m_words,
        "m_scales": m_scales,
        "bu_words": bu_words,
        "bu_scales": bu_scales,
    }


def core(x, w0_words, w0_scales, a_words, a_scales, d, m_words, m_scales, bu_words, bu_scales):
    rank = d.shape[0]
    xq = mxq(f64(x), 1, "e4m3")
    base = xq @ unpack4(w0_words, w0_scales)
    p = xq @ unpack4(a_words, a_scales)
    pg = p * f64(d)[None, :]
    c = unpack4(m_words, m_scales).T @ unpack4(bu_words, bu_scales)
    t = mxq(pg, 1, "e4m3") @ mxq(c, 0, "e4m3")
    return base + t / np.sqrt(rank)


def setup_inputs():
    drawn = draw0()
    full = np.asarray(drawn['x']).astype(np.float64)
    scale = (np.abs(full).reshape(8, 128, 8, 128).max(axis=(1, 3)) / 448.0).astype(np.float32)
    given = {}
    for key, value in drawn.items():
        if key == 'x':
            given['x_bytes'] = e4m3fn_bytes(full / np.repeat(np.repeat(scale.astype(np.float64), 128, axis=0), 128, axis=1))
            given['x_scale'] = scale
        else:
            given[key] = value
    return given


def reference(x_bytes, x_scale, w0_words, w0_scales, a_words, a_scales, d, m_words, m_scales, bu_words, bu_scales):
    return core(e4m3fn_values(x_bytes) * np.repeat(np.repeat(x_scale.astype(np.float64), 128, axis=0), 128, axis=1), w0_words, w0_scales, a_words, a_scales, d, m_words, m_scales, bu_words, bu_scales)

@@ -1,0 +1,271 @@
+import math
+from contextlib import ExitStack
+
+import concourse.mybir as mybir
+from concourse.masks import make_identity
+
+N, D, F, R = 1024, 1024, 1024, 512
+FLOPS = 2 * N * D * F + 2 * N * D * R + 2 * R * R * F + 2 * N * R * F
+
+F32 = mybir.dt.float32
+BF16 = mybir.dt.bfloat16
+I32 = mybir.dt.int32
+U32 = mybir.dt.uint32
+U8 = mybir.dt.uint8
+FP8 = mybir.dt.float8_e4m3fn
+FP8X4 = mybir.dt.float8_e4m3fn_x4
+FP4X4 = mybir.dt.float4_e2m1fn_x4
+ALU = mybir.AluOpType
+ACT = mybir.ActivationFunctionType
+
+P = 128
+SCALAR_WIDENS = [(0, 1),(1, 1)]
+ORDER = [("W",0,1,),("W",0,0,),("T",0,0,),("T",0,1,),("W",1,1,),("W",1,0,),("pa",),("E",0,),("T",1,1,),("T",1,0,),("TD",),("Q",0,),("E",1,),("W",3,1,),("P",0,),("TDc",),("Q",1,),("pm",),("B",0,0,),("W",3,0,),("B",1,0,),("W",2,1,),("BE",0,0,),("W",2,0,),("C",0,0,),("W",5,0,),("C",0,1,),("W",4,1,),("CE",0,0,),("C",0,3,),("C",1,2,),("W",5,1,),("BE",1,0,),("T",2,0,),("W",4,0,),("T",2,1,),("CE",0,1,),("T",3,0,),("PE",0,),("T",3,1,),("C",0,2,),("E",2,),("W",6,1,),("C",1,1,),("E",3,),("P",1,),("CE",0,3,),("B",0,1,),("Q",3,),("Q",2,),("CE",1,1,),("T",4,1,),("W",7,1,),("T",5,0,),("CE",1,2,),("T",4,0,),("PE",1,),("T",5,1,),("C",1,3,),("CE",0,2,),("W",7,0,),("C",1,0,),("W",6,0,),("BE",0,1,),("P",2,),("QP",0,),("E",4,),("B",2,1,),("CE",1,3,),("PE",2,),("B",1,1,),("E",5,),("CQ",0,),("P",3,),("CE",1,0,),("Q",4,),("T",6,0,),("T",7,0,),("PE",3,),("T",6,1,),("T",7,1,),("B",2,0,),("QP",2,),("E",6,),("QP",1,),("QP",3,),("Q",5,),("P",4,),("BE",1,1,),("CQ",1,),("BE",2,1,),("B",4,0,),("PE",4,),("BE",2,0,),("M",2,0,),("M",1,0,),("Q",6,),("E",7,),("B",5,0,),("QP",4,),("F",1,0,),("BE",4,0,),("M",0,0,),("P",5,),("F",2,0,),("BE",5,0,),("F",0,0,),("B",3,0,),("PE",5,),("M",2,1,),("ST",0,0,),("ST",1,0,),("B",3,1,),("BE",3,0,),("Q",7,),("QP",5,),("M",3,0,),("F",2,1,),("M",3,1,),("BE",3,1,),("M",4,0,),("F",3,0,),("B",4,1,),("ST",2,1,),("F",4,0,),("M",0,1,),("P",6,),("BE",4,1,),("F",3,1,),("ST",4,0,),("ST",3,0,),("ST",2,0,),("F",0,1,),("B",5,1,),("PE",6,),("M",1,1,),("ST",0,1,),("M",4,1,),("BE",5,1,),("ST",3,1,),("M",5,0,),("F",1,1,),("M",5,1,),("P",7,),("QP",6,),("F",4,1,),("ST",1,1,),("B",6,0,),("F",5,1,),("ST",4,1,),("B",6,1,),("F",5,0,),("BE",6,0,),("M",6,0,),("PE",7,),("B",7,0,),("BE",6,1,),("ST",5,0,),("ST",5,1,),("F",6,0,),("M",6,1,),("B",7,1,),("BE",7,0,),("QP",7,),("F",6,1,),("ST",6,0,),("M",7,0,),("M",7,1,),("BE",7,1,),("ST",6,1,),("F",7,0,),("F",7,1,),("ST",7,0,),("ST",7,1,)]
+
+
+def tile_moslorasubspacemixerrankgain_d2p_kernel(
+    tc, x_bytes, x_scale, w0_words, w0_scales, a_words, a_scales, d, m_words, m_scales, bu_words, bu_scales, out
+):
+    nc = tc.nc
+    with ExitStack() as ctx:
+        keep = ctx.enter_context(tc.tile_pool(name="keep", bufs=1))
+        work = ctx.enter_context(tc.tile_pool(name="work", bufs=3))
+        psum = ctx.enter_context(tc.psum_pool(name="psum", bufs=1))
+        ctx.enter_context(tc.manual_schedule())
+
+        ident32 = keep.tile([P, P], F32, align_bytes=64)
+        ident16 = keep.tile([P, P], BF16, align_bytes=64)
+        d_rows = keep.tile([P, P], BF16, align_bytes=64)
+        d_cols = keep.tile([P, 4], F32, align_bytes=64)
+        xs = keep.tile([P, 64], F32, align_bytes=64)
+        xb = keep.tile([P, 8, 1024], U8, align_bytes=64)
+        a_raw = keep.tile([P, 2, 1024], U8, align_bytes=64)
+        a_w = keep.tile([P, 2, 1024], U8, align_bytes=64)
+        a_sraw = keep.tile([P, 2, 512], U8, align_bytes=64)
+        a_s = keep.tile([P, 2, 512], U8, align_bytes=64)
+        m_raw = keep.tile([P, 1, 1024], U8, align_bytes=64)
+        m_w = keep.tile([P, 1, 1024], U8, align_bytes=64)
+        m_sraw = keep.tile([P, 1, 512], U8, align_bytes=64)
+        m_s = keep.tile([P, 1, 512], U8, align_bytes=64)
+        w0_w = keep.tile([P, 2, 2048], U8, align_bytes=64)
+        w0_s = keep.tile([P, 2, 1024], U8, align_bytes=64)
+        bu_w = keep.tile([P, 1, 2048], U8, align_bytes=64)
+        bu_s = keep.tile([P, 1, 1024], U8, align_bytes=64)
+        xq = keep.tile([P, 8, 256], U32, align_bytes=64)
+        xq_s = keep.tile([P, 8, 256], U8, align_bytes=64)
+        pq = keep.tile([P, 8, 128], U32, align_bytes=64)
+        pq_s = keep.tile([P, 8, 128], U8, align_bytes=64)
+        cq = keep.tile([P, 1024], U32, align_bytes=64)
+        cq_s = keep.tile([P, 1024], U8, align_bytes=64)
+        c_grouped = keep.tile([P, 2, 2048], BF16, align_bytes=64)
+        res = keep.tile([P, 8, 1024], F32, align_bytes=64)
+        xw = keep.tile([P, 8, 1024], BF16, align_bytes=64)
+        xg = keep.tile([P, 8, 1024], BF16, align_bytes=64)
+        pg = keep.tile([P, 8, 512], BF16, align_bytes=64)
+
+        def load_scales(queue, plane, src):
+            rows = src.bitcast(I32).rearrange("g (q j) n -> j q g n", j=4)
+            for j in range(4):
+                queue.dma_start(out=plane[j:P:32].bitcast(I32), in_=rows[j])
+
+        def load_x(i0, i1):
+            nc.sync.dma_start(out=xb[:, i0:i1, :], in_=x_bytes[i0 * P : i1 * P, :].rearrange("(i p) k -> p i k", p=P))
+
+        def load_words(dst, src):
+            nc.sync.dma_start(out=dst.bitcast(I32), in_=src.rearrange("g p n -> p g n").bitcast(I32))
+
+        nc.vector.memset(d_rows[:], 0.0)
+        for plane in (a_sraw, m_sraw, w0_s, bu_s):
+            nc.vector.memset(plane[:].bitcast(I32), 0)
+        make_identity(nc, ident32[:])
+        nc.gpsimd.dma_start(
+            out=d_rows[0:4, :].rearrange("t (q e) -> t q e", e=8), in_=d.rearrange("(q t e) -> t q e", t=4, e=8)
+        )
+        nc.scalar.copy(out=ident16[:], in_=ident32[:])
+        load_scales(nc.gpsimd, m_sraw, m_scales)
+
+        nc.sync.dma_start(out=xs[:], in_=x_scale.rearrange("i j -> (i j)").partition_broadcast(P))
+        load_x(0, 1)
+        load_scales(nc.sync, a_sraw, a_scales)
+        load_words(a_raw[:], a_words)
+        load_x(1, 2)
+        load_scales(nc.sync, w0_s, w0_scales)
+        load_words(w0_w[:, :, 0:1024], w0_words[:, :, 0:1024])
+        load_x(2, 4)
+        load_words(w0_w[:, :, 1024:2048], w0_words[:, :, 1024:2048])
+        load_words(m_raw[:], m_words)
+        load_scales(nc.sync, bu_s, bu_scales)
+        load_words(bu_w[:], bu_words)
+        load_x(4, 6)
+        load_x(6, 8)
+
+        live = {}
+
+        def permute(words, raw, scales, sraw, g):
+            nc.vector.tensor_copy(
+                out=words[:, g, :].bitcast(I32).rearrange("p (t q w) -> p t q w", t=4, q=16),
+                in_=raw[:, g, :].bitcast(I32).rearrange("p (q t w) -> p t q w", t=4, q=16),
+            )
+            nc.vector.tensor_copy(
+                out=scales[:, g, :].bitcast(I32).rearrange("p (t q w) -> p t q w", t=4, q=16),
+                in_=sraw[:, g, :].bitcast(I32).rearrange("p (q t w) -> p t q w", t=4, q=16),
+            )
+
+        def permute_a():
+            permute(a_w, a_raw, a_s, a_sraw, 0)
+            permute(a_w, a_raw, a_s, a_sraw, 1)
+
+        def permute_m():
+            permute(m_w, m_raw, m_s, m_sraw, 0)
+
+        def turn_d():
+            bank = psum.tile([P, P], BF16, tag="acc", bufs=5, name="d_bank")
+            live.setdefault("d", bank)
+            nc.tensor.transpose(bank[:], d_rows[:], ident16[:])
+
+        def empty_d():
+            nc.scalar.copy(out=d_cols[:], in_=live["d"][:, 0:4])
+
+        def widen(i, g):
+            for b in range(4):
+                j = 4 * g + b
+                src = xb[:, i, j * P : (j + 1) * P].bitcast(FP8)
+                scale = xs[:, 8 * i + j : 8 * i + j + 1]
+                if (i, g) in SCALAR_WIDENS:
+                    nc.scalar.activation(out=xw[:, i, j * P : (j + 1) * P], in_=src, func=ACT.Copy, scale=scale)
+                else:
+                    dst = xw[:, i, g * 512 : (g + 1) * 512].rearrange("p (u q e) -> p q u e", u=2, e=2)
+                    nc.vector.tensor_scalar(
+                        out=dst[:, 32 * b : 32 * (b + 1)],
+                        in0=src.rearrange("p (q u e) -> p q u e", u=2, e=2),
+                        scalar1=scale,
+                        scalar2=None,
+                        op0=ALU.mult,
+                    )
+
+        def turn_x(i, g):
+            if ("xt", i) not in live:
+                live.setdefault(("xt", i), psum.tile([P, 2, 2, P], F32, tag="xbank", bufs=2, name="x_bank"))
+            bank = live[("xt", i)]
+            words = xw[:, i, g * 512 : (g + 1) * 512].bitcast(F32)
+            for u in range(2):
+                src = words[:, u:256:2] if (i, g) in SCALAR_WIDENS else words[:, u * P : (u + 1) * P]
+                nc.tensor.transpose(bank[:, g, u, :], src, ident32[:])
+
+        def empty_x(i):
+            nc.scalar.copy(
+                out=xg[:, i, :].bitcast(F32).rearrange("p (g r u) -> p g r u", g=2, u=2),
+                in_=live[("xt", i)][:].rearrange("p g u r -> p g r u"),
+            )
+
+        def quant_x(i):
+            nc.vector.quantize_mx(out=xq[:, i, :].bitcast(FP8X4), scales=xq_s[:, i, :], in_=xg[:, i, :])
+
+        def down(i):
+            bank = psum.tile([P, 4, P], F32, tag="pbank", bufs=1, name="p_bank")
+            live.setdefault(("p", i), bank)
+            for t in range(4):
+                for g in range(2):
+                    nc.tensor.matmul_mx(
+                        out=bank[:, t, :],
+                        lhsT=a_w[:, g, t * 256 : (t + 1) * 256].bitcast(FP4X4),
+                        lhsT_scale=a_s[:, g, t * P : (t + 1) * P],
+                        rhs=xq[:, i, g * P : (g + 1) * P].bitcast(FP8X4),
+                        rhs_scale=xq_s[:, i, g * P : (g + 1) * P],
+                        start=(g == 0),
+                        stop=(g == 1),
+                    )
+
+        def gain(i):
+            nc.vector.tensor_tensor(
+                out=pg[:, i, :].rearrange("p (n t) -> p n t", t=4),
+                in0=live[("p", i)][:].rearrange("p t n -> p n t"),
+                in1=d_cols[:].unsqueeze(1).to_broadcast([P, P, 4]),
+                op=ALU.mult,
+            )
+
+        def quant_p(i):
+            nc.vector.quantize_mx(out=pq[:, i, :].bitcast(FP8X4), scales=pq_s[:, i, :], in_=pg[:, i, :])
+
+        def acc_bank(key):
+            bank = psum.tile([P, 512], F32, tag="acc", bufs=5, name="acc_bank")
+            live.setdefault(key, bank)
+            return bank
+
+        def base(i, h):
+            bank = acc_bank(("b", i, h))
+            for g in range(2):
+                nc.tensor.matmul_mx(
+                    out=bank[:],
+                    lhsT=xq[:, i, g * P : (g + 1) * P].bitcast(FP8X4),
+                    lhsT_scale=xq_s[:, i, g * P : (g + 1) * P],
+                    rhs=w0_w[:, g, h * 1024 : (h + 1) * 1024].bitcast(FP4X4),
+                    rhs_scale=w0_s[:, g, h * 512 : (h + 1) * 512],
+                    start=(g == 0),
+                    stop=(g == 1),
+                )
+
+        def empty_base(i, h):
+            nc.scalar.copy(out=res[:, i, h * 512 : (h + 1) * 512], in_=live[("b", i, h)][:])
+
+        def mix(h, b):
+            bank = acc_bank(("c", h, b))
+            f0 = h * 512 + b * P
+            for t in range(4):
+                nc.tensor.matmul_mx(
+                    out=bank[:, t * P : (t + 1) * P],
+                    lhsT=m_w[:, 0, t * 256 : (t + 1) * 256].bitcast(FP4X4),
+                    lhsT_scale=m_s[:, 0, t * P : (t + 1) * P],
+                    rhs=bu_w[:, 0, 2 * f0 : 2 * (f0 + P)].bitcast(FP4X4),
+                    rhs_scale=bu_s[:, 0, f0 : f0 + P],
+                    start=(t == 0),
+                    stop=(t == 3),
+                )
+
+        def empty_c(h, b):
+            nc.scalar.copy(
+                out=c_grouped[:, h, b * 512 : (b + 1) * 512].rearrange("p (f t) -> p f t", t=4),
+                in_=live[("c", h, b)][:].rearrange("p (t f) -> p f t", t=4),
+            )
+
+        def quant_c(h):
+            nc.vector.quantize_mx(
+                out=cq[:, h * 512 : (h + 1) * 512].bitcast(FP8X4),
+                scales=cq_s[:, h * 512 : (h + 1) * 512],
+                in_=c_grouped[:, h, :],
+            )
+
+        def up(i, h):
+            bank = acc_bank(("t", i, h))
+            nc.tensor.matmul_mx(
+                out=bank[:],
+                lhsT=pq[:, i, :].bitcast(FP8X4),
+                lhsT_scale=pq_s[:, i, :],
+                rhs=cq[:, h * 512 : (h + 1) * 512].bitcast(FP8X4),
+                rhs_scale=cq_s[:, h * 512 : (h + 1) * 512],
+                start=True,
+                stop=True,
+            )
+
+        def finish(i, h):
+            cols = slice(h * 512, (h + 1) * 512)
+            nc.vector.scalar_tensor_tensor(
+                out=res[:, i, cols],
+                in0=live[("t", i, h)][:],
+                scalar=1.0 / math.sqrt(R),
+                in1=res[:, i, cols],
+                op0=ALU.mult,
+                op1=ALU.add,
+            )
+
+        def store(i, h):
+            cols = slice(h * 512, (h + 1) * 512)
+            nc.sync.dma_start(out=out[i * P : (i + 1) * P, cols], in_=res[:, i, cols])
+
+        steps = {
+            "W": widen, "T": turn_x, "E": empty_x, "Q": quant_x, "P": down, "PE": gain, "QP": quant_p,
+            "B": base, "BE": empty_base, "C": mix, "CE": empty_c, "CQ": quant_c,
+            "M": up, "F": finish, "ST": store, "pa": permute_a, "pm": permute_m, "TD": turn_d, "TDc": empty_d,
+        }
+        for step in ORDER:
+            steps[step[0]](*step[1:])

@@ -20,7 +20,7 @@ ACT = mybir.ActivationFunctionType
 
 P = 128
 SCALAR_WIDENS = [(0, 1),(1, 1)]
-ORDER = [("W",0,1,),("W",0,0,),("T",0,0,),("T",0,1,),("W",1,1,),("W",1,0,),("pa",),("E",0,),("T",1,1,),("T",1,0,),("TD",),("Q",0,),("E",1,),("W",3,1,),("P",0,),("TDc",),("Q",1,),("pm",),("B",0,0,),("W",3,0,),("B",1,0,),("W",2,1,),("BE",0,0,),("W",2,0,),("C",0,0,),("W",5,0,),("C",0,1,),("W",4,1,),("CE",0,0,),("C",0,3,),("C",1,2,),("W",5,1,),("BE",1,0,),("T",2,0,),("W",4,0,),("T",2,1,),("CE",0,1,),("T",3,0,),("PE",0,),("T",3,1,),("C",0,2,),("E",2,),("W",6,1,),("C",1,1,),("E",3,),("P",1,),("CE",0,3,),("B",0,1,),("Q",3,),("Q",2,),("CE",1,1,),("T",4,1,),("W",7,1,),("T",5,0,),("CE",1,2,),("T",4,0,),("PE",1,),("T",5,1,),("C",1,3,),("CE",0,2,),("W",7,0,),("C",1,0,),("W",6,0,),("BE",0,1,),("P",2,),("QP",0,),("E",4,),("B",2,1,),("CE",1,3,),("PE",2,),("B",1,1,),("E",5,),("CQ",0,),("P",3,),("CE",1,0,),("Q",4,),("T",6,0,),("T",7,0,),("PE",3,),("T",6,1,),("T",7,1,),("B",2,0,),("QP",2,),("E",6,),("QP",1,),("QP",3,),("Q",5,),("P",4,),("BE",1,1,),("CQ",1,),("BE",2,1,),("B",4,0,),("PE",4,),("BE",2,0,),("M",2,0,),("M",1,0,),("Q",6,),("E",7,),("B",5,0,),("QP",4,),("F",1,0,),("BE",4,0,),("M",0,0,),("P",5,),("F",2,0,),("BE",5,0,),("F",0,0,),("B",3,0,),("PE",5,),("M",2,1,),("ST",0,0,),("ST",1,0,),("B",3,1,),("BE",3,0,),("Q",7,),("QP",5,),("M",3,0,),("F",2,1,),("M",3,1,),("BE",3,1,),("M",4,0,),("F",3,0,),("B",4,1,),("ST",2,1,),("F",4,0,),("M",0,1,),("P",6,),("BE",4,1,),("F",3,1,),("ST",4,0,),("ST",3,0,),("ST",2,0,),("F",0,1,),("B",5,1,),("PE",6,),("M",1,1,),("ST",0,1,),("M",4,1,),("BE",5,1,),("ST",3,1,),("M",5,0,),("F",1,1,),("M",5,1,),("P",7,),("QP",6,),("F",4,1,),("ST",1,1,),("B",6,0,),("F",5,1,),("ST",4,1,),("B",6,1,),("F",5,0,),("BE",6,0,),("M",6,0,),("PE",7,),("B",7,0,),("BE",6,1,),("ST",5,0,),("ST",5,1,),("F",6,0,),("M",6,1,),("B",7,1,),("BE",7,0,),("QP",7,),("F",6,1,),("ST",6,0,),("M",7,0,),("M",7,1,),("BE",7,1,),("ST",6,1,),("F",7,0,),("F",7,1,),("ST",7,0,),("ST",7,1,)]
+ORDER = [("D",3,),("W",0,0,),("W",0,1,),("T",0,0,),("T",0,1,),("D",2,),("E",0,0,),("W",1,0,),("E",0,),("Q",0,0,),("W",1,1,),("Q",0,),("pa",),("B",0,0,),("W",2,0,),("T",1,0,),("W",2,1,),("T",1,1,),("BE",0,0,),("W",3,0,),("TD",),("P",0,),("E",1,),("W",3,1,),("B",0,1,),("TDc",),("Q",1,),("PE",0,),("T",2,0,),("T",2,1,),("BE",0,1,),("T",3,0,),("pm",),("T",3,1,),("B",1,0,),("W",4,0,),("E",2,),("W",4,1,),("E",3,),("P",1,),("BE",1,0,),("B",1,1,),("PE",1,),("C",0,0,),("BE",1,1,),("Q",2,),("C",0,1,),("W",5,0,),("CE",0,0,),("P",2,),("Q",3,),("W",5,1,),("CE",0,1,),("C",0,2,),("QP",0,),("PE",2,),("B",2,0,),("CE",0,2,),("QP",1,),("C",0,3,),("W",6,0,),("BE",2,0,),("T",4,0,),("W",6,1,),("T",4,1,),("T",5,0,),("CE",0,3,),("T",5,1,),("P",3,),("E",4,),("CQ",0,),("C",1,0,),("E",5,),("W",7,0,),("B",2,1,),("CE",1,0,),("W",7,1,),("C",1,1,),("QP",2,),("BE",2,1,),("M",0,0,),("PE",3,),("C",1,2,),("CE",1,1,),("Q",4,),("B",3,0,),("F",0,0,),("CE",1,2,),("C",1,3,),("Q",5,),("M",1,0,),("BE",3,0,),("ST",0,0,),("QP",3,),("P",4,),("F",1,0,),("CE",1,3,),("T",6,0,),("T",6,1,),("PE",4,),("T",7,0,),("ST",1,0,),("T",7,1,),("E",6,),("M",2,0,),("CQ",1,),("B",3,1,),("E",7,),("F",2,0,),("M",3,0,),("P",5,),("BE",3,1,),("QP",4,),("ST",2,0,),("F",3,0,),("B",4,0,),("Q",6,),("ST",3,0,),("PE",5,),("M",0,1,),("M",1,1,),("BE",4,0,),("Q",7,),("B",4,1,),("F",0,1,),("M",2,1,),("QP",5,),("P",6,),("BE",4,1,),("F",1,1,),("ST",0,1,),("B",5,0,),("F",2,1,),("ST",1,1,),("M",3,1,),("PE",6,),("ST",2,1,),("M",4,0,),("BE",5,0,),("B",5,1,),("F",3,1,),("M",4,1,),("QP",6,),("F",4,0,),("P",7,),("ST",3,1,),("BE",5,1,),("F",4,1,),("B",6,0,),("ST",4,0,),("PE",7,),("M",5,0,),("ST",4,1,),("M",5,1,),("BE",6,0,),("B",6,1,),("F",5,0,),("M",6,0,),("QP",7,),("F",5,1,),("B",7,0,),("ST",5,0,),("BE",6,1,),("F",6,0,),("M",6,1,),("ST",5,1,),("B",7,1,),("BE",7,0,),("F",6,1,),("ST",6,0,),("M",7,0,),("M",7,1,),("BE",7,1,),("ST",6,1,),("F",7,0,),("F",7,1,),("ST",7,0,),("ST",7,1,)]
 
 
 def tile_moslorasubspacemixerrankgain_d2p_kernel(
@@ -36,6 +36,7 @@ def tile_moslorasubspacemixerrankgain_d2p_kernel(
         ident32 = keep.tile([P, P], F32, align_bytes=64)
         ident16 = keep.tile([P, P], BF16, align_bytes=64)
         d_rows = keep.tile([P, P], BF16, align_bytes=64)
+        warm = keep.tile([P, 512], BF16, align_bytes=64)
         d_cols = keep.tile([P, 4], F32, align_bytes=64)
         xs = keep.tile([P, 64], F32, align_bytes=64)
         xb = keep.tile([P, 8, 1024], U8, align_bytes=64)
@@ -74,29 +75,31 @@ def tile_moslorasubspacemixerrankgain_d2p_kernel(
         def load_words(dst, src):
             nc.sync.dma_start(out=dst.bitcast(I32), in_=src.rearrange("g p n -> p g n").bitcast(I32))
 
-        nc.vector.memset(d_rows[:], 0.0)
-        for plane in (a_sraw, m_sraw, w0_s, bu_s):
+        nc.vector.memset(warm[:], 0.0)
+        nc.vector.memset(w0_s[:].bitcast(I32), 0)
+        for plane in (a_sraw, m_sraw, bu_s):
             nc.vector.memset(plane[:].bitcast(I32), 0)
         make_identity(nc, ident32[:])
+        nc.gpsimd.memset(d_rows[:], 0.0)
         nc.gpsimd.dma_start(
             out=d_rows[0:4, :].rearrange("t (q e) -> t q e", e=8), in_=d.rearrange("(q t e) -> t q e", t=4, e=8)
         )
         nc.scalar.copy(out=ident16[:], in_=ident32[:])
-        load_scales(nc.gpsimd, m_sraw, m_scales)
 
         nc.sync.dma_start(out=xs[:], in_=x_scale.rearrange("i j -> (i j)").partition_broadcast(P))
         load_x(0, 1)
-        load_scales(nc.sync, a_sraw, a_scales)
-        load_words(a_raw[:], a_words)
-        load_x(1, 2)
         load_scales(nc.sync, w0_s, w0_scales)
         load_words(w0_w[:, :, 0:1024], w0_words[:, :, 0:1024])
+        load_x(1, 2)
+        load_scales(nc.sync, a_sraw, a_scales)
+        load_words(a_raw[:], a_words)
         load_x(2, 4)
         load_words(w0_w[:, :, 1024:2048], w0_words[:, :, 1024:2048])
         load_words(m_raw[:], m_words)
+        load_x(4, 6)
+        load_scales(nc.sync, m_sraw, m_scales)
         load_scales(nc.sync, bu_s, bu_scales)
         load_words(bu_w[:], bu_words)
-        load_x(4, 6)
         load_x(6, 8)
 
         live = {}
@@ -144,22 +147,34 @@ def tile_moslorasubspacemixerrankgain_d2p_kernel(
                     )
 
         def turn_x(i, g):
-            if ("xt", i) not in live:
-                live.setdefault(("xt", i), psum.tile([P, 2, 2, P], F32, tag="xbank", bufs=2, name="x_bank"))
-            bank = live[("xt", i)]
+            key = ("xt", i, g if i == 0 else 0)
+            if key not in live:
+                live.setdefault(key, psum.tile([P, 2, 2, P], F32, tag="xbank", bufs=2, name="x_bank"))
+            bank = live[key]
             words = xw[:, i, g * 512 : (g + 1) * 512].bitcast(F32)
             for u in range(2):
                 src = words[:, u:256:2] if (i, g) in SCALAR_WIDENS else words[:, u * P : (u + 1) * P]
                 nc.tensor.transpose(bank[:, g, u, :], src, ident32[:])
 
-        def empty_x(i):
+        def empty_x(i, first=None):
+            g0, g1 = (0, 2) if i else ((0, 1) if first == 0 else (1, 2))
             nc.scalar.copy(
-                out=xg[:, i, :].bitcast(F32).rearrange("p (g r u) -> p g r u", g=2, u=2),
-                in_=live[("xt", i)][:].rearrange("p g u r -> p g r u"),
+                out=xg[:, i, g0 * 512 : g1 * 512].bitcast(F32).rearrange("p (g r u) -> p g r u", r=P, u=2),
+                in_=live[("xt", i, g0)][:, g0:g1].rearrange("p g u r -> p g r u"),
             )
 
-        def quant_x(i):
-            nc.vector.quantize_mx(out=xq[:, i, :].bitcast(FP8X4), scales=xq_s[:, i, :], in_=xg[:, i, :])
+        def quant_x(i, first=None):
+            g0, g1 = (0, 2) if i else ((0, 1) if first == 0 else (1, 2))
+            nc.vector.quantize_mx(
+                out=xq[:, i, g0 * P : g1 * P].bitcast(FP8X4),
+                scales=xq_s[:, i, g0 * P : g1 * P],
+                in_=xg[:, i, g0 * 512 : g1 * 512],
+            )
+
+        def warm_up(count):
+            bank = psum.tile([P, 512], F32, tag="pbank", bufs=1, name="warm_bank")
+            for n in range(count):
+                nc.tensor.matmul(bank[:], lhsT=warm[:, 0:P], rhs=warm[:], start=True, stop=True)
 
         def down(i):
             bank = psum.tile([P, 4, P], F32, tag="pbank", bufs=1, name="p_bank")
@@ -247,25 +262,31 @@ def tile_moslorasubspacemixerrankgain_d2p_kernel(
                 stop=True,
             )
 
+        def pieces(i, h):
+            width = 256 if (i, h) == (7, 1) else 512
+            return [(c, c + width) for c in range(0, 512, width)]
+
         def finish(i, h):
-            cols = slice(h * 512, (h + 1) * 512)
-            nc.vector.scalar_tensor_tensor(
-                out=res[:, i, cols],
-                in0=live[("t", i, h)][:],
-                scalar=1.0 / math.sqrt(R),
-                in1=res[:, i, cols],
-                op0=ALU.mult,
-                op1=ALU.add,
-            )
+            for c0, c1 in pieces(i, h):
+                cols = slice(h * 512 + c0, h * 512 + c1)
+                nc.vector.scalar_tensor_tensor(
+                    out=res[:, i, cols],
+                    in0=live[("t", i, h)][:, c0:c1],
+                    scalar=1.0 / math.sqrt(R),
+                    in1=res[:, i, cols],
+                    op0=ALU.mult,
+                    op1=ALU.add,
+                )
 
         def store(i, h):
-            cols = slice(h * 512, (h + 1) * 512)
-            nc.sync.dma_start(out=out[i * P : (i + 1) * P, cols], in_=res[:, i, cols])
+            for c0, c1 in pieces(i, h):
+                cols = slice(h * 512 + c0, h * 512 + c1)
+                nc.sync.dma_start(out=out[i * P : (i + 1) * P, cols], in_=res[:, i, cols])
 
         steps = {
             "W": widen, "T": turn_x, "E": empty_x, "Q": quant_x, "P": down, "PE": gain, "QP": quant_p,
             "B": base, "BE": empty_base, "C": mix, "CE": empty_c, "CQ": quant_c,
-            "M": up, "F": finish, "ST": store, "pa": permute_a, "pm": permute_m, "TD": turn_d, "TDc": empty_d,
+            "M": up, "F": finish, "ST": store, "pa": permute_a, "pm": permute_m, "D": warm_up, "TD": turn_d, "TDc": empty_d,
         }
         for step in ORDER:
             steps[step[0]](*step[1:])

@@ -19,8 +19,8 @@ ALU = mybir.AluOpType
 ACT = mybir.ActivationFunctionType
 
 P = 128
-SCALAR_WIDENS = [(0, 1),(1, 1)]
-ORDER = [("D",3,),("W",0,0,),("W",0,1,),("T",0,0,),("T",0,1,),("D",2,),("E",0,0,),("W",1,0,),("E",0,),("Q",0,0,),("W",1,1,),("Q",0,),("pa",),("B",0,0,),("W",2,0,),("T",1,0,),("W",2,1,),("T",1,1,),("BE",0,0,),("W",3,0,),("TD",),("P",0,),("E",1,),("W",3,1,),("B",0,1,),("TDc",),("Q",1,),("PE",0,),("T",2,0,),("T",2,1,),("BE",0,1,),("T",3,0,),("pm",),("T",3,1,),("B",1,0,),("W",4,0,),("E",2,),("W",4,1,),("E",3,),("P",1,),("BE",1,0,),("B",1,1,),("PE",1,),("C",0,0,),("BE",1,1,),("Q",2,),("C",0,1,),("W",5,0,),("CE",0,0,),("P",2,),("Q",3,),("W",5,1,),("CE",0,1,),("C",0,2,),("QP",0,),("PE",2,),("B",2,0,),("CE",0,2,),("QP",1,),("C",0,3,),("W",6,0,),("BE",2,0,),("T",4,0,),("W",6,1,),("T",4,1,),("T",5,0,),("CE",0,3,),("T",5,1,),("P",3,),("E",4,),("CQ",0,),("C",1,0,),("E",5,),("W",7,0,),("B",2,1,),("CE",1,0,),("W",7,1,),("C",1,1,),("QP",2,),("BE",2,1,),("M",0,0,),("PE",3,),("C",1,2,),("CE",1,1,),("Q",4,),("B",3,0,),("F",0,0,),("CE",1,2,),("C",1,3,),("Q",5,),("M",1,0,),("BE",3,0,),("ST",0,0,),("QP",3,),("P",4,),("F",1,0,),("CE",1,3,),("T",6,0,),("T",6,1,),("PE",4,),("T",7,0,),("ST",1,0,),("T",7,1,),("E",6,),("M",2,0,),("CQ",1,),("B",3,1,),("E",7,),("F",2,0,),("M",3,0,),("P",5,),("BE",3,1,),("QP",4,),("ST",2,0,),("F",3,0,),("B",4,0,),("Q",6,),("ST",3,0,),("PE",5,),("M",0,1,),("M",1,1,),("BE",4,0,),("Q",7,),("B",4,1,),("F",0,1,),("M",2,1,),("QP",5,),("P",6,),("BE",4,1,),("F",1,1,),("ST",0,1,),("B",5,0,),("F",2,1,),("ST",1,1,),("M",3,1,),("PE",6,),("ST",2,1,),("M",4,0,),("BE",5,0,),("B",5,1,),("F",3,1,),("M",4,1,),("QP",6,),("F",4,0,),("P",7,),("ST",3,1,),("BE",5,1,),("F",4,1,),("B",6,0,),("ST",4,0,),("PE",7,),("M",5,0,),("ST",4,1,),("M",5,1,),("BE",6,0,),("B",6,1,),("F",5,0,),("M",6,0,),("QP",7,),("F",5,1,),("B",7,0,),("ST",5,0,),("BE",6,1,),("F",6,0,),("M",6,1,),("ST",5,1,),("B",7,1,),("BE",7,0,),("F",6,1,),("ST",6,0,),("M",7,0,),("M",7,1,),("BE",7,1,),("ST",6,1,),("F",7,0,),("F",7,1,),("ST",7,0,),("ST",7,1,)]
+SCALAR_WIDENS = [(0, 1)]
+ORDER = [("D",4,),("W",0,0,),("W",0,1,),("W",1,0,),("T",0,0,),("W",1,1,),("T",0,1,),("D",2,),("E",0,0,),("E",0,),("T",1,0,),("Q",0,0,),("T",1,1,),("Q",0,),("E",1,),("pa",),("B",0,0,),("W",2,0,),("P",0,),("W",2,1,),("BE",0,0,),("W",3,0,),("B",0,1,),("W",3,1,),("TD",),("Q",1,),("T",2,0,),("T",2,1,),("W",4,0,),("TDc",),("T",3,0,),("BE",0,1,),("T",3,1,),("PE",0,),("B",1,0,),("E",2,),("W",4,1,),("B",1,1,),("E",3,),("Q",2,),("P",1,),("pm",),("BE",1,0,),("W",5,0,),("C",0,0,),("BE",1,1,),("Q",3,),("C",0,1,),("PE",1,),("CE",0,0,),("C",0,2,),("W",5,1,),("B",2,0,),("CE",0,1,),("QP",0,),("W",6,0,),("C",0,3,),("CE",0,2,),("W",6,1,),("C",1,0,),("P",2,),("QP",1,),("CE",0,3,),("W",7,0,),("BE",2,0,),("T",4,0,),("T",4,1,),("PE",2,),("T",5,0,),("CE",1,0,),("T",5,1,),("C",1,1,),("W",7,1,),("E",4,),("B",2,1,),("CQ",0,),("E",5,),("C",1,2,),("QP",2,),("Q",4,),("CE",1,1,),("P",3,),("Q",5,),("BE",2,1,),("M",0,0,),("M",1,0,),("PE",3,),("CE",1,2,),("T",6,0,),("T",6,1,),("F",0,0,),("T",7,0,),("T",7,1,),("C",1,3,),("QP",3,),("F",1,0,),("ST",0,0,),("M",2,0,),("P",4,),("CE",1,3,),("F",2,0,),("ST",1,0,),("E",6,),("B",3,0,),("CQ",1,),("ST",2,0,),("E",7,),("B",3,1,),("PE",4,),("BE",3,0,),("B",4,0,),("Q",6,),("BE",3,1,),("QP",4,),("M",3,0,),("Q",7,),("M",0,1,),("BE",4,0,),("M",1,1,),("F",3,0,),("P",5,),("F",0,1,),("ST",3,0,),("M",2,1,),("B",4,1,),("PE",5,),("ST",0,1,),("M",3,1,),("F",1,1,),("B",5,0,),("BE",4,1,),("QP",5,),("F",2,1,),("P",6,),("ST",1,1,),("BE",5,0,),("F",3,1,),("M",4,0,),("ST",2,1,),("M",4,1,),("B",5,1,),("F",4,0,),("ST",3,1,),("B",6,0,),("PE",6,),("ST",4,0,),("BE",5,1,),("M",5,0,),("F",4,1,),("P",7,),("BE",6,0,),("QP",6,),("F",5,0,),("ST",4,1,),("M",5,1,),("B",6,1,),("PE",7,),("ST",5,0,),("M",6,0,),("F",5,1,),("B",7,0,),("BE",6,1,),("QP",7,),("F",6,0,),("M",6,1,),("ST",5,1,),("B",7,1,),("BE",7,0,),("F",6,1,),("ST",6,0,),("M",7,0,),("M",7,1,),("BE",7,1,),("ST",6,1,),("F",7,0,),("F",7,1,),("ST",7,0,),("ST",7,1,)]
 
 
 def tile_moslorasubspacemixerrankgain_d2p_kernel(
@@ -88,9 +88,9 @@ def tile_moslorasubspacemixerrankgain_d2p_kernel(
 
         nc.sync.dma_start(out=xs[:], in_=x_scale.rearrange("i j -> (i j)").partition_broadcast(P))
         load_x(0, 1)
+        load_x(1, 2)
         load_scales(nc.sync, w0_s, w0_scales)
         load_words(w0_w[:, :, 0:1024], w0_words[:, :, 0:1024])
-        load_x(1, 2)
         load_scales(nc.sync, a_sraw, a_scales)
         load_words(a_raw[:], a_words)
         load_x(2, 4)
@@ -193,9 +193,9 @@ def tile_moslorasubspacemixerrankgain_d2p_kernel(
 
         def gain(i):
             nc.vector.tensor_tensor(
-                out=pg[:, i, :].rearrange("p (n t) -> p n t", t=4),
-                in0=live[("p", i)][:].rearrange("p t n -> p n t"),
-                in1=d_cols[:].unsqueeze(1).to_broadcast([P, P, 4]),
+                out=pg[:, i, :].rearrange("p (c n t) -> p c t n", n=2, t=4),
+                in0=live[("p", i)][:].rearrange("p t (c n) -> p c t n", n=2),
+                in1=d_cols[:].unsqueeze(1).unsqueeze(3).to_broadcast([P, 64, 4, 2]),
                 op=ALU.mult,
             )
 

@@ -19,8 +19,11 @@ ALU = mybir.AluOpType
 ACT = mybir.ActivationFunctionType
 
 P = 128
-SCALAR_WIDENS = [(0, 1)]
-ORDER = [("D",4,),("W",0,0,),("W",0,1,),("W",1,0,),("T",0,0,),("W",1,1,),("T",0,1,),("D",2,),("E",0,0,),("E",0,),("T",1,0,),("Q",0,0,),("T",1,1,),("Q",0,),("E",1,),("pa",),("B",0,0,),("W",2,0,),("P",0,),("W",2,1,),("BE",0,0,),("W",3,0,),("B",0,1,),("W",3,1,),("TD",),("Q",1,),("T",2,0,),("T",2,1,),("W",4,0,),("TDc",),("T",3,0,),("BE",0,1,),("T",3,1,),("PE",0,),("B",1,0,),("E",2,),("W",4,1,),("B",1,1,),("E",3,),("Q",2,),("P",1,),("pm",),("BE",1,0,),("W",5,0,),("C",0,0,),("BE",1,1,),("Q",3,),("C",0,1,),("PE",1,),("CE",0,0,),("C",0,2,),("W",5,1,),("B",2,0,),("CE",0,1,),("QP",0,),("W",6,0,),("C",0,3,),("CE",0,2,),("W",6,1,),("C",1,0,),("P",2,),("QP",1,),("CE",0,3,),("W",7,0,),("BE",2,0,),("T",4,0,),("T",4,1,),("PE",2,),("T",5,0,),("CE",1,0,),("T",5,1,),("C",1,1,),("W",7,1,),("E",4,),("B",2,1,),("CQ",0,),("E",5,),("C",1,2,),("QP",2,),("Q",4,),("CE",1,1,),("P",3,),("Q",5,),("BE",2,1,),("M",0,0,),("M",1,0,),("PE",3,),("CE",1,2,),("T",6,0,),("T",6,1,),("F",0,0,),("T",7,0,),("T",7,1,),("C",1,3,),("QP",3,),("F",1,0,),("ST",0,0,),("M",2,0,),("P",4,),("CE",1,3,),("F",2,0,),("ST",1,0,),("E",6,),("B",3,0,),("CQ",1,),("ST",2,0,),("E",7,),("B",3,1,),("PE",4,),("BE",3,0,),("B",4,0,),("Q",6,),("BE",3,1,),("QP",4,),("M",3,0,),("Q",7,),("M",0,1,),("BE",4,0,),("M",1,1,),("F",3,0,),("P",5,),("F",0,1,),("ST",3,0,),("M",2,1,),("B",4,1,),("PE",5,),("ST",0,1,),("M",3,1,),("F",1,1,),("B",5,0,),("BE",4,1,),("QP",5,),("F",2,1,),("P",6,),("ST",1,1,),("BE",5,0,),("F",3,1,),("M",4,0,),("ST",2,1,),("M",4,1,),("B",5,1,),("F",4,0,),("ST",3,1,),("B",6,0,),("PE",6,),("ST",4,0,),("BE",5,1,),("M",5,0,),("F",4,1,),("P",7,),("BE",6,0,),("QP",6,),("F",5,0,),("ST",4,1,),("M",5,1,),("B",6,1,),("PE",7,),("ST",5,0,),("M",6,0,),("F",5,1,),("B",7,0,),("BE",6,1,),("QP",7,),("F",6,0,),("M",6,1,),("ST",5,1,),("B",7,1,),("BE",7,0,),("F",6,1,),("ST",6,0,),("M",7,0,),("M",7,1,),("BE",7,1,),("ST",6,1,),("F",7,0,),("F",7,1,),("ST",7,0,),("ST",7,1,)]
+TILES = N // P
+BANKS = 8
+EARLY = 2
+WARM_UPS = 4
+ALPHA = 1.0 / math.sqrt(R)
 
 
 def tile_moslorasubspacemixerrankgain_d2p_kernel(
@@ -29,55 +32,72 @@ def tile_moslorasubspacemixerrankgain_d2p_kernel(
     nc = tc.nc
     with ExitStack() as ctx:
         keep = ctx.enter_context(tc.tile_pool(name="keep", bufs=1))
-        work = ctx.enter_context(tc.tile_pool(name="work", bufs=3))
         psum = ctx.enter_context(tc.psum_pool(name="psum", bufs=1))
         ctx.enter_context(tc.manual_schedule())
 
-        ident32 = keep.tile([P, P], F32, align_bytes=64)
-        ident16 = keep.tile([P, P], BF16, align_bytes=64)
-        d_rows = keep.tile([P, P], BF16, align_bytes=64)
-        warm = keep.tile([P, 512], BF16, align_bytes=64)
-        d_cols = keep.tile([P, 4], F32, align_bytes=64)
-        xs = keep.tile([P, 64], F32, align_bytes=64)
-        xb = keep.tile([P, 8, 1024], U8, align_bytes=64)
-        a_raw = keep.tile([P, 2, 1024], U8, align_bytes=64)
-        a_w = keep.tile([P, 2, 1024], U8, align_bytes=64)
-        a_sraw = keep.tile([P, 2, 512], U8, align_bytes=64)
-        a_s = keep.tile([P, 2, 512], U8, align_bytes=64)
-        m_raw = keep.tile([P, 1, 1024], U8, align_bytes=64)
-        m_w = keep.tile([P, 1, 1024], U8, align_bytes=64)
-        m_sraw = keep.tile([P, 1, 512], U8, align_bytes=64)
-        m_s = keep.tile([P, 1, 512], U8, align_bytes=64)
-        w0_w = keep.tile([P, 2, 2048], U8, align_bytes=64)
-        w0_s = keep.tile([P, 2, 1024], U8, align_bytes=64)
-        bu_w = keep.tile([P, 1, 2048], U8, align_bytes=64)
-        bu_s = keep.tile([P, 1, 1024], U8, align_bytes=64)
-        xq = keep.tile([P, 8, 256], U32, align_bytes=64)
-        xq_s = keep.tile([P, 8, 256], U8, align_bytes=64)
-        pq = keep.tile([P, 8, 128], U32, align_bytes=64)
-        pq_s = keep.tile([P, 8, 128], U8, align_bytes=64)
-        cq = keep.tile([P, 1024], U32, align_bytes=64)
-        cq_s = keep.tile([P, 1024], U8, align_bytes=64)
-        c_grouped = keep.tile([P, 2, 2048], BF16, align_bytes=64)
-        res = keep.tile([P, 8, 1024], F32, align_bytes=64)
-        xw = keep.tile([P, 8, 1024], BF16, align_bytes=64)
-        xg = keep.tile([P, 8, 1024], BF16, align_bytes=64)
-        pg = keep.tile([P, 8, 512], BF16, align_bytes=64)
+        def sbuf(name, shape, dtype):
+            return keep.tile([P] + shape, dtype, align_bytes=64, name=name)
 
-        def load_scales(queue, plane, src):
+        def per_tile(name, shape, dtype, count=TILES):
+            return [sbuf("%s%d" % (name, i), shape, dtype) for i in range(count)]
+
+        ident32 = sbuf("ident32", [P], F32)
+        ident16 = sbuf("ident16", [P], BF16)
+        d_rows = sbuf("d_rows", [P], BF16)
+        d_cols = sbuf("d_cols", [4], F32)
+        warm = sbuf("warm", [512], BF16)
+        xs = sbuf("xs", [8], F32)
+        x_loads = [(0, 2), (2, 4), (4, 8)]
+        xb_parts = [sbuf("xb%d" % i0, [i1 - i0, D], U8) for i0, i1 in x_loads]
+        xb = [part[:, i - i0, :] for part, (i0, i1) in zip(xb_parts, x_loads) for i in range(i0, i1)]
+        a_raw = sbuf("a_raw", [2, 1024], U8)
+        a_w = sbuf("a_w", [2, 1024], U8)
+        a_sraw = sbuf("a_sraw", [2, 512], U8)
+        a_s = sbuf("a_s", [2, 512], U8)
+        m_raw = sbuf("m_raw", [1, 1024], U8)
+        m_w = sbuf("m_w", [1, 1024], U8)
+        m_sraw = sbuf("m_sraw", [1, 512], U8)
+        m_s = sbuf("m_s", [1, 512], U8)
+        w0_w = per_tile("w0_w", [2, 1024], U8, 2)
+        w0_s = sbuf("w0_s", [2, 1024], U8)
+        bu_w = sbuf("bu_w", [1, 2048], U8)
+        bu_s = sbuf("bu_s", [1, 1024], U8)
+        xw = per_tile("xw", [D], BF16)
+        xg = per_tile("xg", [D], BF16)
+        xq = per_tile("xq", [256], U32)
+        xq_s = per_tile("xq_s", [256], U8)
+        pg = per_tile("pg", [R], BF16)
+        pq = per_tile("pq", [P], U32)
+        pq_s = per_tile("pq_s", [P], U8)
+        cg = per_tile("cg", [2048], BF16, 2)
+        cq = per_tile("cq", [512], U32, 2)
+        cq_s = per_tile("cq_s", [512], U8, 2)
+        res = [per_tile("res%d_" % h, [512], F32) for h in range(2)]
+        banks = [psum.tile([P, 512], F32, name="bank%d" % b) for b in range(BANKS)]
+
+        x_rows = x_bytes.rearrange("(p i) k -> p i k", i=TILES)
+        out_rows = out.rearrange("(p i) f -> p i f", i=TILES)
+
+        held = {}
+
+        def next_bank(key):
+            held.setdefault(key, banks[len(held) % BANKS])
+            return held[key]
+
+        def load_scales(plane, src):
             rows = src.bitcast(I32).rearrange("g (q j) n -> j q g n", j=4)
             for j in range(4):
-                queue.dma_start(out=plane[j:P:32].bitcast(I32), in_=rows[j])
+                nc.sync.dma_start(out=plane[j:P:32].bitcast(I32), in_=rows[j])
 
-        def load_x(i0, i1):
-            nc.sync.dma_start(out=xb[:, i0:i1, :], in_=x_bytes[i0 * P : i1 * P, :].rearrange("(i p) k -> p i k", p=P))
+        def load_x(n):
+            i0, i1 = x_loads[n]
+            nc.sync.dma_start(out=xb_parts[n][:], in_=x_rows[:, i0:i1, :])
 
         def load_words(dst, src):
             nc.sync.dma_start(out=dst.bitcast(I32), in_=src.rearrange("g p n -> p g n").bitcast(I32))
 
         nc.vector.memset(warm[:], 0.0)
-        nc.vector.memset(w0_s[:].bitcast(I32), 0)
-        for plane in (a_sraw, m_sraw, bu_s):
+        for plane in (w0_s, m_sraw, bu_s, a_sraw):
             nc.vector.memset(plane[:].bitcast(I32), 0)
         make_identity(nc, ident32[:])
         nc.gpsimd.memset(d_rows[:], 0.0)
@@ -86,207 +106,235 @@ def tile_moslorasubspacemixerrankgain_d2p_kernel(
         )
         nc.scalar.copy(out=ident16[:], in_=ident32[:])
 
-        nc.sync.dma_start(out=xs[:], in_=x_scale.rearrange("i j -> (i j)").partition_broadcast(P))
-        load_x(0, 1)
-        load_x(1, 2)
-        load_scales(nc.sync, w0_s, w0_scales)
-        load_words(w0_w[:, :, 0:1024], w0_words[:, :, 0:1024])
-        load_scales(nc.sync, a_sraw, a_scales)
-        load_words(a_raw[:], a_words)
-        load_x(2, 4)
-        load_words(w0_w[:, :, 1024:2048], w0_words[:, :, 1024:2048])
+        nc.sync.dma_start(out=xs[:], in_=x_scale.unsqueeze(1).to_broadcast([8, 16, 8]))
+        load_x(0)
+        load_scales(w0_s, w0_scales)
+        for h in range(2):
+            load_words(w0_w[h][:], w0_words[:, :, h * 1024 : (h + 1) * 1024])
+        load_x(1)
         load_words(m_raw[:], m_words)
-        load_x(4, 6)
-        load_scales(nc.sync, m_sraw, m_scales)
-        load_scales(nc.sync, bu_s, bu_scales)
+        load_scales(m_sraw, m_scales)
+        load_x(2)
         load_words(bu_w[:], bu_words)
-        load_x(6, 8)
+        load_scales(bu_s, bu_scales)
+        load_words(a_raw[:], a_words)
+        load_scales(a_sraw, a_scales)
 
-        live = {}
+        def reorder(words, raw, scales, sraw):
+            for dst, src in ((words, raw), (scales, sraw)):
+                nc.vector.tensor_copy(
+                    out=dst[:].bitcast(I32).rearrange("p g (t q w) -> p g t q w", t=4, q=16),
+                    in_=src[:].bitcast(I32).rearrange("p g (q t w) -> p g t q w", t=4, q=16),
+                )
 
-        def permute(words, raw, scales, sraw, g):
-            nc.vector.tensor_copy(
-                out=words[:, g, :].bitcast(I32).rearrange("p (t q w) -> p t q w", t=4, q=16),
-                in_=raw[:, g, :].bitcast(I32).rearrange("p (q t w) -> p t q w", t=4, q=16),
-            )
-            nc.vector.tensor_copy(
-                out=scales[:, g, :].bitcast(I32).rearrange("p (t q w) -> p t q w", t=4, q=16),
-                in_=sraw[:, g, :].bitcast(I32).rearrange("p (q t w) -> p t q w", t=4, q=16),
-            )
-
-        def permute_a():
-            permute(a_w, a_raw, a_s, a_sraw, 0)
-            permute(a_w, a_raw, a_s, a_sraw, 1)
-
-        def permute_m():
-            permute(m_w, m_raw, m_s, m_sraw, 0)
+        def warm_up():
+            bank = next_bank("warm")
+            for n in range(WARM_UPS):
+                nc.tensor.matmul(bank[:], lhsT=warm[:, 0:P], rhs=warm[:], start=True, stop=True)
 
         def turn_d():
-            bank = psum.tile([P, P], BF16, tag="acc", bufs=5, name="d_bank")
-            live.setdefault("d", bank)
-            nc.tensor.transpose(bank[:], d_rows[:], ident16[:])
+            bank = next_bank("d")[:].bitcast(BF16)
+            nc.tensor.transpose(bank[:, 0:P], d_rows[:], ident16[:])
+            nc.scalar.copy(out=d_cols[:], in_=bank[:, 0:4])
 
-        def empty_d():
-            nc.scalar.copy(out=d_cols[:], in_=live["d"][:, 0:4])
-
-        def widen(i, g):
-            for b in range(4):
-                j = 4 * g + b
-                src = xb[:, i, j * P : (j + 1) * P].bitcast(FP8)
-                scale = xs[:, 8 * i + j : 8 * i + j + 1]
-                if (i, g) in SCALAR_WIDENS:
-                    nc.scalar.activation(out=xw[:, i, j * P : (j + 1) * P], in_=src, func=ACT.Copy, scale=scale)
-                else:
-                    dst = xw[:, i, g * 512 : (g + 1) * 512].rearrange("p (u q e) -> p q u e", u=2, e=2)
+        def widen(i, passes=(0, 1)):
+            for g in passes:
+                dst = xw[i][:, g * 512 : (g + 1) * 512].rearrange("p (u q e) -> p q u e", u=2, e=2)
+                for b in range(4):
+                    j = 4 * g + b
                     nc.vector.tensor_scalar(
                         out=dst[:, 32 * b : 32 * (b + 1)],
-                        in0=src.rearrange("p (q u e) -> p q u e", u=2, e=2),
-                        scalar1=scale,
+                        in0=xb[i][:, j * P : (j + 1) * P].bitcast(FP8).rearrange("p (q u e) -> p q u e", u=2, e=2),
+                        scalar1=xs[:, j : j + 1],
                         scalar2=None,
                         op0=ALU.mult,
                     )
 
-        def turn_x(i, g):
-            key = ("xt", i, g if i == 0 else 0)
-            if key not in live:
-                live.setdefault(key, psum.tile([P, 2, 2, P], F32, tag="xbank", bufs=2, name="x_bank"))
-            bank = live[key]
-            words = xw[:, i, g * 512 : (g + 1) * 512].bitcast(F32)
-            for u in range(2):
-                src = words[:, u:256:2] if (i, g) in SCALAR_WIDENS else words[:, u * P : (u + 1) * P]
-                nc.tensor.transpose(bank[:, g, u, :], src, ident32[:])
+        def turn_x(i, g0=0, g1=2):
+            bank = next_bank(("x", i, g0))
+            words = xw[i][:].bitcast(F32)
+            for n in range(2 * g0, 2 * g1):
+                nc.tensor.transpose(bank[:, n * P : (n + 1) * P], words[:, n * P : (n + 1) * P], ident32[:])
 
-        def empty_x(i, first=None):
-            g0, g1 = (0, 2) if i else ((0, 1) if first == 0 else (1, 2))
+        def empty_x(i, g0=0, g1=2):
             nc.scalar.copy(
-                out=xg[:, i, g0 * 512 : g1 * 512].bitcast(F32).rearrange("p (g r u) -> p g r u", r=P, u=2),
-                in_=live[("xt", i, g0)][:, g0:g1].rearrange("p g u r -> p g r u"),
+                out=xg[i][:, g0 * 512 : g1 * 512].bitcast(F32).rearrange("p (g r u) -> p g r u", r=P, u=2),
+                in_=held[("x", i, g0)][:, g0 * 256 : g1 * 256].rearrange("p (g u r) -> p g r u", u=2, r=P),
             )
 
-        def quant_x(i, first=None):
-            g0, g1 = (0, 2) if i else ((0, 1) if first == 0 else (1, 2))
+        def quant_x(i, g0=0, g1=2):
             nc.vector.quantize_mx(
-                out=xq[:, i, g0 * P : g1 * P].bitcast(FP8X4),
-                scales=xq_s[:, i, g0 * P : g1 * P],
-                in_=xg[:, i, g0 * 512 : g1 * 512],
+                out=xq[i][:, g0 * P : g1 * P].bitcast(FP8X4),
+                scales=xq_s[i][:, g0 * P : g1 * P],
+                in_=xg[i][:, g0 * 512 : g1 * 512],
             )
-
-        def warm_up(count):
-            bank = psum.tile([P, 512], F32, tag="pbank", bufs=1, name="warm_bank")
-            for n in range(count):
-                nc.tensor.matmul(bank[:], lhsT=warm[:, 0:P], rhs=warm[:], start=True, stop=True)
 
         def down(i):
-            bank = psum.tile([P, 4, P], F32, tag="pbank", bufs=1, name="p_bank")
-            live.setdefault(("p", i), bank)
+            bank = next_bank(("p", i))
             for t in range(4):
                 for g in range(2):
                     nc.tensor.matmul_mx(
-                        out=bank[:, t, :],
+                        out=bank[:, t * P : (t + 1) * P],
                         lhsT=a_w[:, g, t * 256 : (t + 1) * 256].bitcast(FP4X4),
                         lhsT_scale=a_s[:, g, t * P : (t + 1) * P],
-                        rhs=xq[:, i, g * P : (g + 1) * P].bitcast(FP8X4),
-                        rhs_scale=xq_s[:, i, g * P : (g + 1) * P],
+                        rhs=xq[i][:, g * P : (g + 1) * P].bitcast(FP8X4),
+                        rhs_scale=xq_s[i][:, g * P : (g + 1) * P],
                         start=(g == 0),
                         stop=(g == 1),
                     )
 
         def gain(i):
             nc.vector.tensor_tensor(
-                out=pg[:, i, :].rearrange("p (c n t) -> p c t n", n=2, t=4),
-                in0=live[("p", i)][:].rearrange("p t (c n) -> p c t n", n=2),
+                out=pg[i][:].rearrange("p (c n t) -> p c t n", n=2, t=4),
+                in0=held[("p", i)][:].rearrange("p (t c n) -> p c t n", t=4, n=2),
                 in1=d_cols[:].unsqueeze(1).unsqueeze(3).to_broadcast([P, 64, 4, 2]),
                 op=ALU.mult,
             )
 
         def quant_p(i):
-            nc.vector.quantize_mx(out=pq[:, i, :].bitcast(FP8X4), scales=pq_s[:, i, :], in_=pg[:, i, :])
+            nc.vector.quantize_mx(out=pq[i][:].bitcast(FP8X4), scales=pq_s[i][:], in_=pg[i][:])
 
-        def acc_bank(key):
-            bank = psum.tile([P, 512], F32, tag="acc", bufs=5, name="acc_bank")
-            live.setdefault(key, bank)
-            return bank
+        def mix(h):
+            for b in range(4):
+                bank = next_bank(("c", h, b))
+                f0 = h * 512 + b * P
+                for t in range(4):
+                    nc.tensor.matmul_mx(
+                        out=bank[:, t * P : (t + 1) * P],
+                        lhsT=m_w[:, 0, t * 256 : (t + 1) * 256].bitcast(FP4X4),
+                        lhsT_scale=m_s[:, 0, t * P : (t + 1) * P],
+                        rhs=bu_w[:, 0, 2 * f0 : 2 * (f0 + P)].bitcast(FP4X4),
+                        rhs_scale=bu_s[:, 0, f0 : f0 + P],
+                        start=(t == 0),
+                        stop=(t == 3),
+                    )
+                nc.scalar.copy(
+                    out=cg[h][:, b * 512 : (b + 1) * 512].rearrange("p (f t) -> p f t", t=4),
+                    in_=bank[:].rearrange("p (t f) -> p f t", t=4),
+                )
+
+        def quant_c(h):
+            nc.vector.quantize_mx(out=cq[h][:].bitcast(FP8X4), scales=cq_s[h][:], in_=cg[h][:])
 
         def base(i, h):
-            bank = acc_bank(("b", i, h))
+            bank = next_bank(("b", i, h))
             for g in range(2):
                 nc.tensor.matmul_mx(
                     out=bank[:],
-                    lhsT=xq[:, i, g * P : (g + 1) * P].bitcast(FP8X4),
-                    lhsT_scale=xq_s[:, i, g * P : (g + 1) * P],
-                    rhs=w0_w[:, g, h * 1024 : (h + 1) * 1024].bitcast(FP4X4),
+                    lhsT=xq[i][:, g * P : (g + 1) * P].bitcast(FP8X4),
+                    lhsT_scale=xq_s[i][:, g * P : (g + 1) * P],
+                    rhs=w0_w[h][:, g, :].bitcast(FP4X4),
                     rhs_scale=w0_s[:, g, h * 512 : (h + 1) * 512],
                     start=(g == 0),
                     stop=(g == 1),
                 )
-
-        def empty_base(i, h):
-            nc.scalar.copy(out=res[:, i, h * 512 : (h + 1) * 512], in_=live[("b", i, h)][:])
-
-        def mix(h, b):
-            bank = acc_bank(("c", h, b))
-            f0 = h * 512 + b * P
-            for t in range(4):
-                nc.tensor.matmul_mx(
-                    out=bank[:, t * P : (t + 1) * P],
-                    lhsT=m_w[:, 0, t * 256 : (t + 1) * 256].bitcast(FP4X4),
-                    lhsT_scale=m_s[:, 0, t * P : (t + 1) * P],
-                    rhs=bu_w[:, 0, 2 * f0 : 2 * (f0 + P)].bitcast(FP4X4),
-                    rhs_scale=bu_s[:, 0, f0 : f0 + P],
-                    start=(t == 0),
-                    stop=(t == 3),
-                )
-
-        def empty_c(h, b):
-            nc.scalar.copy(
-                out=c_grouped[:, h, b * 512 : (b + 1) * 512].rearrange("p (f t) -> p f t", t=4),
-                in_=live[("c", h, b)][:].rearrange("p (t f) -> p f t", t=4),
-            )
-
-        def quant_c(h):
-            nc.vector.quantize_mx(
-                out=cq[:, h * 512 : (h + 1) * 512].bitcast(FP8X4),
-                scales=cq_s[:, h * 512 : (h + 1) * 512],
-                in_=c_grouped[:, h, :],
-            )
+            if i < EARLY:
+                nc.scalar.copy(out=res[h][i][:], in_=bank[:])
 
         def up(i, h):
-            bank = acc_bank(("t", i, h))
+            bank = next_bank(("t", i, h))
             nc.tensor.matmul_mx(
                 out=bank[:],
-                lhsT=pq[:, i, :].bitcast(FP8X4),
-                lhsT_scale=pq_s[:, i, :],
-                rhs=cq[:, h * 512 : (h + 1) * 512].bitcast(FP8X4),
-                rhs_scale=cq_s[:, h * 512 : (h + 1) * 512],
+                lhsT=pq[i][:].bitcast(FP8X4),
+                lhsT_scale=pq_s[i][:],
+                rhs=cq[h][:].bitcast(FP8X4),
+                rhs_scale=cq_s[h][:],
                 start=True,
                 stop=True,
             )
-
-        def pieces(i, h):
-            width = 256 if (i, h) == (7, 1) else 512
-            return [(c, c + width) for c in range(0, 512, width)]
+            if i >= EARLY:
+                nc.scalar.activation(out=res[h][i][:], in_=bank[:], func=ACT.Copy, scale=ALPHA)
 
         def finish(i, h):
-            for c0, c1 in pieces(i, h):
-                cols = slice(h * 512 + c0, h * 512 + c1)
-                nc.vector.scalar_tensor_tensor(
-                    out=res[:, i, cols],
-                    in0=live[("t", i, h)][:, c0:c1],
-                    scalar=1.0 / math.sqrt(R),
-                    in1=res[:, i, cols],
-                    op0=ALU.mult,
-                    op1=ALU.add,
-                )
+            width = 256 if (i, h) == (TILES - 1, 1) else 512
+            for c0 in range(0, 512, width):
+                cols = slice(c0, c0 + width)
+                acc = res[h][i][:, cols]
+                if i < EARLY:
+                    nc.vector.scalar_tensor_tensor(
+                        out=acc, in0=held[("t", i, h)][:, cols], scalar=ALPHA, in1=acc, op0=ALU.mult, op1=ALU.add
+                    )
+                else:
+                    nc.vector.tensor_tensor(out=acc, in0=held[("b", i, h)][:, cols], in1=acc, op=ALU.add)
+                nc.sync.dma_start(out=out_rows[:, i, h * 512 + c0 : h * 512 + c0 + width], in_=acc)
 
-        def store(i, h):
-            for c0, c1 in pieces(i, h):
-                cols = slice(h * 512 + c0, h * 512 + c1)
-                nc.sync.dma_start(out=out[i * P : (i + 1) * P, cols], in_=res[:, i, cols])
-
-        steps = {
-            "W": widen, "T": turn_x, "E": empty_x, "Q": quant_x, "P": down, "PE": gain, "QP": quant_p,
-            "B": base, "BE": empty_base, "C": mix, "CE": empty_c, "CQ": quant_c,
-            "M": up, "F": finish, "ST": store, "pa": permute_a, "pm": permute_m, "D": warm_up, "TD": turn_d, "TDc": empty_d,
-        }
-        for step in ORDER:
-            steps[step[0]](*step[1:])
+        warm_up()
+        for g in range(2):
+            widen(0, (g,))
+            turn_x(0, g, g + 1)
+            empty_x(0, g, g + 1)
+        widen(1)
+        quant_x(0, 0, 1)
+        quant_x(0, 1, 2)
+        turn_x(1)
+        empty_x(1)
+        base(0, 0)
+        base(0, 1)
+        widen(2)
+        quant_x(1)
+        widen(3)
+        base(1, 0)
+        base(1, 1)
+        reorder(m_w, m_raw, m_s, m_sraw)
+        turn_x(2)
+        turn_x(3)
+        empty_x(2)
+        empty_x(3)
+        turn_d()
+        widen(4)
+        widen(5)
+        mix(0)
+        reorder(a_w, a_raw, a_s, a_sraw)
+        quant_x(2)
+        down(0)
+        widen(6)
+        quant_x(3)
+        gain(0)
+        mix(1)
+        widen(7)
+        quant_c(0)
+        quant_p(0)
+        down(1)
+        turn_x(4)
+        turn_x(5)
+        empty_x(4)
+        empty_x(5)
+        gain(1)
+        down(2)
+        up(0, 0)
+        quant_c(1)
+        quant_p(1)
+        gain(2)
+        up(1, 0)
+        down(3)
+        finish(0, 0)
+        quant_x(4)
+        finish(1, 0)
+        quant_p(2)
+        up(0, 1)
+        up(1, 1)
+        turn_x(6)
+        turn_x(7)
+        empty_x(6)
+        empty_x(7)
+        gain(3)
+        finish(0, 1)
+        quant_x(5)
+        finish(1, 1)
+        quant_p(3)
+        for i in range(EARLY, TILES):
+            ahead = i + 2
+            if ahead < TILES:
+                down(ahead)
+            up(i, 0)
+            up(i, 1)
+            base(i, 0)
+            base(i, 1)
+            if ahead < TILES:
+                gain(ahead)
+            if i + 4 < TILES:
+                quant_x(i + 4)
+            finish(i, 0)
+            if ahead < TILES:
+                quant_p(ahead)
+            finish(i, 1)

@@ -22,7 +22,6 @@ P = 128
 TILES = N // P
 BANKS = 8
 EARLY = 2
-WARM_UPS = 4
 ALPHA = 1.0 / math.sqrt(R)
 
 
@@ -47,7 +46,7 @@ def tile_moslorasubspacemixerrankgain_d2p_kernel(
         d_cols = sbuf("d_cols", [4], F32)
         warm = sbuf("warm", [512], BF16)
         xs = sbuf("xs", [8], F32)
-        x_loads = [(0, 2), (2, 4), (4, 8)]
+        x_loads = [(0, 1), (1, 3), (3, 5), (5, 8)]
         xb_parts = [sbuf("xb%d" % i0, [i1 - i0, D], U8) for i0, i1 in x_loads]
         xb = [part[:, i - i0, :] for part, (i0, i1) in zip(xb_parts, x_loads) for i in range(i0, i1)]
         a_raw = sbuf("a_raw", [2, 1024], U8)
@@ -78,11 +77,15 @@ def tile_moslorasubspacemixerrankgain_d2p_kernel(
         x_rows = x_bytes.rearrange("(p i) k -> p i k", i=TILES)
         out_rows = out.rearrange("(p i) f -> p i f", i=TILES)
 
+        free = list(banks)
         held = {}
 
         def next_bank(key):
-            held.setdefault(key, banks[len(held) % BANKS])
+            held.setdefault(key, free.pop(0))
             return held[key]
+
+        def release(key):
+            free.append(held[key])
 
         def load_scales(plane, src):
             rows = src.bitcast(I32).rearrange("g (q j) n -> j q g n", j=4)
@@ -96,29 +99,40 @@ def tile_moslorasubspacemixerrankgain_d2p_kernel(
         def load_words(dst, src):
             nc.sync.dma_start(out=dst.bitcast(I32), in_=src.rearrange("g p n -> p g n").bitcast(I32))
 
-        nc.vector.memset(warm[:], 0.0)
-        for plane in (w0_s, m_sraw, bu_s, a_sraw):
-            nc.vector.memset(plane[:].bitcast(I32), 0)
-        make_identity(nc, ident32[:])
-        nc.gpsimd.memset(d_rows[:], 0.0)
-        nc.gpsimd.dma_start(
-            out=d_rows[0:4, :].rearrange("t (q e) -> t q e", e=8), in_=d.rearrange("(q t e) -> t q e", t=4, e=8)
-        )
-        nc.scalar.copy(out=ident16[:], in_=ident32[:])
+        def load_xs():
+            nc.sync.dma_start(out=xs[:], in_=x_scale.unsqueeze(1).to_broadcast([8, 16, 8]))
 
-        nc.sync.dma_start(out=xs[:], in_=x_scale.unsqueeze(1).to_broadcast([8, 16, 8]))
+        def load_d():
+            nc.gpsimd.memset(d_rows[:], 0.0)
+            nc.gpsimd.dma_start(
+                out=d_rows[0:4, :].rearrange("t (q e) -> t q e", e=8), in_=d.rearrange("(q t e) -> t q e", t=4, e=8)
+            )
+
+        def zero(tile):
+            nc.vector.memset(tile[:].bitcast(I32), 0)
+
+        def identity():
+            make_identity(nc, ident32[:])
+            nc.scalar.activation(out=ident16[:], in_=ident32[:], func=ACT.Copy)
+
+        for tile in (w0_s, warm, m_sraw, bu_s, a_sraw):
+            zero(tile)
+        identity()
+        load_d()
         load_x(0)
+        load_xs()
+        load_x(1)
         load_scales(w0_s, w0_scales)
         for h in range(2):
             load_words(w0_w[h][:], w0_words[:, :, h * 1024 : (h + 1) * 1024])
-        load_x(1)
+        load_x(2)
         load_words(m_raw[:], m_words)
         load_scales(m_sraw, m_scales)
-        load_x(2)
         load_words(bu_w[:], bu_words)
         load_scales(bu_s, bu_scales)
         load_words(a_raw[:], a_words)
         load_scales(a_sraw, a_scales)
+        load_x(3)
 
         def reorder(words, raw, scales, sraw):
             for dst, src in ((words, raw), (scales, sraw)):
@@ -127,15 +141,17 @@ def tile_moslorasubspacemixerrankgain_d2p_kernel(
                     in_=src[:].bitcast(I32).rearrange("p g (q t w) -> p g t q w", t=4, q=16),
                 )
 
-        def warm_up():
-            bank = next_bank("warm")
-            for n in range(WARM_UPS):
+        def warm_up(count):
+            bank = next_bank(("warm", count))
+            for n in range(count):
                 nc.tensor.matmul(bank[:], lhsT=warm[:, 0:P], rhs=warm[:], start=True, stop=True)
+            release(("warm", count))
 
         def turn_d():
             bank = next_bank("d")[:].bitcast(BF16)
             nc.tensor.transpose(bank[:, 0:P], d_rows[:], ident16[:])
             nc.scalar.copy(out=d_cols[:], in_=bank[:, 0:4])
+            release("d")
 
         def widen(i, passes=(0, 1)):
             for g in passes:
@@ -161,6 +177,7 @@ def tile_moslorasubspacemixerrankgain_d2p_kernel(
                 out=xg[i][:, g0 * 512 : g1 * 512].bitcast(F32).rearrange("p (g r u) -> p g r u", r=P, u=2),
                 in_=held[("x", i, g0)][:, g0 * 256 : g1 * 256].rearrange("p (g u r) -> p g r u", u=2, r=P),
             )
+            release(("x", i, g0))
 
         def quant_x(i, g0=0, g1=2):
             nc.vector.quantize_mx(
@@ -190,6 +207,7 @@ def tile_moslorasubspacemixerrankgain_d2p_kernel(
                 in1=d_cols[:].unsqueeze(1).unsqueeze(3).to_broadcast([P, 64, 4, 2]),
                 op=ALU.mult,
             )
+            release(("p", i))
 
         def quant_p(i):
             nc.vector.quantize_mx(out=pq[i][:].bitcast(FP8X4), scales=pq_s[i][:], in_=pg[i][:])
@@ -212,6 +230,7 @@ def tile_moslorasubspacemixerrankgain_d2p_kernel(
                     out=cg[h][:, b * 512 : (b + 1) * 512].rearrange("p (f t) -> p f t", t=4),
                     in_=bank[:].rearrange("p (t f) -> p f t", t=4),
                 )
+                release(("c", h, b))
 
         def quant_c(h):
             nc.vector.quantize_mx(out=cq[h][:].bitcast(FP8X4), scales=cq_s[h][:], in_=cg[h][:])
@@ -230,6 +249,7 @@ def tile_moslorasubspacemixerrankgain_d2p_kernel(
                 )
             if i < EARLY:
                 nc.scalar.copy(out=res[h][i][:], in_=bank[:])
+                release(("b", i, h))
 
         def up(i, h):
             bank = next_bank(("t", i, h))
@@ -244,6 +264,7 @@ def tile_moslorasubspacemixerrankgain_d2p_kernel(
             )
             if i >= EARLY:
                 nc.scalar.activation(out=res[h][i][:], in_=bank[:], func=ACT.Copy, scale=ALPHA)
+                release(("t", i, h))
 
         def finish(i, h):
             width = 256 if (i, h) == (TILES - 1, 1) else 512
@@ -257,66 +278,68 @@ def tile_moslorasubspacemixerrankgain_d2p_kernel(
                 else:
                     nc.vector.tensor_tensor(out=acc, in0=held[("b", i, h)][:, cols], in1=acc, op=ALU.add)
                 nc.sync.dma_start(out=out_rows[:, i, h * 512 + c0 : h * 512 + c0 + width], in_=acc)
+            release(("t" if i < EARLY else "b", i, h))
 
-        warm_up()
+        warm_up(3)
         for g in range(2):
             widen(0, (g,))
             turn_x(0, g, g + 1)
             empty_x(0, g, g + 1)
         widen(1)
+        warm_up(2)
+        widen(2)
         quant_x(0, 0, 1)
         quant_x(0, 1, 2)
         turn_x(1)
         empty_x(1)
         base(0, 0)
         base(0, 1)
-        widen(2)
         quant_x(1)
         widen(3)
+        widen(4)
         base(1, 0)
         base(1, 1)
         reorder(m_w, m_raw, m_s, m_sraw)
         turn_x(2)
         turn_x(3)
-        empty_x(2)
-        empty_x(3)
+        turn_x(4)
         turn_d()
-        widen(4)
-        widen(5)
+        empty_x(2)
         mix(0)
         reorder(a_w, a_raw, a_s, a_sraw)
+        widen(5)
         quant_x(2)
-        down(0)
         widen(6)
-        quant_x(3)
-        gain(0)
+        down(0)
+        empty_x(3)
         mix(1)
+        gain(0)
         widen(7)
+        down(1)
         quant_c(0)
         quant_p(0)
-        down(1)
-        turn_x(4)
-        turn_x(5)
         empty_x(4)
-        empty_x(5)
-        gain(1)
         down(2)
+        gain(1)
+        quant_x(3)
         up(0, 0)
-        quant_c(1)
+        turn_x(5)
+        turn_x(6)
+        turn_x(7)
+        empty_x(5)
         quant_p(1)
         gain(2)
-        up(1, 0)
+        quant_c(1)
         down(3)
+        up(1, 0)
+        empty_x(6)
+        empty_x(7)
         finish(0, 0)
-        quant_x(4)
-        finish(1, 0)
         quant_p(2)
         up(0, 1)
         up(1, 1)
-        turn_x(6)
-        turn_x(7)
-        empty_x(6)
-        empty_x(7)
+        quant_x(4)
+        finish(1, 0)
         gain(3)
         finish(0, 1)
         quant_x(5)

@@ -22,6 +22,7 @@ P = 128
 TILES = N // P
 BANKS = 8
 EARLY = 2
+VECTOR_EMPTIES = (3,)
 ALPHA = 1.0 / math.sqrt(R)
 
 
@@ -46,7 +47,7 @@ def tile_moslorasubspacemixerrankgain_d2p_kernel(
         d_cols = sbuf("d_cols", [4], F32)
         warm = sbuf("warm", [512], BF16)
         xs = sbuf("xs", [8], F32)
-        x_loads = [(0, 1), (1, 3), (3, 5), (5, 8)]
+        x_loads = [(0, 1), (1, 4), (4, 8)]
         xb_parts = [sbuf("xb%d" % i0, [i1 - i0, D], U8) for i0, i1 in x_loads]
         xb = [part[:, i - i0, :] for part, (i0, i1) in zip(xb_parts, x_loads) for i in range(i0, i1)]
         a_raw = sbuf("a_raw", [2, 1024], U8)
@@ -57,7 +58,7 @@ def tile_moslorasubspacemixerrankgain_d2p_kernel(
         m_w = sbuf("m_w", [1, 1024], U8)
         m_sraw = sbuf("m_sraw", [1, 512], U8)
         m_s = sbuf("m_s", [1, 512], U8)
-        w0_w = per_tile("w0_w", [2, 1024], U8, 2)
+        w0_w = sbuf("w0_w", [2, 2048], U8)
         w0_s = sbuf("w0_s", [2, 1024], U8)
         bu_w = sbuf("bu_w", [1, 2048], U8)
         bu_s = sbuf("bu_s", [1, 1024], U8)
@@ -123,8 +124,7 @@ def tile_moslorasubspacemixerrankgain_d2p_kernel(
         load_xs()
         load_x(1)
         load_scales(w0_s, w0_scales)
-        for h in range(2):
-            load_words(w0_w[h][:], w0_words[:, :, h * 1024 : (h + 1) * 1024])
+        load_words(w0_w[:], w0_words)
         load_x(2)
         load_words(m_raw[:], m_words)
         load_scales(m_sraw, m_scales)
@@ -132,7 +132,6 @@ def tile_moslorasubspacemixerrankgain_d2p_kernel(
         load_scales(bu_s, bu_scales)
         load_words(a_raw[:], a_words)
         load_scales(a_sraw, a_scales)
-        load_x(3)
 
         def reorder(words, raw, scales, sraw):
             for dst, src in ((words, raw), (scales, sraw)):
@@ -144,7 +143,7 @@ def tile_moslorasubspacemixerrankgain_d2p_kernel(
         def warm_up(count):
             bank = next_bank(("warm", count))
             for n in range(count):
-                nc.tensor.matmul(bank[:], lhsT=warm[:, 0:P], rhs=warm[:], start=True, stop=True)
+                nc.tensor.matmul(bank[:], lhsT=ident32[:].bitcast(BF16)[:, 0:P], rhs=warm[:], start=True, stop=True)
             release(("warm", count))
 
         def turn_d():
@@ -173,7 +172,8 @@ def tile_moslorasubspacemixerrankgain_d2p_kernel(
                 nc.tensor.transpose(bank[:, n * P : (n + 1) * P], words[:, n * P : (n + 1) * P], ident32[:])
 
         def empty_x(i, g0=0, g1=2):
-            nc.scalar.copy(
+            copy = nc.vector.tensor_copy if i in VECTOR_EMPTIES else nc.scalar.copy
+            copy(
                 out=xg[i][:, g0 * 512 : g1 * 512].bitcast(F32).rearrange("p (g r u) -> p g r u", r=P, u=2),
                 in_=held[("x", i, g0)][:, g0 * 256 : g1 * 256].rearrange("p (g u r) -> p g r u", u=2, r=P),
             )
@@ -242,7 +242,7 @@ def tile_moslorasubspacemixerrankgain_d2p_kernel(
                     out=bank[:],
                     lhsT=xq[i][:, g * P : (g + 1) * P].bitcast(FP8X4),
                     lhsT_scale=xq_s[i][:, g * P : (g + 1) * P],
-                    rhs=w0_w[h][:, g, :].bitcast(FP4X4),
+                    rhs=w0_w[:, g, h * 1024 : (h + 1) * 1024].bitcast(FP4X4),
                     rhs_scale=w0_s[:, g, h * 512 : (h + 1) * 512],
                     start=(g == 0),
                     stop=(g == 1),
@@ -287,49 +287,47 @@ def tile_moslorasubspacemixerrankgain_d2p_kernel(
             empty_x(0, g, g + 1)
         widen(1)
         warm_up(2)
-        widen(2)
         quant_x(0, 0, 1)
         quant_x(0, 1, 2)
         turn_x(1)
         empty_x(1)
+        widen(2)
         base(0, 0)
         base(0, 1)
         quant_x(1)
         widen(3)
         widen(4)
+        widen(5)
         base(1, 0)
         base(1, 1)
-        reorder(m_w, m_raw, m_s, m_sraw)
-        turn_x(2)
-        turn_x(3)
-        turn_x(4)
+        for i in range(2, 6):
+            turn_x(i)
         turn_d()
+        reorder(m_w, m_raw, m_s, m_sraw)
         empty_x(2)
+        widen(6)
+        widen(7)
         mix(0)
         reorder(a_w, a_raw, a_s, a_sraw)
-        widen(5)
         quant_x(2)
-        widen(6)
-        down(0)
         empty_x(3)
+        down(0)
         mix(1)
+        quant_x(3)
         gain(0)
-        widen(7)
         down(1)
         quant_c(0)
         quant_p(0)
         empty_x(4)
+        empty_x(5)
         down(2)
         gain(1)
-        quant_x(3)
         up(0, 0)
-        turn_x(5)
         turn_x(6)
         turn_x(7)
-        empty_x(5)
+        quant_c(1)
         quant_p(1)
         gain(2)
-        quant_c(1)
         down(3)
         up(1, 0)
         empty_x(6)

@@ -16,13 +16,11 @@ FP8 = mybir.dt.float8_e4m3fn
 FP8X4 = mybir.dt.float8_e4m3fn_x4
 FP4X4 = mybir.dt.float4_e2m1fn_x4
 ALU = mybir.AluOpType
-ACT = mybir.ActivationFunctionType
 
 P = 128
 TILES = N // P
 BANKS = 8
 EARLY = 2
-VECTOR_EMPTIES = (3,)
 ALPHA = 1.0 / math.sqrt(R)
 
 
@@ -114,9 +112,9 @@ def tile_moslorasubspacemixerrankgain_d2p_kernel(
 
         def identity():
             make_identity(nc, ident32[:])
-            nc.scalar.activation(out=ident16[:], in_=ident32[:], func=ACT.Copy)
+            nc.scalar.copy(out=ident16[:], in_=ident32[:])
 
-        for tile in (w0_s, warm, m_sraw, bu_s, a_sraw):
+        for tile in (w0_s, warm, a_sraw, m_sraw, bu_s):
             zero(tile)
         identity()
         load_d()
@@ -125,13 +123,13 @@ def tile_moslorasubspacemixerrankgain_d2p_kernel(
         load_x(1)
         load_scales(w0_s, w0_scales)
         load_words(w0_w[:], w0_words)
+        load_scales(a_sraw, a_scales)
         load_x(2)
-        load_words(m_raw[:], m_words)
+        load_words(a_raw[:], a_words)
         load_scales(m_sraw, m_scales)
+        load_words(m_raw[:], m_words)
         load_words(bu_w[:], bu_words)
         load_scales(bu_s, bu_scales)
-        load_words(a_raw[:], a_words)
-        load_scales(a_sraw, a_scales)
 
         def reorder(words, raw, scales, sraw):
             for dst, src in ((words, raw), (scales, sraw)):
@@ -172,8 +170,7 @@ def tile_moslorasubspacemixerrankgain_d2p_kernel(
                 nc.tensor.transpose(bank[:, n * P : (n + 1) * P], words[:, n * P : (n + 1) * P], ident32[:])
 
         def empty_x(i, g0=0, g1=2):
-            copy = nc.vector.tensor_copy if i in VECTOR_EMPTIES else nc.scalar.copy
-            copy(
+            nc.scalar.copy(
                 out=xg[i][:, g0 * 512 : g1 * 512].bitcast(F32).rearrange("p (g r u) -> p g r u", r=P, u=2),
                 in_=held[("x", i, g0)][:, g0 * 256 : g1 * 256].rearrange("p (g u r) -> p g r u", u=2, r=P),
             )
@@ -212,8 +209,8 @@ def tile_moslorasubspacemixerrankgain_d2p_kernel(
         def quant_p(i):
             nc.vector.quantize_mx(out=pq[i][:].bitcast(FP8X4), scales=pq_s[i][:], in_=pg[i][:])
 
-        def mix(h):
-            for b in range(4):
+        def mix(h, b0=0, b1=4, on_vector=()):
+            for b in range(b0, b1):
                 bank = next_bank(("c", h, b))
                 f0 = h * 512 + b * P
                 for t in range(4):
@@ -226,7 +223,8 @@ def tile_moslorasubspacemixerrankgain_d2p_kernel(
                         start=(t == 0),
                         stop=(t == 3),
                     )
-                nc.scalar.copy(
+                copy = nc.vector.tensor_copy if b in on_vector else nc.scalar.copy
+                copy(
                     out=cg[h][:, b * 512 : (b + 1) * 512].rearrange("p (f t) -> p f t", t=4),
                     in_=bank[:].rearrange("p (t f) -> p f t", t=4),
                 )
@@ -263,7 +261,7 @@ def tile_moslorasubspacemixerrankgain_d2p_kernel(
                 stop=True,
             )
             if i >= EARLY:
-                nc.scalar.activation(out=res[h][i][:], in_=bank[:], func=ACT.Copy, scale=ALPHA)
+                nc.scalar.copy(out=res[h][i][:], in_=bank[:])
                 release(("t", i, h))
 
         def finish(i, h):
@@ -272,11 +270,12 @@ def tile_moslorasubspacemixerrankgain_d2p_kernel(
                 cols = slice(c0, c0 + width)
                 acc = res[h][i][:, cols]
                 if i < EARLY:
-                    nc.vector.scalar_tensor_tensor(
-                        out=acc, in0=held[("t", i, h)][:, cols], scalar=ALPHA, in1=acc, op0=ALU.mult, op1=ALU.add
-                    )
+                    t_part, base_part = held[("t", i, h)][:, cols], acc
                 else:
-                    nc.vector.tensor_tensor(out=acc, in0=held[("b", i, h)][:, cols], in1=acc, op=ALU.add)
+                    t_part, base_part = acc, held[("b", i, h)][:, cols]
+                nc.vector.scalar_tensor_tensor(
+                    out=acc, in0=t_part, scalar=ALPHA, in1=base_part, op0=ALU.mult, op1=ALU.add
+                )
                 nc.sync.dma_start(out=out_rows[:, i, h * 512 + c0 : h * 512 + c0 + width], in_=acc)
             release(("t" if i < EARLY else "b", i, h))
 
@@ -297,65 +296,71 @@ def tile_moslorasubspacemixerrankgain_d2p_kernel(
         quant_x(1)
         widen(3)
         widen(4)
-        widen(5)
+        reorder(a_w, a_raw, a_s, a_sraw)
         base(1, 0)
         base(1, 1)
-        for i in range(2, 6):
+        for i in range(2, 5):
             turn_x(i)
         turn_d()
+        widen(5)
         reorder(m_w, m_raw, m_s, m_sraw)
-        empty_x(2)
+        for i in range(2, 5):
+            empty_x(i)
         widen(6)
-        widen(7)
-        mix(0)
-        reorder(a_w, a_raw, a_s, a_sraw)
-        quant_x(2)
-        empty_x(3)
         down(0)
-        mix(1)
-        quant_x(3)
-        gain(0)
         down(1)
-        quant_c(0)
-        quant_p(0)
-        empty_x(4)
-        empty_x(5)
-        down(2)
+        gain(0)
+        quant_x(2)
         gain(1)
-        up(0, 0)
-        turn_x(6)
-        turn_x(7)
-        quant_c(1)
+        quant_x(3)
+        mix(0, 0, 4, (0,))
+        quant_p(0)
+        widen(7)
         quant_p(1)
+        down(2)
+        mix(1, 0, 2)
         gain(2)
         down(3)
-        up(1, 0)
-        empty_x(6)
-        empty_x(7)
-        finish(0, 0)
-        quant_p(2)
-        up(0, 1)
-        up(1, 1)
-        quant_x(4)
-        finish(1, 0)
+        mix(1, 2, 4)
+        quant_c(0)
         gain(3)
-        finish(0, 1)
-        quant_x(5)
-        finish(1, 1)
+        quant_p(2)
+        up(0, 0)
+        for i in range(5, 8):
+            turn_x(i)
+        for i in range(5, 8):
+            empty_x(i)
+        up(1, 0)
+        quant_x(4)
         quant_p(3)
+        finish(0, 0)
+        quant_c(1)
+        finish(1, 0)
+        quant_x(5)
         for i in range(EARLY, TILES):
             ahead = i + 2
             if ahead < TILES:
                 down(ahead)
             up(i, 0)
-            up(i, 1)
+            if i == EARLY:
+                up(0, 1)
+            if i == TILES - 1:
+                up(i, 1)
             base(i, 0)
+            if i == EARLY:
+                up(1, 1)
+            if i < TILES - 1:
+                up(i, 1)
             base(i, 1)
             if ahead < TILES:
                 gain(ahead)
+            if i == EARLY:
+                finish(0, 1)
+                quant_p(ahead)
+                finish(1, 1)
             if i + 4 < TILES:
                 quant_x(i + 4)
             finish(i, 0)
-            if ahead < TILES:
+            if EARLY < i < TILES - 2:
                 quant_p(ahead)
             finish(i, 1)

@@ -285,10 +285,10 @@ def tile_moslorasubspacemixerrankgain_d2p_kernel(
             turn_x(0, g, g + 1)
             empty_x(0, g, g + 1)
         widen(1)
+        turn_x(1)
         warm_up(2)
         quant_x(0, 0, 1)
         quant_x(0, 1, 2)
-        turn_x(1)
         empty_x(1)
         widen(2)
         base(0, 0)
@@ -313,13 +313,13 @@ def tile_moslorasubspacemixerrankgain_d2p_kernel(
         quant_x(2)
         gain(1)
         quant_x(3)
-        mix(0, 0, 4, (0,))
+        mix(0, 0, 4)
         quant_p(0)
-        widen(7)
-        quant_p(1)
         down(2)
+        quant_p(1)
         mix(1, 0, 2)
         gain(2)
+        widen(7)
         down(3)
         mix(1, 2, 4)
         quant_c(0)

@@ -2,7 +2,6 @@ import math
 from contextlib import ExitStack
 
 import concourse.mybir as mybir
-from concourse.masks import make_identity
 
 N, D, F, R = 1024, 1024, 1024, 512
 FLOPS = 2 * N * D * F + 2 * N * D * R + 2 * R * R * F + 2 * N * R * F
@@ -40,6 +39,7 @@ def tile_moslorasubspacemixerrankgain_d2p_kernel(
             return [sbuf("%s%d" % (name, i), shape, dtype) for i in range(count)]
 
         ident32 = sbuf("ident32", [P], F32)
+        offsets = sbuf("offsets", [P], I32)
         ident16 = sbuf("ident16", [P], BF16)
         d_rows = sbuf("d_rows", [P], BF16)
         d_cols = sbuf("d_cols", [4], F32)
@@ -56,7 +56,7 @@ def tile_moslorasubspacemixerrankgain_d2p_kernel(
         m_w = sbuf("m_w", [1, 1024], U8)
         m_sraw = sbuf("m_sraw", [1, 512], U8)
         m_s = sbuf("m_s", [1, 512], U8)
-        w0_w = sbuf("w0_w", [2, 2048], U8)
+        w0_w = per_tile("w0_w", [2, 1024], U8, 2)
         w0_s = sbuf("w0_s", [2, 1024], U8)
         bu_w = sbuf("bu_w", [1, 2048], U8)
         bu_s = sbuf("bu_s", [1, 1024], U8)
@@ -86,10 +86,10 @@ def tile_moslorasubspacemixerrankgain_d2p_kernel(
         def release(key):
             free.append(held[key])
 
-        def load_scales(plane, src):
+        def load_scales(plane, src, queue=nc.sync, rows_j=range(4)):
             rows = src.bitcast(I32).rearrange("g (q j) n -> j q g n", j=4)
-            for j in range(4):
-                nc.sync.dma_start(out=plane[j:P:32].bitcast(I32), in_=rows[j])
+            for j in rows_j:
+                queue.dma_start(out=plane[j:P:32].bitcast(I32), in_=rows[j])
 
         def load_x(n):
             i0, i1 = x_loads[n]
@@ -99,10 +99,9 @@ def tile_moslorasubspacemixerrankgain_d2p_kernel(
             nc.sync.dma_start(out=dst.bitcast(I32), in_=src.rearrange("g p n -> p g n").bitcast(I32))
 
         def load_xs():
-            nc.sync.dma_start(out=xs[:], in_=x_scale.unsqueeze(1).to_broadcast([8, 16, 8]))
+            nc.scalar.dma_start(out=xs[:], in_=x_scale.unsqueeze(1).to_broadcast([8, 16, 8]))
 
         def load_d():
-            nc.gpsimd.memset(d_rows[:], 0.0)
             nc.gpsimd.dma_start(
                 out=d_rows[0:4, :].rearrange("t (q e) -> t q e", e=8), in_=d.rearrange("(q t e) -> t q e", t=4, e=8)
             )
@@ -111,25 +110,28 @@ def tile_moslorasubspacemixerrankgain_d2p_kernel(
             nc.vector.memset(tile[:].bitcast(I32), 0)
 
         def identity():
-            make_identity(nc, ident32[:])
-            nc.scalar.copy(out=ident16[:], in_=ident32[:])
+            nc.gpsimd.iota(offsets[:], pattern=[[1, P]], base=0, channel_multiplier=-1)
+            for ident in (ident32, ident16):
+                nc.vector.tensor_scalar(out=ident[:], in0=offsets[:], scalar1=0, scalar2=None, op0=ALU.is_equal)
 
-        for tile in (w0_s, warm, a_sraw, m_sraw, bu_s):
+        for tile in (warm, d_rows, w0_s, bu_s, a_sraw, m_sraw):
             zero(tile)
+        load_xs()
+        load_x(0)
         identity()
         load_d()
-        load_x(0)
-        load_xs()
+        load_scales(bu_s, bu_scales, nc.gpsimd, range(1))
         load_x(1)
         load_scales(w0_s, w0_scales)
-        load_words(w0_w[:], w0_words)
+        for h in range(2):
+            load_words(w0_w[h][:], w0_words[:, :, h * 1024 : (h + 1) * 1024])
         load_scales(a_sraw, a_scales)
         load_x(2)
         load_words(a_raw[:], a_words)
         load_scales(m_sraw, m_scales)
         load_words(m_raw[:], m_words)
         load_words(bu_w[:], bu_words)
-        load_scales(bu_s, bu_scales)
+        load_scales(bu_s, bu_scales, nc.sync, range(1, 4))
 
         def reorder(words, raw, scales, sraw):
             for dst, src in ((words, raw), (scales, sraw)):
@@ -141,7 +143,7 @@ def tile_moslorasubspacemixerrankgain_d2p_kernel(
         def warm_up(count):
             bank = next_bank(("warm", count))
             for n in range(count):
-                nc.tensor.matmul(bank[:], lhsT=ident32[:].bitcast(BF16)[:, 0:P], rhs=warm[:], start=True, stop=True)
+                nc.tensor.matmul(bank[:], lhsT=warm[:, 0:P], rhs=warm[:], start=True, stop=True)
             release(("warm", count))
 
         def turn_d():
@@ -240,7 +242,7 @@ def tile_moslorasubspacemixerrankgain_d2p_kernel(
                     out=bank[:],
                     lhsT=xq[i][:, g * P : (g + 1) * P].bitcast(FP8X4),
                     lhsT_scale=xq_s[i][:, g * P : (g + 1) * P],
-                    rhs=w0_w[:, g, h * 1024 : (h + 1) * 1024].bitcast(FP4X4),
+                    rhs=w0_w[h][:, g, :].bitcast(FP4X4),
                     rhs_scale=w0_s[:, g, h * 512 : (h + 1) * 512],
                     start=(g == 0),
                     stop=(g == 1),
@@ -279,21 +281,21 @@ def tile_moslorasubspacemixerrankgain_d2p_kernel(
                 nc.sync.dma_start(out=out_rows[:, i, h * 512 + c0 : h * 512 + c0 + width], in_=acc)
             release(("t" if i < EARLY else "b", i, h))
 
-        warm_up(3)
-        for g in range(2):
-            widen(0, (g,))
-            turn_x(0, g, g + 1)
-            empty_x(0, g, g + 1)
-        widen(1)
-        turn_x(1)
-        warm_up(2)
+        warm_up(4)
+        for i in range(EARLY):
+            for g in range(2):
+                widen(i, (g,))
+                turn_x(i, g, g + 1)
+                empty_x(i, g, g + 1)
+            if i == 0:
+                warm_up(2)
         quant_x(0, 0, 1)
         quant_x(0, 1, 2)
-        empty_x(1)
-        widen(2)
+        for g in range(2):
+            widen(2, (g,))
+            quant_x(1, g, g + 1)
         base(0, 0)
         base(0, 1)
-        quant_x(1)
         widen(3)
         widen(4)
         reorder(a_w, a_raw, a_s, a_sraw)

@@ -15,11 +15,12 @@ FP8 = mybir.dt.float8_e4m3fn
 FP8X4 = mybir.dt.float8_e4m3fn_x4
 FP4X4 = mybir.dt.float4_e2m1fn_x4
 ALU = mybir.AluOpType
+ACT = mybir.ActivationFunctionType
 
 P = 128
 TILES = N // P
 BANKS = 8
-EARLY = 2
+WIDE = 4
 ALPHA = 1.0 / math.sqrt(R)
 
 
@@ -58,12 +59,16 @@ def tile_moslorasubspacemixerrankgain_d2p_kernel(
         m_s = sbuf("m_s", [1, 512], U8)
         w0_w = per_tile("w0_w", [2, 1024], U8, 2)
         w0_s = sbuf("w0_s", [2, 1024], U8)
-        bu_w = sbuf("bu_w", [1, 2048], U8)
+        bu_all = sbuf("bu_all", [1, 2048], U8)
+        bu_w = [bu_all[:, :, h * 1024 : (h + 1) * 1024] for h in range(2)]
         bu_s = sbuf("bu_s", [1, 1024], U8)
         xw = per_tile("xw", [D], BF16)
         xg = per_tile("xg", [D], BF16)
-        xq = per_tile("xq", [256], U32)
-        xq_s = per_tile("xq_s", [256], U8)
+        xq = per_tile("xq", [256], U32, WIDE)
+        xq_s = per_tile("xq_s", [256], U8, WIDE)
+        xq_wide = per_tile("xq_wide", [512], U32, 2)
+        xq_wide_s = per_tile("xq_wide_s", [512], U8, 2)
+        planes = sbuf("planes", [2048], BF16)
         pg = per_tile("pg", [R], BF16)
         pq = per_tile("pq", [P], U32)
         pq_s = per_tile("pq_s", [P], U8)
@@ -78,28 +83,30 @@ def tile_moslorasubspacemixerrankgain_d2p_kernel(
 
         free = list(banks)
         held = {}
+        parked = {}
 
         def next_bank(key):
-            held.setdefault(key, free.pop(0))
+            if key not in held:
+                held.setdefault(key, free.pop(0))
             return held[key]
 
         def release(key):
             free.append(held[key])
 
-        def load_scales(plane, src, queue=nc.sync, rows_j=range(4)):
+        def load_scales(plane, src, queues):
             rows = src.bitcast(I32).rearrange("g (q j) n -> j q g n", j=4)
-            for j in rows_j:
+            for j, queue in queues:
                 queue.dma_start(out=plane[j:P:32].bitcast(I32), in_=rows[j])
 
         def load_x(n):
             i0, i1 = x_loads[n]
             nc.sync.dma_start(out=xb_parts[n][:], in_=x_rows[:, i0:i1, :])
 
-        def load_words(dst, src):
-            nc.sync.dma_start(out=dst.bitcast(I32), in_=src.rearrange("g p n -> p g n").bitcast(I32))
+        def load_words(dst, src, queue=nc.sync):
+            queue.dma_start(out=dst.bitcast(I32), in_=src.rearrange("g p n -> p g n").bitcast(I32))
 
-        def load_xs():
-            nc.scalar.dma_start(out=xs[:], in_=x_scale.unsqueeze(1).to_broadcast([8, 16, 8]))
+        def load_xs(queue):
+            queue.dma_start(out=xs[:], in_=x_scale.unsqueeze(1).to_broadcast([8, 16, 8]))
 
         def load_d():
             nc.gpsimd.dma_start(
@@ -114,42 +121,24 @@ def tile_moslorasubspacemixerrankgain_d2p_kernel(
             for ident in (ident32, ident16):
                 nc.vector.tensor_scalar(out=ident[:], in0=offsets[:], scalar1=0, scalar2=None, op0=ALU.is_equal)
 
-        for tile in (warm, d_rows, w0_s, bu_s, a_sraw, m_sraw):
-            zero(tile)
-        load_xs()
-        load_x(0)
-        identity()
-        load_d()
-        load_scales(bu_s, bu_scales, nc.gpsimd, range(1))
-        load_x(1)
-        load_scales(w0_s, w0_scales)
-        for h in range(2):
-            load_words(w0_w[h][:], w0_words[:, :, h * 1024 : (h + 1) * 1024])
-        load_scales(a_sraw, a_scales)
-        load_x(2)
-        load_words(a_raw[:], a_words)
-        load_scales(m_sraw, m_scales)
-        load_words(m_raw[:], m_words)
-        load_words(bu_w[:], bu_words)
-        load_scales(bu_s, bu_scales, nc.sync, range(1, 4))
+        def reorder(dst, src):
+            nc.vector.tensor_copy(
+                out=dst[:].bitcast(I32).rearrange("p g (t q w) -> p g t q w", t=4, q=16),
+                in_=src[:].bitcast(I32).rearrange("p g (q t w) -> p g t q w", t=4, q=16),
+            )
 
-        def reorder(words, raw, scales, sraw):
-            for dst, src in ((words, raw), (scales, sraw)):
-                nc.vector.tensor_copy(
-                    out=dst[:].bitcast(I32).rearrange("p g (t q w) -> p g t q w", t=4, q=16),
-                    in_=src[:].bitcast(I32).rearrange("p g (q t w) -> p g t q w", t=4, q=16),
-                )
-
-        def warm_up(count):
-            bank = next_bank(("warm", count))
+        def warm_up(count, key):
+            bank = next_bank(key)
             for n in range(count):
                 nc.tensor.matmul(bank[:], lhsT=warm[:, 0:P], rhs=warm[:], start=True, stop=True)
-            release(("warm", count))
+            release(key)
 
         def turn_d():
             bank = next_bank("d")[:].bitcast(BF16)
             nc.tensor.transpose(bank[:, 0:P], d_rows[:], ident16[:])
-            nc.scalar.copy(out=d_cols[:], in_=bank[:, 0:4])
+
+        def empty_d():
+            nc.scalar.copy(out=d_cols[:], in_=held["d"][:].bitcast(BF16)[:, 0:4])
             release("d")
 
         def widen(i, passes=(0, 1)):
@@ -178,11 +167,51 @@ def tile_moslorasubspacemixerrankgain_d2p_kernel(
             )
             release(("x", i, g0))
 
+        def x_codes(i, g):
+            if i < WIDE:
+                return xq[i][:, g * P : (g + 1) * P].bitcast(FP8X4), xq_s[i][:, g * P : (g + 1) * P]
+            cols = slice((i - WIDE) * P, (i - WIDE + 1) * P)
+            return xq_wide[g][:, cols].bitcast(FP8X4), xq_wide_s[g][:, cols]
+
         def quant_x(i, g0=0, g1=2):
-            nc.vector.quantize_mx(
-                out=xq[i][:, g0 * P : g1 * P].bitcast(FP8X4),
-                scales=xq_s[i][:, g0 * P : g1 * P],
-                in_=xg[i][:, g0 * 512 : g1 * 512],
+            if i < WIDE:
+                nc.vector.quantize_mx(
+                    out=xq[i][:, g0 * P : g1 * P].bitcast(FP8X4),
+                    scales=xq_s[i][:, g0 * P : g1 * P],
+                    in_=xg[i][:, g0 * 512 : g1 * 512],
+                )
+            else:
+                for g in range(g0, g1):
+                    codes, scales = x_codes(i, g)
+                    nc.vector.quantize_mx(out=codes, scales=scales, in_=xg[i][:, g * 512 : (g + 1) * 512])
+
+        def down_wide(t):
+            bank = next_bank(("pw", t))
+            for g in range(2):
+                nc.tensor.matmul_mx(
+                    out=bank[:],
+                    lhsT=a_w[:, g, t * 256 : (t + 1) * 256].bitcast(FP4X4),
+                    lhsT_scale=a_s[:, g, t * P : (t + 1) * P],
+                    rhs=xq_wide[g][:].bitcast(FP8X4),
+                    rhs_scale=xq_wide_s[g][:],
+                    start=(g == 0),
+                    stop=(g == 1),
+                )
+
+        def gain_wide(t):
+            nc.scalar.activation(
+                out=planes[:, t * 512 : (t + 1) * 512],
+                in_=held[("pw", t)][:],
+                func=ACT.Copy,
+                scale=d_cols[:, t : t + 1],
+            )
+            release(("pw", t))
+
+        def weave(i):
+            n0 = (i - WIDE) * P
+            nc.vector.tensor_copy(
+                out=pg[i][:].rearrange("p (c n t) -> p c t n", n=4, t=4),
+                in_=planes[:].rearrange("p (t c n) -> p c t n", t=4, n=4)[:, n0 // 4 : (n0 + P) // 4],
             )
 
         def down(i):
@@ -211,101 +240,124 @@ def tile_moslorasubspacemixerrankgain_d2p_kernel(
         def quant_p(i):
             nc.vector.quantize_mx(out=pq[i][:].bitcast(FP8X4), scales=pq_s[i][:], in_=pg[i][:])
 
-        def mix(h, b0=0, b1=4, on_vector=()):
-            for b in range(b0, b1):
-                bank = next_bank(("c", h, b))
-                f0 = h * 512 + b * P
-                for t in range(4):
-                    nc.tensor.matmul_mx(
-                        out=bank[:, t * P : (t + 1) * P],
-                        lhsT=m_w[:, 0, t * 256 : (t + 1) * 256].bitcast(FP4X4),
-                        lhsT_scale=m_s[:, 0, t * P : (t + 1) * P],
-                        rhs=bu_w[:, 0, 2 * f0 : 2 * (f0 + P)].bitcast(FP4X4),
-                        rhs_scale=bu_s[:, 0, f0 : f0 + P],
-                        start=(t == 0),
-                        stop=(t == 3),
-                    )
-                copy = nc.vector.tensor_copy if b in on_vector else nc.scalar.copy
-                copy(
-                    out=cg[h][:, b * 512 : (b + 1) * 512].rearrange("p (f t) -> p f t", t=4),
-                    in_=bank[:].rearrange("p (t f) -> p f t", t=4),
+        def mix(h, b):
+            bank = next_bank(("c", h, b))
+            f0 = h * 512 + b * P
+            for t in range(4):
+                nc.tensor.matmul_mx(
+                    out=bank[:, t * P : (t + 1) * P],
+                    lhsT=m_w[:, 0, t * 256 : (t + 1) * 256].bitcast(FP4X4),
+                    lhsT_scale=m_s[:, 0, t * P : (t + 1) * P],
+                    rhs=bu_w[h][:, 0, 2 * b * P : 2 * (b + 1) * P].bitcast(FP4X4),
+                    rhs_scale=bu_s[:, 0, f0 : f0 + P],
+                    start=(t == 0),
+                    stop=(t == 3),
                 )
-                release(("c", h, b))
+
+        def empty_c(h, b, copy=nc.scalar.copy):
+            copy(
+                out=cg[h][:, b * 512 : (b + 1) * 512].rearrange("p (f t) -> p f t", t=4),
+                in_=held[("c", h, b)][:].rearrange("p (t f) -> p f t", t=4),
+            )
+            release(("c", h, b))
 
         def quant_c(h):
             nc.vector.quantize_mx(out=cq[h][:].bitcast(FP8X4), scales=cq_s[h][:], in_=cg[h][:])
 
-        def base(i, h):
-            bank = next_bank(("b", i, h))
-            for g in range(2):
-                nc.tensor.matmul_mx(
-                    out=bank[:],
-                    lhsT=xq[i][:, g * P : (g + 1) * P].bitcast(FP8X4),
-                    lhsT_scale=xq_s[i][:, g * P : (g + 1) * P],
-                    rhs=w0_w[h][:, g, :].bitcast(FP4X4),
-                    rhs_scale=w0_s[:, g, h * 512 : (h + 1) * 512],
-                    start=(g == 0),
-                    stop=(g == 1),
-                )
-            if i < EARLY:
-                nc.scalar.copy(out=res[h][i][:], in_=bank[:])
-                release(("b", i, h))
+        def base(i, h, c0=0, c1=512):
+            bank = next_bank(("b", i, h, c0))
+            width = 512 if c1 - c0 == 512 else P
+            for n0 in range(c0, c1, width):
+                for g in range(2):
+                    nc.tensor.matmul_mx(
+                        out=bank[:, n0 : n0 + width],
+                        lhsT=x_codes(i, g)[0],
+                        lhsT_scale=x_codes(i, g)[1],
+                        rhs=w0_w[h][:, g, 2 * n0 : 2 * (n0 + width)].bitcast(FP4X4),
+                        rhs_scale=w0_s[:, g, h * 512 + n0 : h * 512 + n0 + width],
+                        start=(g == 0),
+                        stop=(g == 1),
+                    )
 
-        def up(i, h):
-            bank = next_bank(("t", i, h))
+        def up(i, h, c0=0, c1=512):
             nc.tensor.matmul_mx(
-                out=bank[:],
+                out=next_bank(("t", i, h, c0))[:, c0:c1],
                 lhsT=pq[i][:].bitcast(FP8X4),
                 lhsT_scale=pq_s[i][:],
-                rhs=cq[h][:].bitcast(FP8X4),
-                rhs_scale=cq_s[h][:],
+                rhs=cq[h][:, c0:c1].bitcast(FP8X4),
+                rhs_scale=cq_s[h][:, c0:c1],
                 start=True,
                 stop=True,
             )
-            if i >= EARLY:
-                nc.scalar.copy(out=res[h][i][:], in_=bank[:])
-                release(("t", i, h))
 
-        def finish(i, h):
-            width = 256 if (i, h) == (TILES - 1, 1) else 512
-            for c0 in range(0, 512, width):
-                cols = slice(c0, c0 + width)
-                acc = res[h][i][:, cols]
-                if i < EARLY:
-                    t_part, base_part = held[("t", i, h)][:, cols], acc
-                else:
-                    t_part, base_part = acc, held[("b", i, h)][:, cols]
-                nc.vector.scalar_tensor_tensor(
-                    out=acc, in0=t_part, scalar=ALPHA, in1=base_part, op0=ALU.mult, op1=ALU.add
-                )
-                nc.sync.dma_start(out=out_rows[:, i, h * 512 + c0 : h * 512 + c0 + width], in_=acc)
-            release(("t" if i < EARLY else "b", i, h))
+        def park(kind, i, h, c0=0, c1=512):
+            nc.scalar.copy(out=res[h][i][:, c0:c1], in_=held[(kind, i, h, c0)][:, c0:c1])
+            release((kind, i, h, c0))
+            parked.setdefault((i, h), kind)
 
-        warm_up(4)
-        for i in range(EARLY):
+        def finish(i, h, c0=0, c1=512, queue=nc.sync, own_bank=False):
+            cols = slice(c0, c1)
+            acc = res[h][i][:, cols]
+            key = ("t" if parked[(i, h)] == "b" else "b", i, h, c0 if own_bank else 0)
+            if key[0] == "t":
+                t_part, base_part = held[key][:, cols], acc
+            else:
+                t_part, base_part = acc, held[key][:, cols]
+            nc.vector.scalar_tensor_tensor(out=acc, in0=t_part, scalar=ALPHA, in1=base_part, op0=ALU.mult, op1=ALU.add)
+            queue.dma_start(out=out_rows[:, i, h * 512 + c0 : h * 512 + c1], in_=acc)
+            if own_bank or c1 == 512:
+                release(key)
+
+        sp, act, pool = nc.sync, nc.scalar, nc.gpsimd
+        for tile in (warm, d_rows, w0_s, bu_s, a_sraw, m_sraw):
+            zero(tile)
+        load_xs(act)
+        load_x(0)
+        identity()
+        load_d()
+        load_scales(bu_s, bu_scales, [(0, pool)])
+        load_x(1)
+        load_scales(w0_s, w0_scales, [(j, sp) for j in range(4)])
+        for h in range(2):
+            load_words(w0_w[h][:], w0_words[:, :, h * 1024 : (h + 1) * 1024])
+        load_scales(a_sraw, a_scales, [(j, sp) for j in range(4)])
+        load_x(2)
+        load_words(a_raw[:], a_words)
+        load_scales(m_sraw, m_scales, [(j, sp) for j in range(4)])
+        load_words(m_raw[:], m_words)
+        load_words(bu_all[:], bu_words)
+        load_scales(bu_s, bu_scales, [(j, sp) for j in range(1, 4)])
+
+        warm_up(4, "warm0")
+        for i in range(2):
             for g in range(2):
                 widen(i, (g,))
                 turn_x(i, g, g + 1)
                 empty_x(i, g, g + 1)
             if i == 0:
-                warm_up(2)
+                warm_up(2, "warm1")
         quant_x(0, 0, 1)
         quant_x(0, 1, 2)
         for g in range(2):
             widen(2, (g,))
             quant_x(1, g, g + 1)
-        base(0, 0)
-        base(0, 1)
+        for h in range(2):
+            base(0, h)
+            park("b", 0, h)
         widen(3)
         widen(4)
-        reorder(a_w, a_raw, a_s, a_sraw)
-        base(1, 0)
-        base(1, 1)
+        reorder(a_w, a_raw)
+        reorder(a_s, a_sraw)
+        for h in range(2):
+            base(1, h)
+            park("b", 1, h)
         for i in range(2, 5):
             turn_x(i)
         turn_d()
+        empty_d()
         widen(5)
-        reorder(m_w, m_raw, m_s, m_sraw)
+        reorder(m_w, m_raw)
+        reorder(m_s, m_sraw)
         for i in range(2, 5):
             empty_x(i)
         widen(6)
@@ -315,54 +367,96 @@ def tile_moslorasubspacemixerrankgain_d2p_kernel(
         quant_x(2)
         gain(1)
         quant_x(3)
-        mix(0, 0, 4)
+        for b in range(4):
+            mix(0, b)
+            empty_c(0, b)
         quant_p(0)
         down(2)
         quant_p(1)
-        mix(1, 0, 2)
+        for b in range(2):
+            mix(1, b)
+            empty_c(1, b)
         gain(2)
         widen(7)
         down(3)
-        mix(1, 2, 4)
+        for b in range(2, 4):
+            mix(1, b)
+            empty_c(1, b)
         quant_c(0)
         gain(3)
         quant_p(2)
-        up(0, 0)
         for i in range(5, 8):
             turn_x(i)
         for i in range(5, 8):
             empty_x(i)
+        up(0, 0)
         up(1, 0)
         quant_x(4)
         quant_p(3)
-        finish(0, 0)
         quant_c(1)
-        finish(1, 0)
+        finish(0, 0)
         quant_x(5)
-        for i in range(EARLY, TILES):
-            ahead = i + 2
-            if ahead < TILES:
-                down(ahead)
+        finish(1, 0)
+        up(2, 0)
+        park("t", 2, 0)
+        base(2, 0)
+        up(0, 1)
+        up(1, 1)
+        quant_x(6)
+        quant_x(7)
+        up(2, 1)
+        park("t", 2, 1)
+        base(2, 1)
+        finish(0, 1)
+        finish(1, 1)
+        for t in range(2):
+            down_wide(t)
+            gain_wide(t)
+        finish(2, 0)
+        up(3, 0)
+        park("t", 3, 0)
+        for t in range(2, 4):
+            down_wide(t)
+            gain_wide(t)
+        finish(2, 1)
+        base(3, 0)
+        up(3, 1)
+        park("t", 3, 1)
+        base(3, 1)
+        finish(3, 0)
+        base(4, 0)
+        park("b", 4, 0)
+        weave(4)
+        weave(5)
+        quant_p(4)
+        quant_p(5)
+        finish(3, 1)
+        base(4, 1)
+        park("b", 4, 1)
+        up(4, 0)
+        up(4, 1)
+        weave(6)
+        finish(4, 0)
+        quant_p(6)
+        for i in range(5, TILES):
+            last = i == TILES - 1
             up(i, 0)
-            if i == EARLY:
-                up(0, 1)
-            if i == TILES - 1:
+            park("t", i, 0)
+            if last:
                 up(i, 1)
+                park("t", i, 1)
             base(i, 0)
-            if i == EARLY:
-                up(1, 1)
-            if i < TILES - 1:
+            if i == 5:
+                weave(7)
+                finish(4, 1)
+                quant_p(7)
+            if not last:
                 up(i, 1)
+                park("t", i, 1)
             base(i, 1)
-            if ahead < TILES:
-                gain(ahead)
-            if i == EARLY:
-                finish(0, 1)
-                quant_p(ahead)
-                finish(1, 1)
-            if i + 4 < TILES:
-                quant_x(i + 4)
             finish(i, 0)
-            if EARLY < i < TILES - 2:
-                quant_p(ahead)
-            finish(i, 1)
+            if last:
+                finish(i, 1, 0, 256)
+                finish(i, 1, 256, 512)
+            else:
+                finish(i, 1)

@@ -321,8 +321,8 @@ def tile_moslorasubspacemixerrankgain_d2p_kernel(
         for h in range(2):
             load_words(w0_w[h][:], w0_words[:, :, h * 1024 : (h + 1) * 1024])
         load_scales(a_sraw, a_scales, [(j, sp) for j in range(4)])
-        load_x(2)
         load_words(a_raw[:], a_words)
+        load_x(2)
         load_scales(m_sraw, m_scales, [(j, sp) for j in range(4)])
         load_words(m_raw[:], m_words)
         load_words(bu_all[:], bu_words)
@@ -345,100 +345,104 @@ def tile_moslorasubspacemixerrankgain_d2p_kernel(
             base(0, h)
             park("b", 0, h)
         widen(3)
-        widen(4)
         reorder(a_w, a_raw)
         reorder(a_s, a_sraw)
         for h in range(2):
             base(1, h)
             park("b", 1, h)
-        for i in range(2, 5):
+        for i in range(2, 4):
             turn_x(i)
         turn_d()
-        empty_d()
-        widen(5)
-        reorder(m_w, m_raw)
-        reorder(m_s, m_sraw)
-        for i in range(2, 5):
+        for i in range(2, 4):
             empty_x(i)
-        widen(6)
+        empty_d()
+        widen(4)
         down(0)
         down(1)
-        gain(0)
         quant_x(2)
-        gain(1)
+        reorder(m_w, m_raw)
+        reorder(m_s, m_sraw)
         quant_x(3)
+        gain(0)
+        down(2)
+        down(3)
+        gain(1)
+        widen(5)
+        gain(2)
+        gain(3)
         for b in range(4):
             mix(0, b)
             empty_c(0, b)
+        widen(6)
+        for i in range(4, 6):
+            turn_x(i)
+            empty_x(i)
         quant_p(0)
-        down(2)
         quant_p(1)
-        for b in range(2):
-            mix(1, b)
-            empty_c(1, b)
-        gain(2)
         widen(7)
-        down(3)
-        for b in range(2, 4):
+        for b in range(4):
             mix(1, b)
             empty_c(1, b)
         quant_c(0)
-        gain(3)
         quant_p(2)
-        for i in range(5, 8):
+        quant_p(3)
+        quant_x(4)
+        quant_x(5)
+        for i in range(6, 8):
             turn_x(i)
-        for i in range(5, 8):
             empty_x(i)
+        base(2, 0)
         up(0, 0)
         up(1, 0)
-        quant_x(4)
-        quant_p(3)
-        quant_c(1)
         finish(0, 0)
-        quant_x(5)
-        finish(1, 0)
+        base(2, 1)
         up(2, 0)
         park("t", 2, 0)
-        base(2, 0)
-        up(0, 1)
-        up(1, 1)
-        quant_x(6)
-        quant_x(7)
-        up(2, 1)
-        park("t", 2, 1)
-        base(2, 1)
-        finish(0, 1)
-        finish(1, 1)
-        for t in range(2):
-            down_wide(t)
-            gain_wide(t)
-        finish(2, 0)
+        quant_c(1)
+        finish(1, 0)
         up(3, 0)
         park("t", 3, 0)
-        for t in range(2, 4):
+        quant_x(6)
+        quant_x(7)
+        base(3, 0)
+        finish(2, 0)
+        for i in range(3):
+            up(i, 1)
+        park("t", 2, 1)
+        finish(3, 0)
+        for t in range(4):
             down_wide(t)
             gain_wide(t)
-        finish(2, 1)
-        base(3, 0)
+            if t < 3:
+                finish(t, 1)
         up(3, 1)
         park("t", 3, 1)
         base(3, 1)
-        finish(3, 0)
-        base(4, 0)
-        park("b", 4, 0)
         weave(4)
         weave(5)
         quant_p(4)
         quant_p(5)
+        for h in range(2):
+            base(4, h)
+            park("b", 4, h)
+        base(5, 0)
         finish(3, 1)
-        base(4, 1)
-        park("b", 4, 1)
-        up(4, 0)
-        up(4, 1)
         weave(6)
-        finish(4, 0)
+        weave(7)
+        up(4, 0)
+        up(5, 0)
+        park("t", 5, 0)
         quant_p(6)
-        for i in range(5, TILES):
+        finish(4, 0)
+        up(4, 1)
+        up(5, 1)
+        park("t", 5, 1)
+        base(5, 1)
+        quant_p(7)
+        finish(4, 1)
+        finish(5, 0)
+        finish(5, 1)
+        for i in range(6, TILES):
             last = i == TILES - 1
             up(i, 0)
             park("t", i, 0)
@@ -446,10 +450,6 @@ def tile_moslorasubspacemixerrankgain_d2p_kernel(
                 up(i, 1)
                 park("t", i, 1)
             base(i, 0)
-            if i == 5:
-                weave(7)
-                finish(4, 1)
-                quant_p(7)
             if not last:
                 up(i, 1)
                 park("t", i, 1)

@@ -46,7 +46,7 @@ def tile_moslorasubspacemixerrankgain_d2p_kernel(
         d_cols = sbuf("d_cols", [4], F32)
         warm = sbuf("warm", [512], BF16)
         xs = sbuf("xs", [8], F32)
-        x_loads = [(0, 1), (1, 4), (4, 8)]
+        x_loads = [(0, 1), (1, 4), (4, 6), (6, 8)]
         xb_parts = [sbuf("xb%d" % i0, [i1 - i0, D], U8) for i0, i1 in x_loads]
         xb = [part[:, i - i0, :] for part, (i0, i1) in zip(xb_parts, x_loads) for i in range(i0, i1)]
         a_raw = sbuf("a_raw", [2, 1024], U8)
@@ -198,13 +198,12 @@ def tile_moslorasubspacemixerrankgain_d2p_kernel(
                     stop=(g == 1),
                 )
 
-        def gain_wide(t):
-            nc.scalar.activation(
-                out=planes[:, t * 512 : (t + 1) * 512],
-                in_=held[("pw", t)][:],
-                func=ACT.Copy,
-                scale=d_cols[:, t : t + 1],
-            )
+        def gain_wide(t, on_vector=False):
+            plane, bank, gains = planes[:, t * 512 : (t + 1) * 512], held[("pw", t)][:], d_cols[:, t : t + 1]
+            if on_vector:
+                nc.vector.tensor_scalar(out=plane, in0=bank, scalar1=gains, scalar2=None, op0=ALU.mult)
+            else:
+                nc.scalar.activation(out=plane, in_=bank, func=ACT.Copy, scale=gains)
             release(("pw", t))
 
         def weave(i):
@@ -318,8 +317,8 @@ def tile_moslorasubspacemixerrankgain_d2p_kernel(
         load_scales(bu_s, bu_scales, [(0, pool)])
         load_x(1)
         load_scales(w0_s, w0_scales, [(j, sp) for j in range(4)])
-        for h in range(2):
-            load_words(w0_w[h][:], w0_words[:, :, h * 1024 : (h + 1) * 1024])
+        load_words(w0_w[0][:], w0_words[:, :, 0:1024])
+        load_words(w0_w[1][:], w0_words[:, :, 1024:2048])
         load_scales(a_sraw, a_scales, [(j, sp) for j in range(4)])
         load_words(a_raw[:], a_words)
         load_x(2)
@@ -327,6 +326,7 @@ def tile_moslorasubspacemixerrankgain_d2p_kernel(
         load_words(m_raw[:], m_words)
         load_words(bu_all[:], bu_words)
         load_scales(bu_s, bu_scales, [(j, sp) for j in range(1, 4)])
+        load_x(3)
 
         warm_up(4, "warm0")
         for i in range(2):
@@ -357,6 +357,7 @@ def tile_moslorasubspacemixerrankgain_d2p_kernel(
             empty_x(i)
         empty_d()
         widen(4)
+        widen(5, (0,))
         down(0)
         down(1)
         quant_x(2)
@@ -365,40 +366,37 @@ def tile_moslorasubspacemixerrankgain_d2p_kernel(
         quant_x(3)
         gain(0)
         down(2)
-        down(3)
         gain(1)
-        widen(5)
-        gain(2)
-        gain(3)
         for b in range(4):
             mix(0, b)
             empty_c(0, b)
+        widen(5, (1,))
+        down(3)
+        gain(2)
         widen(6)
-        for i in range(4, 6):
-            turn_x(i)
-            empty_x(i)
-        quant_p(0)
-        quant_p(1)
-        widen(7)
         for b in range(4):
             mix(1, b)
             empty_c(1, b)
+        gain(3)
+        widen(7)
+        quant_p(0)
+        quant_p(1)
         quant_c(0)
         quant_p(2)
         quant_p(3)
-        quant_x(4)
-        quant_x(5)
-        for i in range(6, 8):
+        for i in range(4, 8):
             turn_x(i)
             empty_x(i)
         base(2, 0)
         up(0, 0)
         up(1, 0)
+        quant_c(1)
         finish(0, 0)
         base(2, 1)
         up(2, 0)
         park("t", 2, 0)
-        quant_c(1)
+        quant_x(4)
+        quant_x(5)
         finish(1, 0)
         up(3, 0)
         park("t", 3, 0)
@@ -412,7 +410,7 @@ def tile_moslorasubspacemixerrankgain_d2p_kernel(
         finish(3, 0)
         for t in range(4):
             down_wide(t)
-            gain_wide(t)
+            gain_wide(t, t == 3)
             if t < 3:
                 finish(t, 1)
         up(3, 1)
@@ -428,19 +426,19 @@ def tile_moslorasubspacemixerrankgain_d2p_kernel(
         base(5, 0)
         finish(3, 1)
         weave(6)
-        weave(7)
         up(4, 0)
         up(5, 0)
         park("t", 5, 0)
-        quant_p(6)
         finish(4, 0)
+        quant_p(6)
         up(4, 1)
         up(5, 1)
         park("t", 5, 1)
         base(5, 1)
-        quant_p(7)
         finish(4, 1)
+        weave(7)
         finish(5, 0)
+        quant_p(7)
         finish(5, 1)
         for i in range(6, TILES):
             last = i == TILES - 1

@@ -21,6 +21,7 @@ P = 128
 TILES = N // P
 BANKS = 8
 WIDE = 4
+PLAIN = ((0, 1), (5, 0), (5, 1))
 ALPHA = 1.0 / math.sqrt(R)
 
 
@@ -118,8 +119,8 @@ def tile_moslorasubspacemixerrankgain_d2p_kernel(
 
         def identity():
             nc.gpsimd.iota(offsets[:], pattern=[[1, P]], base=0, channel_multiplier=-1)
-            for ident in (ident32, ident16):
-                nc.vector.tensor_scalar(out=ident[:], in0=offsets[:], scalar1=0, scalar2=None, op0=ALU.is_equal)
+            nc.vector.tensor_scalar(out=ident32[:], in0=offsets[:], scalar1=0, scalar2=None, op0=ALU.is_equal)
+            nc.scalar.copy(out=ident16[:], in_=ident32[:])
 
         def reorder(dst, src):
             nc.vector.tensor_copy(
@@ -154,11 +155,26 @@ def tile_moslorasubspacemixerrankgain_d2p_kernel(
                         op0=ALU.mult,
                     )
 
+        def widen_plain(i, g):
+            for j in range(4 * g, 4 * g + 4):
+                nc.scalar.activation(
+                    out=xw[i][:, j * P : (j + 1) * P],
+                    in_=xb[i][:, j * P : (j + 1) * P].bitcast(FP8),
+                    func=ACT.Copy,
+                    scale=xs[:, j : j + 1],
+                )
+
         def turn_x(i, g0=0, g1=2):
             bank = next_bank(("x", i, g0))
             words = xw[i][:].bitcast(F32)
-            for n in range(2 * g0, 2 * g1):
-                nc.tensor.transpose(bank[:, n * P : (n + 1) * P], words[:, n * P : (n + 1) * P], ident32[:])
+            for g in range(g0, g1):
+                for u in range(2):
+                    n = 2 * g + u
+                    if (i, g) in PLAIN:
+                        src = words[:, 256 * g + u : 256 * (g + 1) : 2]
+                    else:
+                        src = words[:, n * P : (n + 1) * P]
+                    nc.tensor.transpose(bank[:, n * P : (n + 1) * P], src, ident32[:])
 
         def empty_x(i, g0=0, g1=2):
             nc.scalar.copy(
@@ -329,9 +345,11 @@ def tile_moslorasubspacemixerrankgain_d2p_kernel(
         load_x(3)
 
         warm_up(4, "warm0")
+        widen_plain(0, 1)
         for i in range(2):
             for g in range(2):
-                widen(i, (g,))
+                if (i, g) not in PLAIN:
+                    widen(i, (g,))
                 turn_x(i, g, g + 1)
                 empty_x(i, g, g + 1)
             if i == 0:
@@ -357,7 +375,8 @@ def tile_moslorasubspacemixerrankgain_d2p_kernel(
             empty_x(i)
         empty_d()
         widen(4)
-        widen(5, (0,))
+        widen_plain(5, 0)
+        widen_plain(5, 1)
         down(0)
         down(1)
         quant_x(2)
@@ -370,7 +389,6 @@ def tile_moslorasubspacemixerrankgain_d2p_kernel(
         for b in range(4):
             mix(0, b)
             empty_c(0, b)
-        widen(5, (1,))
         down(3)
         gain(2)
         widen(6)

@@ -64,15 +64,19 @@ def tile_moslorasubspacemixerrankgain_d2p_kernel(
         bu_w = [bu_all[:, :, h * 1024 : (h + 1) * 1024] for h in range(2)]
         bu_s = sbuf("bu_s", [1, 1024], U8)
         xw = per_tile("xw", [D], BF16)
-        xg = per_tile("xg", [D], BF16)
+        xg = per_tile("xg", [D], BF16, WIDE)
+        xg_pairs = per_tile("xg_pair", [2 * D], BF16, 2)
         xq = per_tile("xq", [256], U32, WIDE)
         xq_s = per_tile("xq_s", [256], U8, WIDE)
         xq_wide = per_tile("xq_wide", [512], U32, 2)
         xq_wide_s = per_tile("xq_wide_s", [512], U8, 2)
         planes = sbuf("planes", [2048], BF16)
-        pg = per_tile("pg", [R], BF16)
-        pq = per_tile("pq", [P], U32)
-        pq_s = per_tile("pq_s", [P], U8)
+        pg_pairs = per_tile("pg", [2 * R], BF16, TILES // 2)
+        pq_pairs = per_tile("pq", [2 * P], U32, TILES // 2)
+        pq_s_pairs = per_tile("pq_s", [2 * P], U8, TILES // 2)
+        pg = [pg_pairs[i // 2][:, i % 2 * R : (i % 2 + 1) * R] for i in range(TILES)]
+        pq = [pq_pairs[i // 2][:, i % 2 * P : (i % 2 + 1) * P] for i in range(TILES)]
+        pq_s = [pq_s_pairs[i // 2][:, i % 2 * P : (i % 2 + 1) * P] for i in range(TILES)]
         cg = per_tile("cg", [2048], BF16, 2)
         cq = per_tile("cq", [512], U32, 2)
         cq_s = per_tile("cq_s", [512], U8, 2)
@@ -177,8 +181,13 @@ def tile_moslorasubspacemixerrankgain_d2p_kernel(
                     nc.tensor.transpose(bank[:, n * P : (n + 1) * P], src, ident32[:])
 
         def empty_x(i, g0=0, g1=2):
+            if i < WIDE:
+                dst = xg[i][:, g0 * 512 : g1 * 512].bitcast(F32).rearrange("p (g r u) -> p g r u", r=P, u=2)
+            else:
+                pair = xg_pairs[(i - WIDE) // 2][:].bitcast(F32)
+                dst = pair.rearrange("p (g i r u) -> p i g r u", g=2, i=2, u=2)[:, i % 2]
             nc.scalar.copy(
-                out=xg[i][:, g0 * 512 : g1 * 512].bitcast(F32).rearrange("p (g r u) -> p g r u", r=P, u=2),
+                out=dst,
                 in_=held[("x", i, g0)][:, g0 * 256 : g1 * 256].rearrange("p (g u r) -> p g r u", u=2, r=P),
             )
             release(("x", i, g0))
@@ -197,9 +206,13 @@ def tile_moslorasubspacemixerrankgain_d2p_kernel(
                     in_=xg[i][:, g0 * 512 : g1 * 512],
                 )
             else:
+                cols = slice((i - WIDE) * P, (i - WIDE + 2) * P)
                 for g in range(g0, g1):
-                    codes, scales = x_codes(i, g)
-                    nc.vector.quantize_mx(out=codes, scales=scales, in_=xg[i][:, g * 512 : (g + 1) * 512])
+                    nc.vector.quantize_mx(
+                        out=xq_wide[g][:, cols].bitcast(FP8X4),
+                        scales=xq_wide_s[g][:, cols],
+                        in_=xg_pairs[(i - WIDE) // 2][:, g * D : (g + 1) * D],
+                    )
 
         def down_wide(t):
             bank = next_bank(("pw", t))
@@ -254,6 +267,11 @@ def tile_moslorasubspacemixerrankgain_d2p_kernel(
 
         def quant_p(i):
             nc.vector.quantize_mx(out=pq[i][:].bitcast(FP8X4), scales=pq_s[i][:], in_=pg[i][:])
+
+        def quant_p_pair(i):
+            nc.vector.quantize_mx(
+                out=pq_pairs[i // 2][:].bitcast(FP8X4), scales=pq_s_pairs[i // 2][:], in_=pg_pairs[i // 2][:]
+            )
 
         def mix(h, b):
             bank = next_bank(("c", h, b))
@@ -365,15 +383,16 @@ def tile_moslorasubspacemixerrankgain_d2p_kernel(
         widen(3)
         reorder(a_w, a_raw)
         reorder(a_s, a_sraw)
-        for h in range(2):
-            base(1, h)
-            park("b", 1, h)
-        for i in range(2, 4):
-            turn_x(i)
+        base(1, 0)
+        park("b", 1, 0)
+        turn_x(2)
+        empty_x(2)
+        turn_x(3)
         turn_d()
-        for i in range(2, 4):
-            empty_x(i)
+        base(1, 1)
+        empty_x(3)
         empty_d()
+        park("b", 1, 1)
         widen(4)
         widen_plain(5, 0)
         widen_plain(5, 1)
@@ -397,11 +416,9 @@ def tile_moslorasubspacemixerrankgain_d2p_kernel(
             empty_c(1, b)
         gain(3)
         widen(7)
-        quant_p(0)
-        quant_p(1)
+        quant_p_pair(0)
         quant_c(0)
-        quant_p(2)
-        quant_p(3)
+        quant_p_pair(2)
         for i in range(4, 8):
             turn_x(i)
             empty_x(i)
@@ -414,12 +431,10 @@ def tile_moslorasubspacemixerrankgain_d2p_kernel(
         up(2, 0)
         park("t", 2, 0)
         quant_x(4)
-        quant_x(5)
         finish(1, 0)
         up(3, 0)
         park("t", 3, 0)
         quant_x(6)
-        quant_x(7)
         base(3, 0)
         finish(2, 0)
         for i in range(3):
@@ -428,12 +443,13 @@ def tile_moslorasubspacemixerrankgain_d2p_kernel(
         finish(3, 0)
         for t in range(4):
             down_wide(t)
-            gain_wide(t, t == 3)
-            if t < 3:
+            gain_wide(t, t == 2)
+            if t < 2:
                 finish(t, 1)
         up(3, 1)
         park("t", 3, 1)
         base(3, 1)
+        finish(2, 1)
         weave(4)
         weave(5)
         quant_p(4)
@@ -442,21 +458,21 @@ def tile_moslorasubspacemixerrankgain_d2p_kernel(
             base(4, h)
             park("b", 4, h)
         base(5, 0)
-        finish(3, 1)
         weave(6)
+        finish(3, 1)
+        quant_p(6)
         up(4, 0)
         up(5, 0)
         park("t", 5, 0)
         finish(4, 0)
-        quant_p(6)
         up(4, 1)
         up(5, 1)
         park("t", 5, 1)
         base(5, 1)
-        finish(4, 1)
         weave(7)
-        finish(5, 0)
+        finish(4, 1)
         quant_p(7)
+        finish(5, 0)
         finish(5, 1)
         for i in range(6, TILES):
             last = i == TILES - 1

@@ -348,7 +348,6 @@ def tile_moslorasubspacemixerrankgain_d2p_kernel(
         load_x(0)
         identity()
         load_d()
-        load_scales(bu_s, bu_scales, [(0, pool)])
         load_x(1)
         load_scales(w0_s, w0_scales, [(j, sp) for j in range(4)])
         load_words(w0_w[0][:], w0_words[:, :, 0:1024])
@@ -359,7 +358,7 @@ def tile_moslorasubspacemixerrankgain_d2p_kernel(
         load_scales(m_sraw, m_scales, [(j, sp) for j in range(4)])
         load_words(m_raw[:], m_words)
         load_words(bu_all[:], bu_words)
-        load_scales(bu_s, bu_scales, [(j, sp) for j in range(1, 4)])
+        load_scales(bu_s, bu_scales, [(j, sp) for j in range(4)])
         load_x(3)
 
         warm_up(4, "warm0")
@@ -414,16 +413,16 @@ def tile_moslorasubspacemixerrankgain_d2p_kernel(
         for b in range(4):
             mix(1, b)
             empty_c(1, b)
-        gain(3)
         widen(7)
+        gain(3)
         quant_p_pair(0)
         quant_c(0)
         quant_p_pair(2)
         for i in range(4, 8):
             turn_x(i)
             empty_x(i)
-        base(2, 0)
         up(0, 0)
+        base(2, 0)
         up(1, 0)
         quant_c(1)
         finish(0, 0)
@@ -453,19 +452,19 @@ def tile_moslorasubspacemixerrankgain_d2p_kernel(
         weave(4)
         weave(5)
         quant_p(4)
+        finish(3, 1)
         quant_p(5)
         for h in range(2):
             base(4, h)
             park("b", 4, h)
         base(5, 0)
         weave(6)
-        finish(3, 1)
-        quant_p(6)
         up(4, 0)
+        up(4, 1)
         up(5, 0)
         park("t", 5, 0)
         finish(4, 0)
-        up(4, 1)
+        quant_p(6)
         up(5, 1)
         park("t", 5, 1)
         base(5, 1)

@@ -20,8 +20,8 @@ ACT = mybir.ActivationFunctionType
 P = 128
 TILES = N // P
 BANKS = 8
-WIDE = 4
-PLAIN = ((0, 1), (5, 0), (5, 1))
+GROUP = 4
+PLAIN = ((0, 1),)
 ALPHA = 1.0 / math.sqrt(R)
 
 
@@ -37,7 +37,7 @@ def tile_moslorasubspacemixerrankgain_d2p_kernel(
         def sbuf(name, shape, dtype):
             return keep.tile([P] + shape, dtype, align_bytes=64, name=name)
 
-        def per_tile(name, shape, dtype, count=TILES):
+        def several(name, shape, dtype, count):
             return [sbuf("%s%d" % (name, i), shape, dtype) for i in range(count)]
 
         ident32 = sbuf("ident32", [P], F32)
@@ -58,29 +58,23 @@ def tile_moslorasubspacemixerrankgain_d2p_kernel(
         m_w = sbuf("m_w", [1, 1024], U8)
         m_sraw = sbuf("m_sraw", [1, 512], U8)
         m_s = sbuf("m_s", [1, 512], U8)
-        w0_w = per_tile("w0_w", [2, 1024], U8, 2)
+        w0_w = several("w0_w", [2, 1024], U8, 2)
         w0_s = sbuf("w0_s", [2, 1024], U8)
-        bu_all = sbuf("bu_all", [1, 2048], U8)
-        bu_w = [bu_all[:, :, h * 1024 : (h + 1) * 1024] for h in range(2)]
+        bu_w = sbuf("bu_w", [1, 2048], U8)
         bu_s = sbuf("bu_s", [1, 1024], U8)
-        xw = per_tile("xw", [D], BF16)
-        xg = per_tile("xg", [D], BF16, WIDE)
-        xg_pairs = per_tile("xg_pair", [2 * D], BF16, 2)
-        xq = per_tile("xq", [256], U32, WIDE)
-        xq_s = per_tile("xq_s", [256], U8, WIDE)
-        xq_wide = per_tile("xq_wide", [512], U32, 2)
-        xq_wide_s = per_tile("xq_wide_s", [512], U8, 2)
-        planes = sbuf("planes", [2048], BF16)
-        pg_pairs = per_tile("pg", [2 * R], BF16, TILES // 2)
-        pq_pairs = per_tile("pq", [2 * P], U32, TILES // 2)
-        pq_s_pairs = per_tile("pq_s", [2 * P], U8, TILES // 2)
-        pg = [pg_pairs[i // 2][:, i % 2 * R : (i % 2 + 1) * R] for i in range(TILES)]
-        pq = [pq_pairs[i // 2][:, i % 2 * P : (i % 2 + 1) * P] for i in range(TILES)]
-        pq_s = [pq_s_pairs[i // 2][:, i % 2 * P : (i % 2 + 1) * P] for i in range(TILES)]
-        cg = per_tile("cg", [2048], BF16, 2)
-        cq = per_tile("cq", [512], U32, 2)
-        cq_s = per_tile("cq_s", [512], U8, 2)
-        res = [per_tile("res%d_" % h, [512], F32) for h in range(2)]
+        xw = several("xw", [D], BF16, TILES)
+        xg = several("xg", [D], BF16, GROUP)
+        xg_pairs = several("xg_pair", [2 * D], BF16, 2)
+        xq = [several("xq%d_" % k, [512], U32, 2) for k in range(2)]
+        xq_s = [several("xq_s%d_" % k, [512], U8, 2) for k in range(2)]
+        planes = several("planes", [2048], BF16, 2)
+        pg = several("pg", [2 * R], BF16, TILES // 2)
+        pq = several("pq", [2 * P], U32, TILES // 2)
+        pq_s = several("pq_s", [2 * P], U8, TILES // 2)
+        cg = several("cg", [2048], BF16, 2)
+        cq = several("cq", [512], U32, 2)
+        cq_s = several("cq_s", [512], U8, 2)
+        res = [several("res%d_" % h, [512], F32, TILES) for h in range(2)]
         banks = [psum.tile([P, 512], F32, name="bank%d" % b) for b in range(BANKS)]
 
         x_rows = x_bytes.rearrange("(p i) k -> p i k", i=TILES)
@@ -90,7 +84,7 @@ def tile_moslorasubspacemixerrankgain_d2p_kernel(
         held = {}
         parked = {}
 
-        def next_bank(key):
+        def take(key):
             if key not in held:
                 held.setdefault(key, free.pop(0))
             return held[key]
@@ -98,23 +92,23 @@ def tile_moslorasubspacemixerrankgain_d2p_kernel(
         def release(key):
             free.append(held[key])
 
-        def load_scales(plane, src, queues):
+        def load_scales(plane, src, which=range(4), queue=nc.sync):
             rows = src.bitcast(I32).rearrange("g (q j) n -> j q g n", j=4)
-            for j, queue in queues:
+            for j in which:
                 queue.dma_start(out=plane[j:P:32].bitcast(I32), in_=rows[j])
 
         def load_x(n):
             i0, i1 = x_loads[n]
             nc.sync.dma_start(out=xb_parts[n][:], in_=x_rows[:, i0:i1, :])
 
-        def load_words(dst, src, queue=nc.sync):
-            queue.dma_start(out=dst.bitcast(I32), in_=src.rearrange("g p n -> p g n").bitcast(I32))
+        def load_words(dst, src):
+            nc.sync.dma_start(out=dst.bitcast(I32), in_=src.rearrange("g p n -> p g n").bitcast(I32))
 
-        def load_xs(queue):
-            queue.dma_start(out=xs[:], in_=x_scale.unsqueeze(1).to_broadcast([8, 16, 8]))
+        def load_xs():
+            nc.scalar.dma_start(out=xs[:], in_=x_scale.unsqueeze(1).to_broadcast([8, 16, 8]))
 
         def load_d():
-            nc.gpsimd.dma_start(
+            nc.sync.dma_start(
                 out=d_rows[0:4, :].rearrange("t (q e) -> t q e", e=8), in_=d.rearrange("(q t e) -> t q e", t=4, e=8)
             )
 
@@ -133,21 +127,20 @@ def tile_moslorasubspacemixerrankgain_d2p_kernel(
             )
 
         def warm_up(count, key):
-            bank = next_bank(key)
+            bank = take(key)
             for n in range(count):
                 nc.tensor.matmul(bank[:], lhsT=warm[:, 0:P], rhs=warm[:], start=True, stop=True)
             release(key)
 
         def turn_d():
-            bank = next_bank("d")[:].bitcast(BF16)
-            nc.tensor.transpose(bank[:, 0:P], d_rows[:], ident16[:])
+            nc.tensor.matmul(take("d")[:, 0:4], lhsT=d_rows[:], rhs=ident16[:, 0:4], start=True, stop=True)
 
         def empty_d():
-            nc.scalar.copy(out=d_cols[:], in_=held["d"][:].bitcast(BF16)[:, 0:4])
+            nc.scalar.copy(out=d_cols[:], in_=held["d"][:, 0:4])
             release("d")
 
-        def widen(i, passes=(0, 1)):
-            for g in passes:
+        def widen(i, g0=0, g1=2):
+            for g in range(g0, g1):
                 dst = xw[i][:, g * 512 : (g + 1) * 512].rearrange("p (u q e) -> p q u e", u=2, e=2)
                 for b in range(4):
                     j = 4 * g + b
@@ -159,8 +152,8 @@ def tile_moslorasubspacemixerrankgain_d2p_kernel(
                         op0=ALU.mult,
                     )
 
-        def widen_plain(i, g):
-            for j in range(4 * g, 4 * g + 4):
+        def widen_plain(i, j0, j1):
+            for j in range(j0, j1):
                 nc.scalar.activation(
                     out=xw[i][:, j * P : (j + 1) * P],
                     in_=xb[i][:, j * P : (j + 1) * P].bitcast(FP8),
@@ -169,119 +162,81 @@ def tile_moslorasubspacemixerrankgain_d2p_kernel(
                 )
 
         def turn_x(i, g0=0, g1=2):
-            bank = next_bank(("x", i, g0))
+            bank = take(("x", i, g0))
             words = xw[i][:].bitcast(F32)
             for g in range(g0, g1):
                 for u in range(2):
                     n = 2 * g + u
-                    if (i, g) in PLAIN:
-                        src = words[:, 256 * g + u : 256 * (g + 1) : 2]
-                    else:
-                        src = words[:, n * P : (n + 1) * P]
+                    src = words[:, 256 * g + u : 256 * (g + 1) : 2] if (i, g) in PLAIN else words[:, n * P : (n + 1) * P]
                     nc.tensor.transpose(bank[:, n * P : (n + 1) * P], src, ident32[:])
 
-        def empty_x(i, g0=0, g1=2):
-            if i < WIDE:
-                dst = xg[i][:, g0 * 512 : g1 * 512].bitcast(F32).rearrange("p (g r u) -> p g r u", r=P, u=2)
+        def empty_x(i, g0=0, g1=2, copy=nc.scalar.copy):
+            if i < GROUP:
+                dst = xg[i][:].bitcast(F32).rearrange("p (g r u) -> p g r u", g=2, u=2)
             else:
-                pair = xg_pairs[(i - WIDE) // 2][:].bitcast(F32)
+                pair = xg_pairs[(i - GROUP) // 2][:].bitcast(F32)
                 dst = pair.rearrange("p (g i r u) -> p i g r u", g=2, i=2, u=2)[:, i % 2]
-            nc.scalar.copy(
-                out=dst,
+            copy(
+                out=dst[:, g0:g1],
                 in_=held[("x", i, g0)][:, g0 * 256 : g1 * 256].rearrange("p (g u r) -> p g r u", u=2, r=P),
             )
             release(("x", i, g0))
 
-        def x_codes(i, g):
-            if i < WIDE:
-                return xq[i][:, g * P : (g + 1) * P].bitcast(FP8X4), xq_s[i][:, g * P : (g + 1) * P]
-            cols = slice((i - WIDE) * P, (i - WIDE + 1) * P)
-            return xq_wide[g][:, cols].bitcast(FP8X4), xq_wide_s[g][:, cols]
-
-        def quant_x(i, g0=0, g1=2):
-            if i < WIDE:
+        def quant_x(i, count=1, g0=0, g1=2):
+            cols = slice(i % GROUP * P, (i % GROUP + count) * P)
+            src = xg[i] if i < GROUP else xg_pairs[(i - GROUP) // 2]
+            for g in range(g0, g1):
                 nc.vector.quantize_mx(
-                    out=xq[i][:, g0 * P : g1 * P].bitcast(FP8X4),
-                    scales=xq_s[i][:, g0 * P : g1 * P],
-                    in_=xg[i][:, g0 * 512 : g1 * 512],
+                    out=xq[i // GROUP][g][:, cols].bitcast(FP8X4),
+                    scales=xq_s[i // GROUP][g][:, cols],
+                    in_=src[:, g * count * 512 : (g + 1) * count * 512],
                 )
-            else:
-                cols = slice((i - WIDE) * P, (i - WIDE + 2) * P)
-                for g in range(g0, g1):
-                    nc.vector.quantize_mx(
-                        out=xq_wide[g][:, cols].bitcast(FP8X4),
-                        scales=xq_wide_s[g][:, cols],
-                        in_=xg_pairs[(i - WIDE) // 2][:, g * D : (g + 1) * D],
-                    )
 
-        def down_wide(t):
-            bank = next_bank(("pw", t))
+        def down(k, t):
+            bank = take(("p", k, t))
             for g in range(2):
                 nc.tensor.matmul_mx(
                     out=bank[:],
                     lhsT=a_w[:, g, t * 256 : (t + 1) * 256].bitcast(FP4X4),
                     lhsT_scale=a_s[:, g, t * P : (t + 1) * P],
-                    rhs=xq_wide[g][:].bitcast(FP8X4),
-                    rhs_scale=xq_wide_s[g][:],
+                    rhs=xq[k][g][:].bitcast(FP8X4),
+                    rhs_scale=xq_s[k][g][:],
                     start=(g == 0),
                     stop=(g == 1),
                 )
 
-        def gain_wide(t, on_vector=False):
-            plane, bank, gains = planes[:, t * 512 : (t + 1) * 512], held[("pw", t)][:], d_cols[:, t : t + 1]
+        def gain(k, t, on_vector=False):
+            plane, bank, gains = planes[k][:, t * 512 : (t + 1) * 512], held[("p", k, t)][:], d_cols[:, t : t + 1]
             if on_vector:
                 nc.vector.tensor_scalar(out=plane, in0=bank, scalar1=gains, scalar2=None, op0=ALU.mult)
             else:
                 nc.scalar.activation(out=plane, in_=bank, func=ACT.Copy, scale=gains)
-            release(("pw", t))
+            release(("p", k, t))
 
-        def weave(i):
-            n0 = (i - WIDE) * P
-            nc.vector.tensor_copy(
-                out=pg[i][:].rearrange("p (c n t) -> p c t n", n=4, t=4),
-                in_=planes[:].rearrange("p (t c n) -> p c t n", t=4, n=4)[:, n0 // 4 : (n0 + P) // 4],
+        def weave(i, copy=nc.vector.tensor_copy):
+            n0 = i % GROUP * P
+            copy(
+                out=pg[i // 2][:, i % 2 * R : (i % 2 + 1) * R].rearrange("p (c n t) -> p c t n", n=4, t=4),
+                in_=planes[i // GROUP][:].rearrange("p (t c n) -> p c t n", t=4, n=4)[:, n0 // 4 : (n0 + P) // 4],
             )
 
-        def down(i):
-            bank = next_bank(("p", i))
-            for t in range(4):
-                for g in range(2):
-                    nc.tensor.matmul_mx(
-                        out=bank[:, t * P : (t + 1) * P],
-                        lhsT=a_w[:, g, t * 256 : (t + 1) * 256].bitcast(FP4X4),
-                        lhsT_scale=a_s[:, g, t * P : (t + 1) * P],
-                        rhs=xq[i][:, g * P : (g + 1) * P].bitcast(FP8X4),
-                        rhs_scale=xq_s[i][:, g * P : (g + 1) * P],
-                        start=(g == 0),
-                        stop=(g == 1),
-                    )
-
-        def gain(i):
-            nc.vector.tensor_tensor(
-                out=pg[i][:].rearrange("p (c n t) -> p c t n", n=2, t=4),
-                in0=held[("p", i)][:].rearrange("p (t c n) -> p c t n", t=4, n=2),
-                in1=d_cols[:].unsqueeze(1).unsqueeze(3).to_broadcast([P, 64, 4, 2]),
-                op=ALU.mult,
-            )
-            release(("p", i))
-
-        def quant_p(i):
-            nc.vector.quantize_mx(out=pq[i][:].bitcast(FP8X4), scales=pq_s[i][:], in_=pg[i][:])
-
-        def quant_p_pair(i):
+        def quant_p(i, count=1):
+            cols = slice(i % 2 * P, (i % 2 + count) * P)
             nc.vector.quantize_mx(
-                out=pq_pairs[i // 2][:].bitcast(FP8X4), scales=pq_s_pairs[i // 2][:], in_=pg_pairs[i // 2][:]
+                out=pq[i // 2][:, cols].bitcast(FP8X4),
+                scales=pq_s[i // 2][:, cols],
+                in_=pg[i // 2][:, i % 2 * R : (i % 2 + count) * R],
             )
 
         def mix(h, b):
-            bank = next_bank(("c", h, b))
+            bank = take(("c", h, b))
             f0 = h * 512 + b * P
             for t in range(4):
                 nc.tensor.matmul_mx(
                     out=bank[:, t * P : (t + 1) * P],
                     lhsT=m_w[:, 0, t * 256 : (t + 1) * 256].bitcast(FP4X4),
                     lhsT_scale=m_s[:, 0, t * P : (t + 1) * P],
-                    rhs=bu_w[h][:, 0, 2 * b * P : 2 * (b + 1) * P].bitcast(FP4X4),
+                    rhs=bu_w[:, 0, 2 * f0 : 2 * (f0 + P)].bitcast(FP4X4),
                     rhs_scale=bu_s[:, 0, f0 : f0 + P],
                     start=(t == 0),
                     stop=(t == 3),
@@ -298,196 +253,188 @@ def tile_moslorasubspacemixerrankgain_d2p_kernel(
             nc.vector.quantize_mx(out=cq[h][:].bitcast(FP8X4), scales=cq_s[h][:], in_=cg[h][:])
 
         def base(i, h, c0=0, c1=512):
-            bank = next_bank(("b", i, h, c0))
-            width = 512 if c1 - c0 == 512 else P
-            for n0 in range(c0, c1, width):
-                for g in range(2):
-                    nc.tensor.matmul_mx(
-                        out=bank[:, n0 : n0 + width],
-                        lhsT=x_codes(i, g)[0],
-                        lhsT_scale=x_codes(i, g)[1],
-                        rhs=w0_w[h][:, g, 2 * n0 : 2 * (n0 + width)].bitcast(FP4X4),
-                        rhs_scale=w0_s[:, g, h * 512 + n0 : h * 512 + n0 + width],
-                        start=(g == 0),
-                        stop=(g == 1),
-                    )
+            bank = take(("b", i, h, c0))
+            cols = slice(i % GROUP * P, (i % GROUP + 1) * P)
+            for g in range(2):
+                nc.tensor.matmul_mx(
+                    out=bank[:, c0:c1],
+                    lhsT=xq[i // GROUP][g][:, cols].bitcast(FP8X4),
+                    lhsT_scale=xq_s[i // GROUP][g][:, cols],
+                    rhs=w0_w[h][:, g, 2 * c0 : 2 * c1].bitcast(FP4X4),
+                    rhs_scale=w0_s[:, g, h * 512 + c0 : h * 512 + c1],
+                    start=(g == 0),
+                    stop=(g == 1),
+                )
 
-        def up(i, h, c0=0, c1=512):
+        def up(i, h):
+            cols = slice(i % 2 * P, (i % 2 + 1) * P)
             nc.tensor.matmul_mx(
-                out=next_bank(("t", i, h, c0))[:, c0:c1],
-                lhsT=pq[i][:].bitcast(FP8X4),
-                lhsT_scale=pq_s[i][:],
-                rhs=cq[h][:, c0:c1].bitcast(FP8X4),
-                rhs_scale=cq_s[h][:, c0:c1],
+                out=take(("t", i, h, 0))[:],
+                lhsT=pq[i // 2][:, cols].bitcast(FP8X4),
+                lhsT_scale=pq_s[i // 2][:, cols],
+                rhs=cq[h][:].bitcast(FP8X4),
+                rhs_scale=cq_s[h][:],
                 start=True,
                 stop=True,
             )
 
-        def park(kind, i, h, c0=0, c1=512):
-            nc.scalar.copy(out=res[h][i][:, c0:c1], in_=held[(kind, i, h, c0)][:, c0:c1])
-            release((kind, i, h, c0))
+        def park(kind, i, h):
+            nc.scalar.copy(out=res[h][i][:], in_=held[(kind, i, h, 0)][:])
+            release((kind, i, h, 0))
             parked.setdefault((i, h), kind)
 
-        def finish(i, h, c0=0, c1=512, queue=nc.sync, own_bank=False):
-            cols = slice(c0, c1)
-            acc = res[h][i][:, cols]
-            key = ("t" if parked[(i, h)] == "b" else "b", i, h, c0 if own_bank else 0)
-            if key[0] == "t":
-                t_part, base_part = held[key][:, cols], acc
-            else:
-                t_part, base_part = acc, held[key][:, cols]
+        def finish(i, h, c0=0, c1=512):
+            acc = res[h][i][:, c0:c1]
+            key = ("t" if parked[(i, h)] == "b" else "b", i, h, c0)
+            fresh = held[key][:, c0:c1]
+            t_part, base_part = (fresh, acc) if key[0] == "t" else (acc, fresh)
             nc.vector.scalar_tensor_tensor(out=acc, in0=t_part, scalar=ALPHA, in1=base_part, op0=ALU.mult, op1=ALU.add)
-            queue.dma_start(out=out_rows[:, i, h * 512 + c0 : h * 512 + c1], in_=acc)
-            if own_bank or c1 == 512:
-                release(key)
+            nc.sync.dma_start(out=out_rows[:, i, h * 512 + c0 : h * 512 + c1], in_=acc)
+            release(key)
 
-        sp, act, pool = nc.sync, nc.scalar, nc.gpsimd
-        for tile in (warm, d_rows, w0_s, bu_s, a_sraw, m_sraw):
+        for tile in (warm, w0_s, bu_s, a_sraw, m_sraw, d_rows):
             zero(tile)
-        load_xs(act)
+        load_xs()
         load_x(0)
         identity()
-        load_d()
+        load_scales(bu_s, bu_scales, range(3), nc.gpsimd)
         load_x(1)
-        load_scales(w0_s, w0_scales, [(j, sp) for j in range(4)])
+        load_scales(w0_s, w0_scales)
         load_words(w0_w[0][:], w0_words[:, :, 0:1024])
         load_words(w0_w[1][:], w0_words[:, :, 1024:2048])
-        load_scales(a_sraw, a_scales, [(j, sp) for j in range(4)])
-        load_words(a_raw[:], a_words)
         load_x(2)
-        load_scales(m_sraw, m_scales, [(j, sp) for j in range(4)])
-        load_words(m_raw[:], m_words)
-        load_words(bu_all[:], bu_words)
-        load_scales(bu_s, bu_scales, [(j, sp) for j in range(4)])
+        load_words(a_raw[:], a_words)
+        load_scales(a_sraw, a_scales)
         load_x(3)
+        load_d()
+        load_words(m_raw[:], m_words)
+        load_words(bu_w[:], bu_words)
+        load_scales(m_sraw, m_scales)
+        load_scales(bu_s, bu_scales, range(3, 4))
 
         warm_up(4, "warm0")
-        widen_plain(0, 1)
-        for i in range(2):
-            for g in range(2):
-                if (i, g) not in PLAIN:
-                    widen(i, (g,))
-                turn_x(i, g, g + 1)
-                empty_x(i, g, g + 1)
-            if i == 0:
-                warm_up(2, "warm1")
-        quant_x(0, 0, 1)
-        quant_x(0, 1, 2)
+        widen_plain(0, 4, 8)
+        widen(0, 0, 1)
         for g in range(2):
-            widen(2, (g,))
-            quant_x(1, g, g + 1)
+            turn_x(0, g, g + 1)
+            empty_x(0, g, g + 1)
+        warm_up(2, "warm1")
+        for g in range(2):
+            widen(1, g, g + 1)
+            turn_x(1, g, g + 1)
+            empty_x(1, g, g + 1)
+        quant_x(0)
+        widen(2)
+        widen(3)
+        quant_x(1)
         for h in range(2):
             base(0, h)
             park("b", 0, h)
-        widen(3)
+        turn_x(2)
+        turn_x(3)
+        empty_x(2)
+        empty_x(3)
+        widen(4, 0, 1)
         reorder(a_w, a_raw)
         reorder(a_s, a_sraw)
-        base(1, 0)
-        park("b", 1, 0)
-        turn_x(2)
-        empty_x(2)
-        turn_x(3)
-        turn_d()
-        base(1, 1)
-        empty_x(3)
-        empty_d()
-        park("b", 1, 1)
-        widen(4)
-        widen_plain(5, 0)
-        widen_plain(5, 1)
-        down(0)
-        down(1)
         quant_x(2)
+        widen(4, 1, 2)
+        quant_x(3)
+        for h in range(2):
+            base(1, h)
+            park("b", 1, h)
+        turn_d()
+        base(2, 0)
+        empty_d()
+        park("b", 2, 0)
+        widen(5)
         reorder(m_w, m_raw)
         reorder(m_s, m_sraw)
-        quant_x(3)
-        gain(0)
-        down(2)
-        gain(1)
+        widen(6)
+        widen(7)
+        for t in range(4):
+            down(0, t)
+            gain(0, t, t == 2)
         for b in range(4):
             mix(0, b)
+        empty_c(0, 0, nc.vector.tensor_copy)
+        for b in (1, 3, 2):
             empty_c(0, b)
-        down(3)
-        gain(2)
-        widen(6)
-        for b in range(4):
-            mix(1, b)
-            empty_c(1, b)
-        widen(7)
-        gain(3)
-        quant_p_pair(0)
-        quant_c(0)
-        quant_p_pair(2)
+        for i in range(4):
+            weave(i)
+        quant_p(0, 2)
         for i in range(4, 8):
             turn_x(i)
+        for i in (5, 4, 7):
             empty_x(i)
-        up(0, 0)
-        base(2, 0)
-        up(1, 0)
-        quant_c(1)
-        finish(0, 0)
-        base(2, 1)
-        up(2, 0)
-        park("t", 2, 0)
-        quant_x(4)
-        finish(1, 0)
+        quant_c(0)
+        quant_p(2, 2)
+        for b in range(4):
+            mix(1, b)
+        empty_c(1, 0, nc.vector.tensor_copy)
+        empty_x(6)
+        quant_x(4, 2)
+        quant_x(6, 2)
+        for i in range(3):
+            up(i, 0)
+        for b in (3, 2, 1):
+            empty_c(1, b)
+        base(3, 0)
         up(3, 0)
         park("t", 3, 0)
-        quant_x(6)
-        base(3, 0)
         finish(2, 0)
-        for i in range(3):
-            up(i, 1)
-        park("t", 2, 1)
+        finish(1, 0)
+        quant_c(1)
+        down(1, 0)
+        down(1, 1)
+        gain(1, 1)
+        gain(1, 0)
+        finish(0, 0)
         finish(3, 0)
-        for t in range(4):
-            down_wide(t)
-            gain_wide(t, t == 2)
-            if t < 2:
-                finish(t, 1)
-        up(3, 1)
-        park("t", 3, 1)
-        base(3, 1)
-        finish(2, 1)
+        down(1, 2)
+        down(1, 3)
+        gain(1, 3)
+        gain(1, 2)
+        up(0, 1)
+        up(1, 1)
+        finish(1, 1)
+        finish(0, 1)
         weave(4)
         weave(5)
         quant_p(4)
-        finish(3, 1)
+        for i in (2, 3):
+            up(i, 1)
+            park("t", i, 1)
+            base(i, 1)
+        weave(6, nc.scalar.copy)
+        weave(7, nc.scalar.copy)
+        finish(2, 1)
         quant_p(5)
+        base(4, 0)
+        base(4, 1)
         for h in range(2):
-            base(4, h)
-            park("b", 4, h)
-        base(5, 0)
-        weave(6)
-        up(4, 0)
-        up(4, 1)
+            up(4, h)
+            park("t", 4, h)
+        finish(3, 1)
+        quant_p(6, 2)
         up(5, 0)
         park("t", 5, 0)
         finish(4, 0)
-        quant_p(6)
-        up(5, 1)
-        park("t", 5, 1)
-        base(5, 1)
-        weave(7)
         finish(4, 1)
-        quant_p(7)
-        finish(5, 0)
-        finish(5, 1)
-        for i in range(6, TILES):
-            last = i == TILES - 1
-            up(i, 0)
-            park("t", i, 0)
-            if last:
-                up(i, 1)
-                park("t", i, 1)
-            base(i, 0)
-            if not last:
-                up(i, 1)
-                park("t", i, 1)
-            base(i, 1)
-            finish(i, 0)
-            if last:
-                finish(i, 1, 0, 256)
-                finish(i, 1, 256, 512)
-            else:
-                finish(i, 1)
+        for i, h in ((5, 0), (5, 1), (6, 0)):
+            ahead = (i, 1) if h == 0 else (i + 1, 0)
+            base(i, h)
+            up(*ahead)
+            park("t", *ahead)
+            finish(i, h)
+        up(7, 0)
+        park("t", 7, 0)
+        base(6, 1, 0, 256)
+        finish(6, 1, 0, 256)
+        base(6, 1, 256, 512)
+        up(7, 1)
+        park("t", 7, 1)
+        finish(6, 1, 256, 512)
+        for h, c0, c1 in ((0, 0, 256), (0, 256, 512), (1, 0, 256), (1, 256, 512)):
+            base(7, h, c0, c1)
+            finish(7, h, c0, c1)

@@ -47,7 +47,7 @@ def tile_moslorasubspacemixerrankgain_d2p_kernel(
         d_cols = sbuf("d_cols", [4], F32)
         warm = sbuf("warm", [512], BF16)
         xs = sbuf("xs", [8], F32)
-        x_loads = [(0, 1), (1, 4), (4, 6), (6, 8)]
+        x_loads = [(0, 2), (2, 4), (4, 6), (6, 8)]
         xb_parts = [sbuf("xb%d" % i0, [i1 - i0, D], U8) for i0, i1 in x_loads]
         xb = [part[:, i - i0, :] for part, (i0, i1) in zip(xb_parts, x_loads) for i in range(i0, i1)]
         a_raw = sbuf("a_raw", [2, 1024], U8)
@@ -101,8 +101,8 @@ def tile_moslorasubspacemixerrankgain_d2p_kernel(
             i0, i1 = x_loads[n]
             nc.sync.dma_start(out=xb_parts[n][:], in_=x_rows[:, i0:i1, :])
 
-        def load_words(dst, src):
-            nc.sync.dma_start(out=dst.bitcast(I32), in_=src.rearrange("g p n -> p g n").bitcast(I32))
+        def load_words(dst, src, queue=nc.sync):
+            queue.dma_start(out=dst.bitcast(I32), in_=src.rearrange("g p n -> p g n").bitcast(I32))
 
         def load_xs():
             nc.scalar.dma_start(out=xs[:], in_=x_scale.unsqueeze(1).to_broadcast([8, 16, 8]))
@@ -278,8 +278,10 @@ def tile_moslorasubspacemixerrankgain_d2p_kernel(
                 stop=True,
             )
 
-        def park(kind, i, h):
-            nc.scalar.copy(out=res[h][i][:], in_=held[(kind, i, h, 0)][:])
+        def park(kind, i, h, pieces=1):
+            for c0 in range(0, 512, 512 // pieces):
+                cols = slice(c0, c0 + 512 // pieces)
+                nc.scalar.copy(out=res[h][i][:, cols], in_=held[(kind, i, h, 0)][:, cols])
             release((kind, i, h, 0))
             parked.setdefault((i, h), kind)
 
@@ -294,63 +296,63 @@ def tile_moslorasubspacemixerrankgain_d2p_kernel(
 
         for tile in (warm, w0_s, bu_s, a_sraw, m_sraw, d_rows):
             zero(tile)
-        load_xs()
         load_x(0)
+        load_xs()
         identity()
         load_scales(bu_s, bu_scales, range(3), nc.gpsimd)
         load_x(1)
-        load_scales(w0_s, w0_scales)
         load_words(w0_w[0][:], w0_words[:, :, 0:1024])
-        load_words(w0_w[1][:], w0_words[:, :, 1024:2048])
+        load_scales(w0_s, w0_scales)
         load_x(2)
+        load_words(w0_w[1][:], w0_words[:, :, 1024:2048])
         load_words(a_raw[:], a_words)
+        load_d()
         load_scales(a_sraw, a_scales)
         load_x(3)
-        load_d()
         load_words(m_raw[:], m_words)
         load_words(bu_w[:], bu_words)
         load_scales(m_sraw, m_scales)
         load_scales(bu_s, bu_scales, range(3, 4))
 
-        warm_up(4, "warm0")
+        warm_up(5, "warm0")
         widen_plain(0, 4, 8)
         widen(0, 0, 1)
         for g in range(2):
             turn_x(0, g, g + 1)
             empty_x(0, g, g + 1)
-        warm_up(2, "warm1")
-        for g in range(2):
-            widen(1, g, g + 1)
-            turn_x(1, g, g + 1)
-            empty_x(1, g, g + 1)
-        quant_x(0)
+        widen(1)
+        turn_x(1)
+        empty_x(1)
+        warm_up(1, "warm1")
         widen(2)
-        widen(3)
-        quant_x(1)
-        for h in range(2):
-            base(0, h)
-            park("b", 0, h)
         turn_x(2)
-        turn_x(3)
         empty_x(2)
+        for g in range(2):
+            quant_x(0, 1, g, g + 1)
+            widen(3, g, g + 1)
+        quant_x(1)
+        base(0, 0)
+        park("b", 0, 0)
+        turn_x(3)
         empty_x(3)
         widen(4, 0, 1)
-        reorder(a_w, a_raw)
-        reorder(a_s, a_sraw)
         quant_x(2)
         widen(4, 1, 2)
+        widen(5, 0, 1)
+        reorder(a_w, a_raw)
+        reorder(a_s, a_sraw)
         quant_x(3)
-        for h in range(2):
-            base(1, h)
-            park("b", 1, h)
+        for i, h in ((1, 0), (0, 1), (1, 1)):
+            base(i, h)
+            park("b", i, h)
         turn_d()
         base(2, 0)
         empty_d()
         park("b", 2, 0)
-        widen(5)
+        widen(5, 1, 2)
+        widen(6)
         reorder(m_w, m_raw)
         reorder(m_s, m_sraw)
-        widen(6)
         widen(7)
         for t in range(4):
             down(0, t)
@@ -385,56 +387,53 @@ def tile_moslorasubspacemixerrankgain_d2p_kernel(
         finish(2, 0)
         finish(1, 0)
         quant_c(1)
-        down(1, 0)
-        down(1, 1)
-        gain(1, 1)
-        gain(1, 0)
-        finish(0, 0)
-        finish(3, 0)
-        down(1, 2)
-        down(1, 3)
-        gain(1, 3)
-        gain(1, 2)
-        up(0, 1)
-        up(1, 1)
-        finish(1, 1)
-        finish(0, 1)
+        for t in range(4):
+            down(1, t)
+            gain(1, t)
+            if t == 2:
+                finish(0, 0)
+                finish(3, 0)
+        for i in range(2):
+            up(i, 1)
+            finish(i, 1)
         weave(4)
         weave(5)
-        quant_p(4)
         for i in (2, 3):
             up(i, 1)
             park("t", i, 1)
             base(i, 1)
-        weave(6, nc.scalar.copy)
-        weave(7, nc.scalar.copy)
+        quant_p(4)
         finish(2, 1)
         quant_p(5)
-        base(4, 0)
-        base(4, 1)
+        finish(3, 1)
+        weave(6, nc.scalar.copy)
+        for h in range(2):
+            base(4, h)
+            park("b", 4, h)
+        quant_p(6)
         for h in range(2):
             up(4, h)
-            park("t", 4, h)
-        finish(3, 1)
-        quant_p(6, 2)
+            finish(4, h)
+        weave(7)
         up(5, 0)
         park("t", 5, 0)
-        finish(4, 0)
-        finish(4, 1)
-        for i, h in ((5, 0), (5, 1), (6, 0)):
-            ahead = (i, 1) if h == 0 else (i + 1, 0)
-            base(i, h)
+        steps = [(5, 0), (5, 1), (6, 0), (6, 1), (7, 0)]
+        for now, ahead in zip(steps[:3], steps[1:]):
             up(*ahead)
             park("t", *ahead)
-            finish(i, h)
+            base(*now)
+            finish(*now)
+            if now == (5, 0):
+                quant_p(7)
         up(7, 0)
         park("t", 7, 0)
-        base(6, 1, 0, 256)
-        finish(6, 1, 0, 256)
-        base(6, 1, 256, 512)
+        for c0 in (0, 256):
+            base(6, 1, c0, c0 + 256)
+            finish(6, 1, c0, c0 + 256)
+        base(7, 0, 0, 256)
+        finish(7, 0, 0, 256)
         up(7, 1)
-        park("t", 7, 1)
-        finish(6, 1, 256, 512)
-        for h, c0, c1 in ((0, 0, 256), (0, 256, 512), (1, 0, 256), (1, 256, 512)):
+        park("t", 7, 1, 2)
+        for h, c0, c1 in ((0, 256, 512), (1, 0, 256), (1, 256, 512)):
             base(7, h, c0, c1)
             finish(7, h, c0, c1)

@@ -21,7 +21,7 @@ P = 128
 TILES = N // P
 BANKS = 8
 GROUP = 4
-PLAIN = ((0, 1),)
+PLAIN = ((0, 1), (2, 1))
 ALPHA = 1.0 / math.sqrt(R)
 
 
@@ -303,53 +303,53 @@ def tile_moslorasubspacemixerrankgain_d2p_kernel(
         load_x(1)
         load_words(w0_w[0][:], w0_words[:, :, 0:1024])
         load_scales(w0_s, w0_scales)
-        load_x(2)
         load_words(w0_w[1][:], w0_words[:, :, 1024:2048])
+        load_x(2)
         load_words(a_raw[:], a_words)
-        load_d()
         load_scales(a_sraw, a_scales)
+        load_d()
         load_x(3)
         load_words(m_raw[:], m_words)
         load_words(bu_w[:], bu_words)
         load_scales(m_sraw, m_scales)
         load_scales(bu_s, bu_scales, range(3, 4))
 
-        warm_up(5, "warm0")
+        warm_up(6, "warm0")
         widen_plain(0, 4, 8)
         widen(0, 0, 1)
-        for g in range(2):
-            turn_x(0, g, g + 1)
-            empty_x(0, g, g + 1)
-        widen(1)
-        turn_x(1)
-        empty_x(1)
+        widen_plain(2, 4, 8)
+        turn_x(0, 0, 1)
+        empty_x(0, 0, 1)
         warm_up(1, "warm1")
-        widen(2)
+        turn_x(0, 1, 2)
+        empty_x(0, 1, 2)
+        widen(1)
+        widen(2, 0, 1)
+        widen(3)
+        for g in range(2):
+            turn_x(1, g, g + 1)
+            empty_x(1, g, g + 1)
         turn_x(2)
         empty_x(2)
-        for g in range(2):
-            quant_x(0, 1, g, g + 1)
-            widen(3, g, g + 1)
-        quant_x(1)
-        base(0, 0)
-        park("b", 0, 0)
+
         turn_x(3)
         empty_x(3)
-        widen(4, 0, 1)
+        quant_x(0)
+        quant_x(1)
         quant_x(2)
-        widen(4, 1, 2)
-        widen(5, 0, 1)
+        widen(4, 0, 1)
+        quant_x(3)
         reorder(a_w, a_raw)
         reorder(a_s, a_sraw)
-        quant_x(3)
-        for i, h in ((1, 0), (0, 1), (1, 1)):
+        widen(4, 1, 2)
+        for i, h in ((0, 0), (1, 0), (0, 1), (1, 1)):
             base(i, h)
             park("b", i, h)
         turn_d()
-        base(2, 0)
         empty_d()
+        base(2, 0)
         park("b", 2, 0)
-        widen(5, 1, 2)
+        widen(5)
         widen(6)
         reorder(m_w, m_raw)
         reorder(m_s, m_sraw)

@@ -47,7 +47,7 @@ def tile_moslorasubspacemixerrankgain_d2p_kernel(
         d_cols = sbuf("d_cols", [4], F32)
         warm = sbuf("warm", [512], BF16)
         xs = sbuf("xs", [8], F32)
-        x_loads = [(0, 2), (2, 4), (4, 6), (6, 8)]
+        x_loads = [(0, 1), (1, 2), (2, 4), (4, 6), (6, 8)]
         xb_parts = [sbuf("xb%d" % i0, [i1 - i0, D], U8) for i0, i1 in x_loads]
         xb = [part[:, i - i0, :] for part, (i0, i1) in zip(xb_parts, x_loads) for i in range(i0, i1)]
         a_raw = sbuf("a_raw", [2, 1024], U8)
@@ -60,7 +60,7 @@ def tile_moslorasubspacemixerrankgain_d2p_kernel(
         m_s = sbuf("m_s", [1, 512], U8)
         w0_w = several("w0_w", [2, 1024], U8, 2)
         w0_s = sbuf("w0_s", [2, 1024], U8)
-        bu_w = sbuf("bu_w", [1, 2048], U8)
+        bu_w = several("bu_w", [1, 1024], U8, 2)
         bu_s = sbuf("bu_s", [1, 1024], U8)
         xw = several("xw", [D], BF16, TILES)
         xg = several("xg", [D], BF16, GROUP)
@@ -236,7 +236,7 @@ def tile_moslorasubspacemixerrankgain_d2p_kernel(
                     out=bank[:, t * P : (t + 1) * P],
                     lhsT=m_w[:, 0, t * 256 : (t + 1) * 256].bitcast(FP4X4),
                     lhsT_scale=m_s[:, 0, t * P : (t + 1) * P],
-                    rhs=bu_w[:, 0, 2 * f0 : 2 * (f0 + P)].bitcast(FP4X4),
+                    rhs=bu_w[h][:, 0, 2 * b * P : 2 * (b + 1) * P].bitcast(FP4X4),
                     rhs_scale=bu_s[:, 0, f0 : f0 + P],
                     start=(t == 0),
                     stop=(t == 3),
@@ -278,10 +278,10 @@ def tile_moslorasubspacemixerrankgain_d2p_kernel(
                 stop=True,
             )
 
-        def park(kind, i, h, pieces=1):
+        def park(kind, i, h, pieces=1, copy=nc.scalar.copy):
             for c0 in range(0, 512, 512 // pieces):
                 cols = slice(c0, c0 + 512 // pieces)
-                nc.scalar.copy(out=res[h][i][:, cols], in_=held[(kind, i, h, 0)][:, cols])
+                copy(out=res[h][i][:, cols], in_=held[(kind, i, h, 0)][:, cols])
             release((kind, i, h, 0))
             parked.setdefault((i, h), kind)
 
@@ -294,25 +294,26 @@ def tile_moslorasubspacemixerrankgain_d2p_kernel(
             nc.sync.dma_start(out=out_rows[:, i, h * 512 + c0 : h * 512 + c1], in_=acc)
             release(key)
 
-        for tile in (warm, w0_s, bu_s, a_sraw, m_sraw, d_rows):
+        for tile in (warm, m_sraw, w0_s, a_sraw, bu_s, d_rows):
             zero(tile)
         load_x(0)
         load_xs()
         identity()
-        load_scales(bu_s, bu_scales, range(3), nc.gpsimd)
+        load_scales(m_sraw, m_scales, range(4), nc.gpsimd)
         load_x(1)
+        load_x(2)
         load_words(w0_w[0][:], w0_words[:, :, 0:1024])
         load_scales(w0_s, w0_scales)
         load_words(w0_w[1][:], w0_words[:, :, 1024:2048])
-        load_x(2)
+        load_x(3)
         load_words(a_raw[:], a_words)
         load_scales(a_sraw, a_scales)
         load_d()
-        load_x(3)
+        load_x(4)
         load_words(m_raw[:], m_words)
-        load_words(bu_w[:], bu_words)
-        load_scales(m_sraw, m_scales)
-        load_scales(bu_s, bu_scales, range(3, 4))
+        load_words(bu_w[0][:], bu_words[:, :, 0:1024])
+        load_scales(bu_s, bu_scales)
+        load_words(bu_w[1][:], bu_words[:, :, 1024:2048])
 
         warm_up(6, "warm0")
         widen_plain(0, 4, 8)
@@ -345,9 +346,9 @@ def tile_moslorasubspacemixerrankgain_d2p_kernel(
         for i, h in ((0, 0), (1, 0), (0, 1), (1, 1)):
             base(i, h)
             park("b", i, h)
+        base(2, 0)
         turn_d()
         empty_d()
-        base(2, 0)
         park("b", 2, 0)
         widen(5)
         widen(6)
@@ -417,23 +418,20 @@ def tile_moslorasubspacemixerrankgain_d2p_kernel(
         weave(7)
         up(5, 0)
         park("t", 5, 0)
-        steps = [(5, 0), (5, 1), (6, 0), (6, 1), (7, 0)]
-        for now, ahead in zip(steps[:3], steps[1:]):
+        steps = [(5, 0), (5, 1), (6, 0)]
+        for now, ahead in zip(steps[:2], steps[1:]):
             up(*ahead)
             park("t", *ahead)
             base(*now)
             finish(*now)
             if now == (5, 0):
                 quant_p(7)
-        up(7, 0)
-        park("t", 7, 0)
-        for c0 in (0, 256):
-            base(6, 1, c0, c0 + 256)
-            finish(6, 1, c0, c0 + 256)
-        base(7, 0, 0, 256)
-        finish(7, 0, 0, 256)
-        up(7, 1)
-        park("t", 7, 1, 2)
-        for h, c0, c1 in ((0, 256, 512), (1, 0, 256), (1, 256, 512)):
-            base(7, h, c0, c1)
-            finish(7, h, c0, c1)
+        last = [(6, 0), (6, 1), (7, 0), (7, 1)]
+        for n, now in enumerate(last):
+            base(*now, 0, 256)
+            finish(*now, 0, 256)
+            if n < 3:
+                up(*last[n + 1])
+                park("t", *last[n + 1], 2)
+            base(*now, 256, 512)
+            finish(*now, 256, 512)

@@ -294,12 +294,12 @@ def tile_moslorasubspacemixerrankgain_d2p_kernel(
             nc.sync.dma_start(out=out_rows[:, i, h * 512 + c0 : h * 512 + c1], in_=acc)
             release(key)
 
-        for tile in (warm, m_sraw, w0_s, a_sraw, bu_s, d_rows):
+        for tile in (warm, bu_s, w0_s, a_sraw, m_sraw, d_rows):
             zero(tile)
         load_x(0)
         load_xs()
         identity()
-        load_scales(m_sraw, m_scales, range(4), nc.gpsimd)
+        load_scales(bu_s, bu_scales, range(3), nc.gpsimd)
         load_x(1)
         load_x(2)
         load_words(w0_w[0][:], w0_words[:, :, 0:1024])
@@ -311,8 +311,9 @@ def tile_moslorasubspacemixerrankgain_d2p_kernel(
         load_d()
         load_x(4)
         load_words(m_raw[:], m_words)
+        load_scales(m_sraw, m_scales)
         load_words(bu_w[0][:], bu_words[:, :, 0:1024])
-        load_scales(bu_s, bu_scales)
+        load_scales(bu_s, bu_scales, range(3, 4))
         load_words(bu_w[1][:], bu_words[:, :, 1024:2048])
 
         warm_up(6, "warm0")

import math
from contextlib import ExitStack

import concourse.mybir as mybir

N, D, F, R = 1024, 1024, 1024, 512
FLOPS = 2 * N * D * F + 2 * N * D * R + 2 * R * R * F + 2 * N * R * F

F32 = mybir.dt.float32
BF16 = mybir.dt.bfloat16
I32 = mybir.dt.int32
U32 = mybir.dt.uint32
U8 = mybir.dt.uint8
FP8 = mybir.dt.float8_e4m3fn
FP8X4 = mybir.dt.float8_e4m3fn_x4
FP4X4 = mybir.dt.float4_e2m1fn_x4
ALU = mybir.AluOpType
ACT = mybir.ActivationFunctionType

P = 128
TILES = N // P
BANKS = 8
GROUP = 4
PLAIN = ((0, 1), (2, 1))
ALPHA = 1.0 / math.sqrt(R)


def tile_moslorasubspacemixerrankgain_d2p_kernel(
    tc, x_bytes, x_scale, w0_words, w0_scales, a_words, a_scales, d, m_words, m_scales, bu_words, bu_scales, out
):
    nc = tc.nc
    with ExitStack() as ctx:
        keep = ctx.enter_context(tc.tile_pool(name="keep", bufs=1))
        psum = ctx.enter_context(tc.psum_pool(name="psum", bufs=1))
        ctx.enter_context(tc.manual_schedule())

        def sbuf(name, shape, dtype):
            return keep.tile([P] + shape, dtype, align_bytes=64, name=name)

        def several(name, shape, dtype, count):
            return [sbuf("%s%d" % (name, i), shape, dtype) for i in range(count)]

        ident32 = sbuf("ident32", [P], F32)
        offsets = sbuf("offsets", [P], I32)
        ident16 = sbuf("ident16", [P], BF16)
        d_rows = sbuf("d_rows", [P], BF16)
        d_cols = sbuf("d_cols", [4], F32)
        warm = sbuf("warm", [512], BF16)
        xs = sbuf("xs", [8], F32)
        x_loads = [(0, 1), (1, 2), (2, 4), (4, 6), (6, 8)]
        xb_parts = [sbuf("xb%d" % i0, [i1 - i0, D], U8) for i0, i1 in x_loads]
        xb = [part[:, i - i0, :] for part, (i0, i1) in zip(xb_parts, x_loads) for i in range(i0, i1)]
        a_raw = sbuf("a_raw", [2, 1024], U8)
        a_w = sbuf("a_w", [2, 1024], U8)
        a_sraw = sbuf("a_sraw", [2, 512], U8)
        a_s = sbuf("a_s", [2, 512], U8)
        m_raw = sbuf("m_raw", [1, 1024], U8)
        m_w = sbuf("m_w", [1, 1024], U8)
        m_sraw = sbuf("m_sraw", [1, 512], U8)
        m_s = sbuf("m_s", [1, 512], U8)
        w0_w = several("w0_w", [2, 1024], U8, 2)
        w0_s = sbuf("w0_s", [2, 1024], U8)
        bu_w = several("bu_w", [1, 1024], U8, 2)
        bu_s = sbuf("bu_s", [1, 1024], U8)
        xw = several("xw", [D], BF16, TILES)
        xg = several("xg", [D], BF16, GROUP)
        xg_pairs = several("xg_pair", [2 * D], BF16, 2)
        xq = [several("xq%d_" % k, [512], U32, 2) for k in range(2)]
        xq_s = [several("xq_s%d_" % k, [512], U8, 2) for k in range(2)]
        planes = several("planes", [2048], BF16, 2)
        pg = several("pg", [2 * R], BF16, TILES // 2)
        pq = several("pq", [2 * P], U32, TILES // 2)
        pq_s = several("pq_s", [2 * P], U8, TILES // 2)
        cg = several("cg", [2048], BF16, 2)
        cq = several("cq", [512], U32, 2)
        cq_s = several("cq_s", [512], U8, 2)
        res = [several("res%d_" % h, [512], F32, TILES) for h in range(2)]
        banks = [psum.tile([P, 512], F32, name="bank%d" % b) for b in range(BANKS)]

        x_rows = x_bytes.rearrange("(p i) k -> p i k", i=TILES)
        out_rows = out.rearrange("(p i) f -> p i f", i=TILES)

        free = list(banks)
        held = {}
        parked = {}

        def take(key):
            if key not in held:
                held.setdefault(key, free.pop(0))
            return held[key]

        def release(key):
            free.append(held[key])

        def load_scales(plane, src, which=range(4), queue=nc.sync):
            rows = src.bitcast(I32).rearrange("g (q j) n -> j q g n", j=4)
            for j in which:
                queue.dma_start(out=plane[j:P:32].bitcast(I32), in_=rows[j])

        def load_x(n):
            i0, i1 = x_loads[n]
            nc.sync.dma_start(out=xb_parts[n][:], in_=x_rows[:, i0:i1, :])

        def load_words(dst, src, queue=nc.sync):
            queue.dma_start(out=dst.bitcast(I32), in_=src.rearrange("g p n -> p g n").bitcast(I32))

        def load_xs():
            nc.scalar.dma_start(out=xs[:], in_=x_scale.unsqueeze(1).to_broadcast([8, 16, 8]))

        def load_d():
            nc.sync.dma_start(
                out=d_rows[0:4, :].rearrange("t (q e) -> t q e", e=8), in_=d.rearrange("(q t e) -> t q e", t=4, e=8)
            )

        def zero(tile):
            nc.vector.memset(tile[:].bitcast(I32), 0)

        def identity():
            nc.gpsimd.iota(offsets[:], pattern=[[1, P]], base=0, channel_multiplier=-1)
            nc.vector.tensor_scalar(out=ident32[:], in0=offsets[:], scalar1=0, scalar2=None, op0=ALU.is_equal)
            nc.scalar.copy(out=ident16[:], in_=ident32[:])

        def reorder(dst, src):
            nc.vector.tensor_copy(
                out=dst[:].bitcast(I32).rearrange("p g (t q w) -> p g t q w", t=4, q=16),
                in_=src[:].bitcast(I32).rearrange("p g (q t w) -> p g t q w", t=4, q=16),
            )

        def warm_up(count, key):
            bank = take(key)
            for n in range(count):
                nc.tensor.matmul(bank[:], lhsT=warm[:, 0:P], rhs=warm[:], start=True, stop=True)
            release(key)

        def turn_d():
            nc.tensor.matmul(take("d")[:, 0:4], lhsT=d_rows[:], rhs=ident16[:, 0:4], start=True, stop=True)

        def empty_d():
            nc.scalar.copy(out=d_cols[:], in_=held["d"][:, 0:4])
            release("d")

        def widen(i, g0=0, g1=2):
            for g in range(g0, g1):
                dst = xw[i][:, g * 512 : (g + 1) * 512].rearrange("p (u q e) -> p q u e", u=2, e=2)
                for b in range(4):
                    j = 4 * g + b
                    nc.vector.tensor_scalar(
                        out=dst[:, 32 * b : 32 * (b + 1)],
                        in0=xb[i][:, j * P : (j + 1) * P].bitcast(FP8).rearrange("p (q u e) -> p q u e", u=2, e=2),
                        scalar1=xs[:, j : j + 1],
                        scalar2=None,
                        op0=ALU.mult,
                    )

        def widen_plain(i, j0, j1):
            for j in range(j0, j1):
                nc.scalar.activation(
                    out=xw[i][:, j * P : (j + 1) * P],
                    in_=xb[i][:, j * P : (j + 1) * P].bitcast(FP8),
                    func=ACT.Copy,
                    scale=xs[:, j : j + 1],
                )

        def turn_x(i, g0=0, g1=2):
            bank = take(("x", i, g0))
            words = xw[i][:].bitcast(F32)
            for g in range(g0, g1):
                for u in range(2):
                    n = 2 * g + u
                    src = words[:, 256 * g + u : 256 * (g + 1) : 2] if (i, g) in PLAIN else words[:, n * P : (n + 1) * P]
                    nc.tensor.transpose(bank[:, n * P : (n + 1) * P], src, ident32[:])

        def empty_x(i, g0=0, g1=2, copy=nc.scalar.copy):
            if i < GROUP:
                dst = xg[i][:].bitcast(F32).rearrange("p (g r u) -> p g r u", g=2, u=2)
            else:
                pair = xg_pairs[(i - GROUP) // 2][:].bitcast(F32)
                dst = pair.rearrange("p (g i r u) -> p i g r u", g=2, i=2, u=2)[:, i % 2]
            copy(
                out=dst[:, g0:g1],
                in_=held[("x", i, g0)][:, g0 * 256 : g1 * 256].rearrange("p (g u r) -> p g r u", u=2, r=P),
            )
            release(("x", i, g0))

        def quant_x(i, count=1, g0=0, g1=2):
            cols = slice(i % GROUP * P, (i % GROUP + count) * P)
            src = xg[i] if i < GROUP else xg_pairs[(i - GROUP) // 2]
            for g in range(g0, g1):
                nc.vector.quantize_mx(
                    out=xq[i // GROUP][g][:, cols].bitcast(FP8X4),
                    scales=xq_s[i // GROUP][g][:, cols],
                    in_=src[:, g * count * 512 : (g + 1) * count * 512],
                )

        def down(k, t):
            bank = take(("p", k, t))
            for g in range(2):
                nc.tensor.matmul_mx(
                    out=bank[:],
                    lhsT=a_w[:, g, t * 256 : (t + 1) * 256].bitcast(FP4X4),
                    lhsT_scale=a_s[:, g, t * P : (t + 1) * P],
                    rhs=xq[k][g][:].bitcast(FP8X4),
                    rhs_scale=xq_s[k][g][:],
                    start=(g == 0),
                    stop=(g == 1),
                )

        def gain(k, t, on_vector=False):
            plane, bank, gains = planes[k][:, t * 512 : (t + 1) * 512], held[("p", k, t)][:], d_cols[:, t : t + 1]
            if on_vector:
                nc.vector.tensor_scalar(out=plane, in0=bank, scalar1=gains, scalar2=None, op0=ALU.mult)
            else:
                nc.scalar.activation(out=plane, in_=bank, func=ACT.Copy, scale=gains)
            release(("p", k, t))

        def weave(i, copy=nc.vector.tensor_copy):
            n0 = i % GROUP * P
            copy(
                out=pg[i // 2][:, i % 2 * R : (i % 2 + 1) * R].rearrange("p (c n t) -> p c t n", n=4, t=4),
                in_=planes[i // GROUP][:].rearrange("p (t c n) -> p c t n", t=4, n=4)[:, n0 // 4 : (n0 + P) // 4],
            )

        def quant_p(i, count=1):
            cols = slice(i % 2 * P, (i % 2 + count) * P)
            nc.vector.quantize_mx(
                out=pq[i // 2][:, cols].bitcast(FP8X4),
                scales=pq_s[i // 2][:, cols],
                in_=pg[i // 2][:, i % 2 * R : (i % 2 + count) * R],
            )

        def mix(h, b):
            bank = take(("c", h, b))
            f0 = h * 512 + b * P
            for t in range(4):
                nc.tensor.matmul_mx(
                    out=bank[:, t * P : (t + 1) * P],
                    lhsT=m_w[:, 0, t * 256 : (t + 1) * 256].bitcast(FP4X4),
                    lhsT_scale=m_s[:, 0, t * P : (t + 1) * P],
                    rhs=bu_w[h][:, 0, 2 * b * P : 2 * (b + 1) * P].bitcast(FP4X4),
                    rhs_scale=bu_s[:, 0, f0 : f0 + P],
                    start=(t == 0),
                    stop=(t == 3),
                )

        def empty_c(h, b, copy=nc.scalar.copy):
            copy(
                out=cg[h][:, b * 512 : (b + 1) * 512].rearrange("p (f t) -> p f t", t=4),
                in_=held[("c", h, b)][:].rearrange("p (t f) -> p f t", t=4),
            )
            release(("c", h, b))

        def quant_c(h):
            nc.vector.quantize_mx(out=cq[h][:].bitcast(FP8X4), scales=cq_s[h][:], in_=cg[h][:])

        def base(i, h, c0=0, c1=512):
            bank = take(("b", i, h, c0))
            cols = slice(i % GROUP * P, (i % GROUP + 1) * P)
            for g in range(2):
                nc.tensor.matmul_mx(
                    out=bank[:, c0:c1],
                    lhsT=xq[i // GROUP][g][:, cols].bitcast(FP8X4),
                    lhsT_scale=xq_s[i // GROUP][g][:, cols],
                    rhs=w0_w[h][:, g, 2 * c0 : 2 * c1].bitcast(FP4X4),
                    rhs_scale=w0_s[:, g, h * 512 + c0 : h * 512 + c1],
                    start=(g == 0),
                    stop=(g == 1),
                )

        def up(i, h):
            cols = slice(i % 2 * P, (i % 2 + 1) * P)
            nc.tensor.matmul_mx(
                out=take(("t", i, h, 0))[:],
                lhsT=pq[i // 2][:, cols].bitcast(FP8X4),
                lhsT_scale=pq_s[i // 2][:, cols],
                rhs=cq[h][:].bitcast(FP8X4),
                rhs_scale=cq_s[h][:],
                start=True,
                stop=True,
            )

        def park(kind, i, h, pieces=1, copy=nc.scalar.copy):
            for c0 in range(0, 512, 512 // pieces):
                cols = slice(c0, c0 + 512 // pieces)
                copy(out=res[h][i][:, cols], in_=held[(kind, i, h, 0)][:, cols])
            release((kind, i, h, 0))
            parked.setdefault((i, h), kind)

        def finish(i, h, c0=0, c1=512):
            acc = res[h][i][:, c0:c1]
            key = ("t" if parked[(i, h)] == "b" else "b", i, h, c0)
            fresh = held[key][:, c0:c1]
            t_part, base_part = (fresh, acc) if key[0] == "t" else (acc, fresh)
            nc.vector.scalar_tensor_tensor(out=acc, in0=t_part, scalar=ALPHA, in1=base_part, op0=ALU.mult, op1=ALU.add)
            nc.sync.dma_start(out=out_rows[:, i, h * 512 + c0 : h * 512 + c1], in_=acc)
            release(key)

        for tile in (warm, bu_s, w0_s, a_sraw, m_sraw, d_rows):
            zero(tile)
        load_x(0)
        load_xs()
        identity()
        load_scales(bu_s, bu_scales, range(3), nc.gpsimd)
        load_x(1)
        load_x(2)
        load_words(w0_w[0][:], w0_words[:, :, 0:1024])
        load_scales(w0_s, w0_scales)
        load_words(w0_w[1][:], w0_words[:, :, 1024:2048])
        load_x(3)
        load_words(a_raw[:], a_words)
        load_scales(a_sraw, a_scales)
        load_d()
        load_x(4)
        load_words(m_raw[:], m_words)
        load_scales(m_sraw, m_scales)
        load_words(bu_w[0][:], bu_words[:, :, 0:1024])
        load_scales(bu_s, bu_scales, range(3, 4))
        load_words(bu_w[1][:], bu_words[:, :, 1024:2048])

        warm_up(6, "warm0")
        widen_plain(0, 4, 8)
        widen(0, 0, 1)
        widen_plain(2, 4, 8)
        turn_x(0, 0, 1)
        empty_x(0, 0, 1)
        warm_up(1, "warm1")
        turn_x(0, 1, 2)
        empty_x(0, 1, 2)
        widen(1)
        widen(2, 0, 1)
        widen(3)
        for g in range(2):
            turn_x(1, g, g + 1)
            empty_x(1, g, g + 1)
        turn_x(2)
        empty_x(2)

        turn_x(3)
        empty_x(3)
        quant_x(0)
        quant_x(1)
        quant_x(2)
        widen(4, 0, 1)
        quant_x(3)
        reorder(a_w, a_raw)
        reorder(a_s, a_sraw)
        widen(4, 1, 2)
        for i, h in ((0, 0), (1, 0), (0, 1), (1, 1)):
            base(i, h)
            park("b", i, h)
        base(2, 0)
        turn_d()
        empty_d()
        park("b", 2, 0)
        widen(5)
        widen(6)
        reorder(m_w, m_raw)
        reorder(m_s, m_sraw)
        widen(7)
        for t in range(4):
            down(0, t)
            gain(0, t, t == 2)
        for b in range(4):
            mix(0, b)
        empty_c(0, 0, nc.vector.tensor_copy)
        for b in (1, 3, 2):
            empty_c(0, b)
        for i in range(4):
            weave(i)
        quant_p(0, 2)
        for i in range(4, 8):
            turn_x(i)
        for i in (5, 4, 7):
            empty_x(i)
        quant_c(0)
        quant_p(2, 2)
        for b in range(4):
            mix(1, b)
        empty_c(1, 0, nc.vector.tensor_copy)
        empty_x(6)
        quant_x(4, 2)
        quant_x(6, 2)
        for i in range(3):
            up(i, 0)
        for b in (3, 2, 1):
            empty_c(1, b)
        base(3, 0)
        up(3, 0)
        park("t", 3, 0)
        finish(2, 0)
        finish(1, 0)
        quant_c(1)
        for t in range(4):
            down(1, t)
            gain(1, t)
            if t == 2:
                finish(0, 0)
                finish(3, 0)
        for i in range(2):
            up(i, 1)
            finish(i, 1)
        weave(4)
        weave(5)
        for i in (2, 3):
            up(i, 1)
            park("t", i, 1)
            base(i, 1)
        quant_p(4)
        finish(2, 1)
        quant_p(5)
        finish(3, 1)
        weave(6, nc.scalar.copy)
        for h in range(2):
            base(4, h)
            park("b", 4, h)
        quant_p(6)
        for h in range(2):
            up(4, h)
            finish(4, h)
        weave(7)
        up(5, 0)
        park("t", 5, 0)
        steps = [(5, 0), (5, 1), (6, 0)]
        for now, ahead in zip(steps[:2], steps[1:]):
            up(*ahead)
            park("t", *ahead)
            base(*now)
            finish(*now)
            if now == (5, 0):
                quant_p(7)
        last = [(6, 0), (6, 1), (7, 0), (7, 1)]
        for n, now in enumerate(last):
            base(*now, 0, 256)
            finish(*now, 0, 256)
            if n < 3:
                up(*last[n + 1])
                park("t", *last[n + 1], 2)
            base(*now, 256, 512)
            finish(*now, 256, 512)
